import numpy as np, ml_dtypes
CORES = [2,3,42,43,82,83,122,123]
N = 8
BF = ml_dtypes.bfloat16
W, TU, RO, Q, S = 8192, 256, 4, 6, 32
HOPS = [1, 7]
BL = TU // len(HOPS)
def pack(x, l, w, k, h):
    return {"field": x.reshape(N, 128, W).astype(np.float32).astype(BF), "tube": np.ascontiguousarray(l.reshape(N, 128, TU)).astype(np.int32),
            "wt": w.reshape(N, 128, 1).astype(np.int32), "kn": k.reshape(N, 128, 1).astype(np.int32), "lim": np.ascontiguousarray(h.reshape(N, 128, RO)).astype(np.int32)}
def parts(rng):
    dark = rng.random((N, 8, 1, W)) < rng.choice(np.array([0.04, 0.08, 0.15]), (N, 8, 1, 1))
    x = np.where(dark, rng.integers(0, 64, (N, 8, 16, W), dtype=np.int16), rng.integers(48, 256, (N, 8, 16, W), dtype=np.int16))
    l = rng.integers(0, W, (N, 8, 16, TU)); w = rng.integers(0, 256, (N, 8, 16)); k = rng.integers(0, 256, (N, 8, 16))
    return x, l, w, k, rng.integers(16, 72, (N, 8, 16, RO))
def setup_inputs(rng):
    return pack(*parts(rng))
def setup_inputs_spread(rng):
    sh = rng.choice(np.array([0, 0, 0, 0, 0, 1, 1, 2, 4, 8], np.int16), (N, 8, 1, W))
    x = rng.integers(0, 256, (N, 8, 16, W), dtype=np.int16) >> sh
    l = rng.integers(0, W, (N, 8, 16, TU)); l[:, 1::2] = np.minimum((W * rng.random((N, 4, 16, TU)) ** 3).astype(np.int64), W - 1)
    w = rng.integers(0, 256, (N, 8, 16)) >> rng.integers(0, 9, (N, 8, 16)); k = rng.integers(0, 256, (N, 8, 16)) >> rng.integers(0, 9, (N, 8, 16))
    h = rng.integers(0, 249, (N, 8, 16, RO)) >> rng.integers(0, 9, (N, 8, 1, RO))
    return pack(x, l, w, k, h)
def ends_of(rng, hi, shape):
    return np.where(rng.random(shape) < 0.14, rng.integers(0, hi + 1, shape), hi * rng.integers(0, 2, shape))
def setup_inputs_ends(rng):
    kind = rng.random((N, 8, 1, W)); top = np.int16(255)
    x = np.where(kind < 0.7, top, np.where(kind < 0.82, np.int16(0), top * rng.integers(0, 2, (N, 8, 16, W), dtype=np.int16)))
    i = np.arange(16)[:, None]
    b = ((np.arange(N)[:, None] + np.arange(8)[None, :]) & 1) * (W - 1)
    l = np.where(i < rng.integers(0, 17, (N, 8, 1, TU)), b[:, :, None, None], (W - 1) * rng.integers(0, 2, (N, 8, 16, TU)))
    free = ((np.arange(TU) * 5) & 15) < 5; l[..., free] = rng.integers(0, W, (N, 8, 16, int(np.count_nonzero(free))))
    w = ends_of(rng, 255, (N, 8, 16)); k = ends_of(rng, 255, (N, 8, 16))
    h = 248 * rng.integers(0, 2, (N, 8, 16, RO)); h[:, 1::2] = 248 * rng.integers(0, 2, (N, 4, 1, RO))
    for q in range(N):
        for g in range(8):
            o = W - 1 - b[q, g]; x[q, g][:, b[q, g]] = 255
            x[q, g][:, o] = 0 if (g & 3) < 2 or q == 1 else 255 * rng.integers(0, 2, 16) if (g & 3) == 2 else 255
    h[0, :, :, 0] = 0; h[0, 0, :, 1] = 248; h[1, :, :, 0] = 248; h[1, 0, :, 1] = 0; l[1, :, 15, :] = (W - 1 - b[1])[:, None]
    h[2, :, :, 0] = 0; h[2, 0, :, 0] = 248; l[2, 0] = b[2, 0]; l[2, 0, 15, :7] = W - 1 - b[2, 0]; h[2, :, :, 1] = 248
    p = N - 1; u = (15 * 65025) & 4095
    for g in range(4, 8):
        x[p, g][:, 0] = 255; x[p, g][:, W - 1] = 255; w[p, g] = 255
        if g == 5: w[p, g] = 0; w[p, g, 0] = 16; w[p, g, 1] = 1; x[p, g, 1, 0] = 15; x[p, g, 1, W - 1] = 15
        if g > 5:
            w[p, g, 0] = 0; k[p, g] = 255 * (np.arange(16) & 1)
            for j in (0, W - 1):
                x[p, g][:, ((u * u >> 4) + j) & (W - 1)] = 0
                x[p, g][:, ((u * u >> 4) + 255 * u + j) & (W - 1)] = 255 if g == 6 else 0
    return pack(x, l, w, k, h)
def setup_inputs_corners(rng):
    x, l, w, k, h = parts(rng); i = np.arange(16)[:, None]; v = np.arange(TU)
    for q in range(N):
        for g in range(8):
            c = (g + q) & 7
            if c == 0: h[q, g] = 0
            if c == 1: h[q, g] = 248; x[q, g] = np.minimum(x[q, g], 247)
            if c == 2:
                s = rng.integers(0, W, TU); s[0] = 0; s[1] = W - 1; l[q, g] = s[None, :]
            if c == 3:
                m = np.where(rng.random(W) < 0.9, Q, Q - 1)[None, :]
                x[q, g] = np.where(i < m, rng.integers(150, 256, (16, W)), rng.integers(0, 90, (16, W))); h[q, g] = 100
            if c == 4: w[q, g] = 0; k[q, g] = 0
            if c == 5:
                m = rng.random(W) < 0.9; x[q, g, 0, m] = 255; x[q, g, 1, m] = 15; w[q, g] = 0; w[q, g, 0] = 16; w[q, g, 1] = 1; k[q, g] = 255 * rng.integers(0, 2, 16)
            if c == 6:
                t = rng.integers(0, 4, (16, TU)); l[q, g] = np.where(t == 0, 0, np.where(t == 1, W - 1, np.where(t == 2, S * v, S * v + S - 1)))
            if c == 7:
                x[q, g][:, 0::2] = rng.integers(200, 256, (16, W // 2)); x[q, g][:, 1::2] = rng.integers(0, 64, (16, W // 2)); h[q, g] = 100
                l[q, g] = 2 * rng.integers(0, W // 2, (16, TU)) + (i == (v % 17)[None, :])
    return pack(x, l, w, k, h)
def setup_inputs_ties(rng):
    x, l, w, k, h = parts(rng)
    pr = 60 + 4 * rng.integers(0, 3, (N, 8, 16, 5)); x = np.take_along_axis(pr, np.broadcast_to(rng.integers(0, 5, (N, 8, 1, W)), (N, 8, 16, W)), 3)
    return pack(x, l, w, k, rng.integers(53, 66, (N, 8, 16, RO)))
def setup_inputs_brink(rng):
    x, l, w, k, h = parts(rng); r0 = int(rng.integers(0, 8)); v = np.arange(TU)
    h[..., 0] = 0; h[..., 1] = 248; h[..., 2:] = rng.integers(246, 249, (N, 8, 1, RO - 2))
    for g in range(8):
        c = (g + r0) & 7; low = rng.permutation(W)[:32]
        for q in range(N):
            if c < 4:
                o = rng.permutation(16); y = np.full((16, W), 254); y[o[:Q]] = 255
                b = np.nonzero(rng.random(W) < 0.1)[0]; y[o[rng.integers(0, Q, len(b))], b] = 254
                x[q, g] = y
            elif c < 6:
                x[q, g] = rng.integers(248, 256, (16, W)); x[q, g][:, low] = rng.integers(7, 9, (16, 32))
            else:
                x[q, g] = rng.integers(243, 256, (16, W)); x[q, g][:, low] = rng.integers(0, 4, (16, 32))
            if c >= 4:
                l[q, g, rng.integers(1, 16, TU), v] = low[rng.integers(0, 32, TU)]; h[q, g] = 0
            if c == 0:
                d = int(rng.integers(0, W)); s = rng.integers(0, W - 1, (16, TU)); l[q, g] = s + (s >= d)
                l[q, g, rng.integers(1, 16, 7), rng.permutation(TU)[:7]] = d
                x[q, g][:, d] = rng.integers(0, 248, 16); h[q, g, :, 0] = 248
    return pack(x, l, w, k, h)
def check_inputs(d):
    bad = []
    for a, lo, hi in (("field", 0, 255), ("tube", 0, W - 1), ("wt", 0, 255), ("kn", 0, 255), ("lim", 0, 248)):
        v = np.asarray(d[a]).astype(np.float64)
        if not (np.min(v) >= lo and np.max(v) <= hi): bad.append("range of " + a)
        elif np.any(v != np.floor(v)): bad.append("whole numbers of " + a)
    return bad
def reference(field, tube, wt, kn, lim):
    x = field.astype(np.float32).astype(np.int32).reshape(N, 8, 16, W)
    l = tube.astype(np.int64).reshape(N, 8, 16, TU)
    w = wt.astype(np.int64).reshape(N, 8, 16, 1); k = kn.astype(np.int64).reshape(N, 8, 16, 1); h = lim.astype(np.int64).reshape(N, 8, 16, RO)
    cut = [0] * N; v = np.arange(TU); j = np.arange(16)[:, None]
    for rnd in range(RO):
        if rnd: l = np.concatenate([np.roll(l[..., b * BL:(b + 1) * BL], HOPS[b], axis=0) for b in range(len(HOPS))], axis=-1)
        nl = np.zeros((N, 8, 16, TU), np.int64); nz = np.zeros((N, 8, 16, TU), np.int64); ncut = [0] * N
        for q in range(N):
            for g in range(8):
                X, L = x[q, g], l[q, g]
                M = np.minimum.accumulate(X[:, L], axis=1)
                holds = (M >= (h[q, g, :, rnd] + (cut[q] & 7))[:, None, None]).astype(np.int64)
                ok = (np.add.reduce(holds, axis=0) >= Q).astype(np.int64)
                m = np.maximum(np.add.reduce(ok, axis=0), 1) - 1
                Z = np.take_along_axis(M, np.broadcast_to(m[None, None, :], (16, 1, TU)), 1)[:, 0].astype(np.int64)
                u = np.add.reduce(w[q, g] * X[:, L[m, v]], axis=0) & 4095
                c = ((u * u >> 4)[None, :] + k[q, g] * u[None, :] + L) & (W - 1)
                s = np.add.reduce(np.abs(X[:, c] - Z[:, None, :]), axis=0)
                best = c[np.argmin(s, axis=0), v]
                back = L[np.clip(m[None, :] + 1 - j, 0, 15), v[None, :]]
                nl[q, g] = np.where(j == 0, best[None, :], np.where(j <= m[None, :], back, c)); nz[q, g] = Z
                y = (Z + X[:, best]) >> 1
                x[q, g][:, S * v + (u & (S - 1))] = y
                ncut[q] += int(np.count_nonzero(m < 15))
        l = nl; cut = ncut
    return {"yl": l.reshape(N, 128, TU).astype(np.float32), "yz": nz.reshape(N, 128, TU).astype(np.float32)}

@@ -1,0 +1,443 @@
+from concourse.mybir import AluOpType, AxisListType, ActivationFunctionType
+
+A = AluOpType
+F = ActivationFunctionType
+RO = 4
+BF, F32, I32, U16 = "bfloat16", "float32", "int32", "uint16"
+
+SCRATCH = {}
+for _b in "AB":
+    for _n in ("p0", "p1", "p2", "p3"):
+        SCRATCH[_n + _b] = ("psum", [128, 512], F32)
+for _b in "AB":
+    for _n in ("G", "M", "H", "Zx", "D", "AD"):
+        SCRATCH[_n + _b] = ("sbuf", [128, 2048], BF)
+    for _n, _d in (("Si", I32), ("Sm", I32), ("us", F32), ("Lp", F32), ("t32", I32), ("c32", I32), ("Wm", F32),
+                   ("cm", F32), ("Rm", F32), ("OHc", F32), ("Km", F32), ("yh", I32), ("pass", BF),
+                   ("OH", BF), ("Y", BF), ("zo", U16), ("cu", U16), ("ej", BF)):
+        SCRATCH[_n + _b] = ("sbuf", [128, 128], _d)
+    SCRATCH["pn" + _b] = ("sbuf", [128, 256], F32)
+    SCRATCH["ys" + _b] = ("sbuf", [128, 256], F32)
+    SCRATCH["ki" + _b] = ("sbuf", [128, 16], I32)
+    SCRATCH["ku" + _b] = ("sbuf", [128, 8], U16)
+    SCRATCH["su" + _b] = ("sbuf", [128, 384], U16)
+    SCRATCH["sr" + _b] = ("sbuf", [128, 384], F32)
+    for _t in range(RO):
+        SCRATCH["win%d%s" % (_t, _b)] = ("sbuf", [128, 2048], F32)
+        SCRATCH["lu%d%s" % (_t, _b)] = ("sbuf", [128, 128], U16)
+for _n, _s, _d in (("X", [128, 8192], BF), ("R", [128, 1024], BF), ("Rk", [128, 128], F32), ("ones", [128, 256], BF),
+                   ("E", [128, 144], BF), ("Bd", [128, 128], BF), ("Id", [128, 128], BF), ("Sh", [128, 128], BF),
+                   ("selM", [128, 128], BF), ("Bn", [128, 128], BF), ("Wn", [128, 128], BF), ("Qe", [128, 128], BF),
+                   ("R16", [128, 128], BF), ("mask", [128, 128], BF), ("K8", [128, 8], BF), ("wE", [128, 144], BF),
+                   ("row16", [128, 128], BF), ("rowi", [128, 128], BF), ("Bd32", [128, 128], F32), ("Bu32", [128, 128], F32),
+                   ("I32", [128, 128], F32), ("J32", [128, 128], F32), ("E32", [128, 144], F32), ("z8", [128, 16], F32),
+                   ("cols", [128, 16], F32), ("wi", [128, 1], I32), ("kni", [128, 1], I32), ("limi", [128, 4], I32),
+                   ("limf", [128, 4], F32), ("tub", [128, 256], I32), ("tubf", [128, 256], F32), ("pi", [128, 32], I32),
+                   ("cvb", [128, 32], I32), ("cv", [128, 32], I32), ("zt", [128, 1920], F32), ("Wi", [128, 16], I32),
+                   ("nu", [128, 32], I32), ("nv", [128, 32], I32), ("rp", [128, 32], U16), ("ei", [128, 2], I32),
+                   ("ec", [128, 2], F32), ("one32", [128, 128], F32)):
+    SCRATCH[_n] = ("sbuf", _s, _d)
+
+SEMAPHORES = ["qV", "qA", "qT", "qG", "lX", "ltub", "lwt", "lkn", "llim", "snd", "out"]
+for _b in "AB":
+    SEMAPHORES += [_n + "%d%s" % (_t, _b) for _n in "wz" for _t in range(RO)]
+    SEMAPHORES += ["au%d%s" % (_t, _b) for _t in range(1, RO)] + ["ar%d%s" % (_t, _b) for _t in range(1, RO)]
+
+CY = 0.83e-3 * 1.2
+PEC = 0.75e-3 * 1.2
+GA = 1.5
+WAKE = 0.12
+PRI = dict(Abs0A=107,Abs0B=-224,Abs1A=-94,Abs1B=-31,Abs2A=-372,Abs2B=-627,Abs3A=322,Abs3B=-436,B=-69,CP0A=-224,CP0B=-356,
+    CP1A=-370,CP1B=317,EA=254,EB=21,EaccA=523,EaccB=-161,G10A=387,G10B=-448,G11A=208,G11B=307,G20A=219,G20B=-180,G21A=-381,
+    G21B=485,G22A=-937,G22B=216,G23A=41,G23B=40,KmA=913,KmB=-364,KpA=588,KpB=-12,LpA=-95,LpB=83,OHA=-510,OHB=54,OHTA=681,
+    OHTB=168,OHcA=-216,OHcB=350,RmA=207,RmB=-136,S0A=523,S0B=90,S1A=679,S1B=279,SC0A=-114,SC0B=-22,SC1A=694,SC1B=-272,SqA=751,
+    SqB=-6,WexpA=-632,WexpB=474,WmA=520,WmB=-166,WpA=203,WpB=248,YA=240,YB=39,ZcA=728,ZcB=-69,Zx0A=-97,Zx0B=129,Zx1A=-141,
+    Zx1B=-374,Zx2A=-274,Zx2B=-130,Zx3A=-34,Zx3B=-221,cmA=3,cmB=334,cnt0A=125,cnt0B=-25,cnt1A=316,cnt1B=678,e1=-192,e2=11,
+    e3=-250,k1A=-245,k1B=232,k2A=196,k2B=-74,k3A=125,k3B=377,kcA=-561,kcB=-194,keyA=126,keyB=649,nat1A=100,nat1B=230,nat2A=312,
+    nat2B=509,npassA=-309,npassB=320,outA=413,outB=538,passA=566,passB=232,revA=113,revB=-114,revcA=-31,revcB=-222,s4A=382,
+    s4B=582,s5A=187,s5B=567,s6A=-629,s6B=-145,s7A=103,s7B=640,s8A=345,s8B=-104,scanA=65,scanB=526,scatA=-30,scatB=-3,scrA=-60,
+    scrB=-65,selA=866,selB=472,sendrA=70,sendrB=-10,senduA=211,senduB=505,suA=-195,suB=126,uA=823,uB=451,usA=-23,usB=-153,
+    w1A=-76,w1B=20,w2=-71,w3=-305,w4=196,w5=557,yhA=-410,yhB=199,ylA=-41,ylB=-98,yzA=-366,yzB=306,zoA=518,zoB=141)
+LOOK = {"V": 0.0, "A": 0.0, "T": 0.2, "G": 0.0, "S": 0.0, "AD": 0.0, "R": 0.0}
+G1Q = {("A", 0): "A", ("A", 1): "V", ("B", 0): "A", ("B", 1): "A"}
+
+
+def vcost(n, f=1.0): return 0.05 + max(64, n * f) * CY
+def gcost(n): return 0.06 + n * GA * CY
+
+
+def make_ops(core, T, topo):
+    ops = []
+    lastw, readers, bank = {}, {}, {}
+    dcount = {}
+    cur = [""]
+
+    def op(q, cost, reads, writes, fn, banks=(), sem=None, cnt=0, sched=(), tag=""):
+        o = {"i": len(ops), "q": q, "c": cost, "fn": fn, "wait": set(), "order": set(sched), "sem": sem, "tag": tag + cur[0], "n": cnt}
+        for k in reads:
+            if k in lastw: o["wait"].add(lastw[k])
+        for k in writes:
+            if k in lastw: o["wait"].add(lastw[k])
+            for r in readers.get(k, ()):
+                if ops[r]["q"] == q and q != "S": o["order"].add(r)
+                else: o["wait"].add(r)
+        for k in banks:
+            if k in bank:
+                r = bank[k]
+                (o["order"] if ops[r]["q"] == q else o["wait"]).add(r)
+            bank[k] = o["i"]
+        for k in reads: readers.setdefault(k, []).append(o["i"])
+        for k in writes:
+            lastw[k] = o["i"]; readers[k] = []
+        o["wait"].discard(o["i"]); o["order"].discard(o["i"])
+        if q in ("S", "AD"):
+            dcount[sem] = dcount.get(sem, 0) + 16
+            o["n"] = dcount[sem]
+        ops.append(o)
+        return o["i"]
+
+    def V(n, f, reads, writes, fn, banks=(), tag=""):
+        return op("V", vcost(n, f), reads, writes, fn, banks, tag=tag)
+
+    def C(n, reads, writes, fn, banks=(), tag=""):
+        return op("A", 0.07 + max(64, n) * CY, reads, writes, fn, banks, tag=tag)
+
+    def P(cyc, reads, fn, banks, tag=""):
+        return op("T", 0.03 + cyc * PEC, reads, (), fn, banks, tag=tag)
+
+    def Gc(n, reads, writes, fn, tag=""):
+        return op("G", 0.17 + 2 * n * CY, reads, writes, fn, tag=tag)
+
+    def DMA(q, cost, reads, writes, out, in_, sem, tag=""):
+        return op(q, cost, reads, writes, lambda e: e.dma_start(out, in_), sem=sem, tag=tag)
+
+    rank = T.rank_of(core)
+    ncore = len(T.cores)
+    peer = {"A": (T.cores[(rank + 1) % ncore], T.cores[(rank - 1) % ncore]),
+            "B": (T.cores[(rank - 1) % ncore], T.cores[(rank + 1) % ncore])}
+
+    def lanes(s, d):
+        return topo.engines(s, d)[:8]
+
+    DMA("AD", 2.0, (), ("tub",), T.tub[:], T.tube[:], "ltub")
+    DMA("AD", 2.0, (), ("wi",), T.wi[:], T.wt[:], "lwt")
+    DMA("AD", 2.0, (), ("kni",), T.kni[:], T.kn[:], "lkn")
+    DMA("AD", 2.0, (), ("limi",), T.limi[:], T.lim[:], "llim")
+    DMA("S", 11.0, (), ("X",), T.X[:], T.field[:], "lX")
+    V(256, .5, (), ("ones",), lambda e: e.memset(T.ones[:], 1.0))
+    V(128, 1, (), ("one32",), lambda e: e.memset(T.one32[:], 1.0))
+    ON, O3 = T.ones, T.one32
+    Gc(128, ("ones",), ("Bd0",), lambda e: e.affine_select(T.Bd[:], ON[:, 0:128], [[-16, 8], [0, 16]], A.is_ge, 0.0, 0, 1))
+    Gc(128, ("Bd0",), ("Bd",), lambda e: e.affine_select(T.Bd[:], T.Bd[:], [[16, 8], [0, 16]], A.is_ge, 0.0, 15, -1))
+    Gc(128, ("ones",), ("Id",), lambda e: e.affine_select(T.Id[:], ON[:, 0:128], [[-1, 128]], A.is_equal, 0.0, 0, 1))
+    Gc(8, ("one32",), ("z8",), lambda e: e.affine_select(T.z8[:, 0:8], O3[:, 0:8], [[-16, 8]], A.is_equal, 0.0, 0, 1))
+    Gc(128, ("one32",), ("J0",), lambda e: e.affine_select(T.J32[:], O3[:], [[-16, 8], [1, 16]], A.is_equal, 0.0, -16, 1))
+    Gc(8, ("one32",), ("z15",), lambda e: e.affine_select(T.z8[:, 8:16], O3[:, 0:8], [[-16, 8]], A.is_equal, 0.0, -15, 1))
+    Gc(144, ("ones",), ("E0",), lambda e: e.affine_select(T.E[:], ON[:, 0:144], [[0, 9], [1, 16]], A.is_equal, 0.0, -15, 0))
+    Gc(144, ("E0",), ("E1",), lambda e: e.affine_select(T.E[:], T.E[:], [[-16, 9], [0, 16]], A.is_ge, 0.0, 0, 1))
+    Gc(144, ("E1",), ("E",), lambda e: e.affine_select(T.E[:], T.E[:], [[16, 9], [0, 16]], A.is_ge, 0.0, 15, -1))
+    Gc(128, ("ones",), ("Sh",), lambda e: e.affine_select(T.Sh[:], ON[:, 0:128], [[-1, 128]], A.is_equal, 0.0, -1, 1))
+    Gc(128, ("ones",), ("R16",), lambda e: e.affine_select(T.R16[:], ON[:, 0:128], [[0, 8], [1, 16]], A.is_equal, 0.0, 0, -1))
+    Gc(128, (), ("row16",), lambda e: e.iota(T.row16[:], [[16, 128]], 0, 0, allow_small_or_imprecise_dtypes=True))
+    Gc(128, (), ("rowi",), lambda e: e.iota(T.rowi[:], [[0, 8], [1, 16]], 0, 0, allow_small_or_imprecise_dtypes=True))
+    Gc(32, (), ("pi",), lambda e: e.iota(T.pi[:], [[0, 32]], 0, 1))
+    Gc(16, (), ("cvb0",), lambda e: e.iota(T.cvb[:, 0:16], [[0, 2], [16, 8]], 0, 0))
+    Gc(16, (), ("cvb1",), lambda e: e.iota(T.cvb[:, 16:32], [[512, 16]], 0, 0))
+    for b in "AB":
+        s = slice(0, 128) if b == "A" else slice(128, 256)
+        V(128, 1, ("tub",), ("lu0" + b,), lambda e, b=b, s=s: e.tensor_copy(T["lu0" + b][:], T.tub[:, s]))
+    V(256, 1, ("tub",), ("tubf",), lambda e: e.tensor_copy(T.tubf[:], T.tub[:]))
+    for b in "AB":
+        s = slice(0, 128) if b == "A" else slice(128, 256)
+        P(512, ("J0", "tubf"), lambda e, b=b, s=s: e.matmul(T["p3" + b][:, 0:128], T.J32[:], T.tubf[:, s], True, True), ("3" + b,))
+        C(128, (), ("win0%s.0" % b,), lambda e, b=b: e.activation(T["win0" + b][:, 0:128], T["p3" + b][:, 0:128], F.Copy), ("3" + b,))
+    V(1920, 1, (), ("zt",), lambda e: e.memset(T.zt[:], 0.0))
+    for t in range(RO):
+        for b in "AB":
+            DMA("S", 2.0, ("zt",), ("win%d%s.z" % (t, b),), T["win%d%s" % (t, b)][112:128, 128:2048], T.zt[112:128, :], "z%d%s" % (t, b))
+    col = T.cols
+    V(8, 1, ("z8",), ("c0",), lambda e: e.tensor_reduce(col[:, 0:1], T.z8[:, 0:8], AxisListType.X, A.add))
+    V(8, 1, ("z15",), ("c2",), lambda e: e.tensor_reduce(col[:, 2:3], T.z8[:, 8:16], AxisListType.X, A.add, negate=True))
+    V(1, 1, ("c0",), ("c1",), lambda e: e.tensor_scalar(col[:, 1:2], col[:, 0:1], -1.0, 1.0, A.mult, A.add))
+    V(1, 1, ("c0",), ("c3",), lambda e: e.tensor_scalar(col[:, 3:4], col[:, 0:1], -7.0, 6.0, A.mult, A.add))
+    V(1, 1, ("c0",), ("c8",), lambda e: e.tensor_scalar(col[:, 8:9], col[:, 0:1], 2048.0, -128.0, A.mult, A.add))
+    V(1, 1, ("wi",), ("c4",), lambda e: e.tensor_copy(col[:, 4:5], T.wi[:]))
+    V(1, 1, ("kni",), ("c5",), lambda e: e.tensor_scalar(col[:, 5:6], T.kni[:], 8.0, None, A.mult))
+    V(1, 1, ("c5",), ("c9",), lambda e: e.tensor_tensor(col[:, 9:10], col[:, 5:6], col[:, 5:6], A.mult))
+    V(1, 1, ("c9",), ("c6",), lambda e: e.tensor_scalar(col[:, 6:7], col[:, 9:10], -1.0, None, A.mult))
+    V(4, 1, ("limi",), ("limf",), lambda e: e.tensor_copy(T.limf[:], T.limi[:]))
+    V(144, .5, ("E", "c4"), ("wE",), lambda e: e.tensor_scalar(T.wE[:], T.E[:], col[:, 4:5], None, A.mult))
+    V(1024, .5, (), ("R0",), lambda e: e.memset(T.R[:], 0.0))
+    V(64, .5, ("R0",), ("R",), lambda e: e.memset(T.R[:, 0:1024:16], 255.0))
+    V(128, 2, ("Sh", "Bd"), ("ShB",), lambda e: e.tensor_tensor(T.Sh[:], T.Sh[:], T.Bd[:], A.mult))
+    V(128, 2, ("Id", "ShB"), ("selM",), lambda e: e.tensor_tensor(T.selM[:], T.Id[:], T.Sh[:], A.subtract))
+    V(128, .5, ("Bd", "c1"), ("Bn",), lambda e: e.tensor_scalar(T.Bn[:], T.Bd[:], col[:, 1:2], None, A.mult))
+    V(128, 1, ("Bd",), ("Bd32",), lambda e: e.tensor_copy(T.Bd32[:], T.Bd[:]))
+    V(128, 1, ("Bd",), ("Bu32",), lambda e: e.tensor_scalar(T.Bu32[:], T.Bd[:], 2048.0, None, A.mult))
+    V(128, .5, ("Bd", "c8"), ("Wn",), lambda e: e.tensor_scalar(T.Wn[:], T.Bd[:], col[:, 8:9], None, A.mult))
+    V(128, .5, ("ones", "c2"), ("Qe",), lambda e: e.tensor_scalar(T.Qe[:], ON[:, 0:128], col[:, 2:3], None, A.mult))
+    P(128, ("R16",), lambda e: e.matmul(T.p2A[:, 0:128], T.R16[:], T.R16[:], True, True), ("2A",))
+    V(128, 1, (), ("mask",), lambda e: e.tensor_copy(T.mask[:], T.p2A[:, 0:128]), ("2A",))
+    V(8, 1, ("Bd",), ("K8",), lambda e: e.tensor_scalar(T.K8[:], T.Bd[:, 0:128:16], 4096.0, None, A.mult))
+    V(128, 1, ("Id", "c1"), ("I32",), lambda e: e.tensor_scalar(T.I32[:], T.Id[:], col[:, 1:2], None, A.mult))
+    V(144, 1, ("E",), ("E32",), lambda e: e.tensor_copy(T.E32[:], T.E[:]))
+    V(128, 1, (), ("Rk0",), lambda e: e.memset(T.Rk[:], 0.0))
+    V(8, 1, ("Rk0",), ("Rk",), lambda e: e.memset(T.Rk[:, 0:128:16], 33554432.0))
+    V(32, 1, ("pi",), ("pi2",), lambda e: e.tensor_scalar(T.pi[:], T.pi[:], 15, None, A.bitwise_and))
+    V(16, 1, ("pi2",), ("pi3",), lambda e: e.tensor_scalar(T.pi[:, 16:32], T.pi[:, 16:32], 32, None, A.mult))
+    V(32, 2, ("pi2", "pi3", "cvb0", "cvb1"), ("cv",), lambda e: e.tensor_tensor(T.cv[:], T.pi[:], T.cvb[:], A.add))
+    V(1, 1, ("limf",), ("thr",), lambda e: e.tensor_copy(col[:, 7:8], T.limf[:, 0:1]))
+
+    pend = {}
+    for t in range(RO):
+        last = t == RO - 1
+        if t:
+            for b in "AB":
+                src = peer[b][1]
+                op("R", 2.2, (), ("lu%d%s" % (t, b),), None, sem="au%d%s" % (t, b), cnt=len(lanes(src, core)), sched=(pend["u" + b],))
+                op("R", 2.2, (), ("win%d%s.0" % (t, b),), None, sem="ar%d%s" % (t, b), cnt=len(lanes(src, core)), sched=(pend["r" + b],))
+        for k in (1, 2, 4, 8):
+            for b in "AB":
+                w = T["win%d%s" % (t, b)]; n = "win%d%s." % (t, b)
+                rd = [n + "z", n + "0"] + [n + str(j) for j in (1, 2, 4) if j < k]
+                DMA("S", 2.0 + k * .06, rd, (n + str(k),), w[0:128 - k, 128 * k:256 * k], w[k:128, 0:128 * k], "w%d%s" % (t, b))
+        for b in "AB":
+            cur[0] = b
+            bk = [str(j) + b for j in range(4)]
+            p0, p1, p2, p3 = T["p0" + b], T["p1" + b], T["p2" + b], T["p3" + b]
+            lu = T["lu%d%s" % (t, b)]; luk = "lu%d%s" % (t, b)
+            tl = {n: T[n + b] for n in ("G", "M", "H", "Si", "Sm", "us", "Lp", "t32", "c32", "Wm", "pass", "zo", "cu", "ej", "Zx")}
+            G, M, H, Zx = tl["G"], tl["M"], tl["H"], tl["Zx"]
+            V(128, 1, (luk, "c6"), ("Lp" + b,), lambda e, d=tl["Lp"], s=lu: e.tensor_scalar(d[:], s[:], 16.0, col[:, 6:7], A.mult, A.add), tag="Lp")
+            for h in (0, 1):
+                f = slice(h * 1024, h * 1024 + 1024); o = slice(h * 64, h * 64 + 64)
+                gk, mk, hk = "G%s%d" % (b, h), "M%s%d" % (b, h), "H%s%d" % (b, h)
+                if G1Q[(b, h)] == "A":
+                    op("A", gcost(1024), ("X", luk), (gk,), lambda e, G=G, f=f, o=o, lu=lu: e.activation(G[:, f], T.X[:, 0:8192].indirect(lu[:, o]), F.Copy), tag="G1%d" % h)
+                else:
+                    op("V", gcost(1024), ("X", luk), (gk,), lambda e, G=G, f=f, o=o, lu=lu: e.tensor_copy(G[:, f], T.X[:, 0:8192].indirect(lu[:, o])), tag="G1%d" % h)
+                V(1024, .5, (gk, "R"), (mk,), lambda e, G=G, M=M, f=f: e.tensor_tensor_scan(M[:, f], T.R[:], G[:, f], 0.0, A.max, A.min), tag="SC%d" % h)
+                V(1024, .5, (mk, "thr"), (hk,), lambda e, H=H, M=M, f=f: e.tensor_scalar(H[:, f], M[:, f], col[:, 7:8], None, A.is_ge), tag="CP%d" % h)
+
+                def mm8(e, dst, w, src, i0, h=h, o=o):
+                    for i in range(i0, i0 + 8):
+                        r = e.matmul(dst[:, o], w[:, 15 - i:143 - i], src[:, h * 1024 + i:h * 1024 + 1024:16], i == 0, i == 15)
+                    return r
+                for i0 in (0, 8):
+                    P(512, (gk, "wE"), lambda e, d=p1, s=G, f=mm8, i0=i0: f(e, d, T.wE, s, i0), (bk[1],), tag="S%d" % h)
+                for i0 in (0, 8):
+                    P(512, (hk, "E"), lambda e, d=p0, s=H, f=mm8, i0=i0: f(e, d, T.E, s, i0), (bk[0],), tag="cnt%d" % h)
+            V(128, 1, (), ("Si" + b,), lambda e, d=tl["Si"], s=p1: e.tensor_copy(d[:], s[:, 0:128]), (bk[1],), tag="s7")
+            V(128, 1, ("Si" + b,), ("Sm" + b,), lambda e, d=tl["Sm"], s=tl["Si"]: e.tensor_scalar(d[:], s[:], 4095, None, A.bitwise_and), tag="s8")
+            V(128, 1, ("c3",), ("pass" + b,), lambda e, d=tl["pass"], s=p0: e.tensor_scalar(d[:], s[:, 0:128], col[:, 3:4], None, A.is_ge), (bk[0],), tag="pass")
+
+            def selnoff(e, p2=p2, ps=tl["pass"]):
+                e.matmul(p2[:, 0:128], T.selM[:], ps[:], True, True)
+                e.matmul(p2[:, 128:256], ON[0:1, 0:128], T.row16[0:1, :], True, False)
+                return e.matmul(p2[:, 128:256], T.Bn[:], ps[:], False, True)
+            P(384, ("pass" + b, "selM", "Bn", "ones", "row16"), selnoff, (bk[2],), tag="sel")
+            V(128, 1, ("Sm" + b,), ("us" + b,), lambda e, d=tl["us"], s=tl["Sm"], p2=p2: e.tensor_tensor(d[:], s[:], p2[:, 0:128], A.mult), (bk[2],), tag="us")
+            V(128, 1, (), ("zo" + b,), lambda e, d=tl["zo"], p2=p2: e.tensor_copy(d[:], p2[:, 128:256]), (bk[2],), tag="zo")
+            P(512, ("us" + b, "Bd32"), lambda e, d=p3, s=tl["us"]: e.matmul(d[:, 0:128], T.Bd32[:], s[:], True, True), (bk[3],), tag="u")
+            C(128, ("c5",), (), lambda e, d=p3: e.activation(d[:, 128:256], d[:, 0:128], F.Square, bias=col[:, 5:6]), (bk[3],), tag="Sq")
+            V(128, 1, ("Lp" + b,), ("t32" + b,), lambda e, d=tl["t32"], p3=p3, l=tl["Lp"]: e.tensor_tensor(d[:], p3[:, 128:256], l[:], A.add), (bk[3],), tag="s4")
+            V(128, 1, ("t32" + b,), ("c32" + b,), lambda e, d=tl["c32"], s=tl["t32"]: e.tensor_scalar(d[:], s[:], 4, 8191, A.arith_shift_right, A.bitwise_and), tag="s5")
+            V(128, 1, ("c32" + b,), ("cu" + b,), lambda e, d=tl["cu"], s=tl["c32"]: e.tensor_copy(d[:], s[:]), tag="s6")
+            for h4 in range(4):
+                f = slice(h4 * 512, h4 * 512 + 512); o = slice(h4 * 32, h4 * 32 + 32)
+                op("A", gcost(512), ("zo" + b, "M%s0" % b, "M%s1" % b), ("Zx%s%d" % (b, h4),),
+                   lambda e, d=Zx, M=M, z=tl["zo"], f=f, o=o: e.activation(d[:, f], M[:, 0:2048].indirect(z[:, o]), F.Copy), tag="Zx%d" % h4)
+            C(128, ("pass" + b,), (), lambda e, d=p3, s=tl["pass"]: e.activation(d[:, 256:384], s[:], F.Copy, bias=1.0, scale=-1.0), (bk[3],), tag="npass")
+
+            def wexp(e, p1=p1, ps=tl["pass"], us=tl["us"], last=last):
+                r = e.matmul(p1[:, 128:256], ps[:], T.Wn[:], True, last)
+                if not last:
+                    r = e.matmul(p1[:, 128:256], us[:], T.Bu32[:], False, True)
+                return r
+            P(640, ("pass" + b, "us" + b, "Wn", "Bu32"), wexp, (bk[1],), tag="Wexp")
+            V(128, 1, ("mask",), ("Wm" + b,), lambda e, d=tl["Wm"], p1=p1: e.tensor_tensor(d[:], p1[:, 128:256], T.mask[:], A.mult), (bk[1],), tag="Wm")
+            P(256, ("Wm" + b, "Bd32"), lambda e, p1=p1, s=tl["Wm"]: e.matmul(p1[:, 256:264], s[:], T.Bd32[:, 0:128:16], True, True), (bk[1],), tag="Wp")
+            c0 = 0 if b == "A" else 8
+            V(8, 1, (), ("Wi" + b,), lambda e, p1=p1, c0=c0: e.tensor_copy(T.Wi[:, c0:c0 + 8], p1[:, 256:264]), (bk[1],), tag="w1")
+            if not last:
+                P(128, ("Qe", "pass" + b), lambda e, d=p0, s=tl["pass"]: e.matmul(d[:, 128:256], T.Qe[:], s[:], True, True), (bk[0],), tag="E")
+                ec = T.ec[:, 0:1] if b == "A" else T.ec[:, 1:2]
+                C(128, (), ("ec" + b, "ej" + b), lambda e, d=tl["ej"], s=p0, c=ec: e.activation(d[:], s[:, 128:256], F.Copy, accum_out=c), (bk[0],), tag="Eacc")
+        cur[0] = ""
+        V(16, 1, ("WiA", "WiB"), ("nu0",), lambda e: e.tensor_scalar(T.nu[:, 0:16], T.Wi[:], 2047, None, A.bitwise_and), tag="w2")
+        if last:
+            V(16, 2, ("nu0", "cv"), ("nv",), lambda e: e.tensor_tensor(T.nv[:, 0:16], T.nu[:, 0:16], T.cv[:, 0:16], A.add), tag="w4")
+            V(16, 1, ("nv",), ("rp",), lambda e: e.tensor_copy(T.rp[:, 0:16], T.nv[:, 0:16]), tag="w5")
+        else:
+            V(16, 1, ("WiA", "WiB"), ("nu1",), lambda e: e.tensor_scalar(T.nu[:, 16:32], T.Wi[:], 11, 31, A.arith_shift_right, A.bitwise_and), tag="w3")
+            V(32, 2, ("nu0", "nu1", "cv"), ("nv",), lambda e: e.tensor_tensor(T.nv[:], T.nu[:], T.cv[:], A.add), tag="w4")
+            V(32, 1, ("nv",), ("rp",), lambda e: e.tensor_copy(T.rp[:], T.nv[:]), tag="w5")
+            V(1, 1, ("ecA", "ecB"), ("ei",), lambda e: e.tensor_tensor(T.ei[:, 0:1], T.ec[:, 0:1], T.ec[:, 1:2], A.add), tag="e1")
+            V(1, 1, ("ei",), ("ej2",), lambda e: e.tensor_scalar(T.ei[:, 1:2], T.ei[:, 0:1], 7, None, A.bitwise_and), tag="e2")
+            V(1, 2, ("ej2", "limf"), ("thr",), lambda e, t=t: e.tensor_tensor(col[:, 7:8], T.ei[:, 1:2], T.limf[:, t + 1:t + 2], A.add), tag="e3")
+        for b in "AB":
+            cur[0] = b
+            D, AD, Zx, cu = T["D" + b], T["AD" + b], T["Zx" + b], T["cu" + b]
+            for h in range(4):
+                f = slice(h * 512, h * 512 + 512); o = slice(h * 32, h * 32 + 32)
+                op("V", gcost(512), ("X", "cu" + b, "Zx%s%d" % (b, h)), ("D%s%d" % (b, h),),
+                   lambda e, D=D, Zx=Zx, cu=cu, f=f, o=o: e.tensor_tensor(D[:, f], T.X[:, 0:8192].indirect(cu[:, o]), Zx[:, f], A.subtract), tag="G2%d" % h)
+                C(512, ("D%s%d" % (b, h),), ("AD%s%d" % (b, h),), lambda e, D=D, AD=AD, f=f: e.activation(AD[:, f], D[:, f], F.Abs), tag="Abs%d" % h)
+        for b in "AB":
+            cur[0] = b
+            bk = [str(j) + b for j in range(4)]
+            p0, p1, p2, p3 = T["p0" + b], T["p1" + b], T["p2" + b], T["p3" + b]
+            D, AD, Zx, pn = T["D" + b], T["AD" + b], T["Zx" + b], T["pn" + b]
+            q4 = [b + str(j) for j in range(4)]
+            zk = ["Zx" + j for j in q4]
+            q = {n: T[n + b] for n in ("cm", "Rm", "OHc", "Km", "yh", "pass", "OH", "Y", "c32", "ki", "ku")}
+            c0 = 0 if b == "A" else 8
+            V(128, 1, ("c32" + b,), ("cm" + b,), lambda e, q=q, p3=p3: e.tensor_tensor(q["cm"][:], q["c32"][:], p3[:, 256:384], A.mult), (bk[3],), tag="cm")
+            if not last:
+                C(128, zk, (), lambda e, d=p3, Zx=Zx: e.activation(d[:, 384:512], Zx[:, 0:2048:16], F.Copy), (bk[3],), tag="Zc")
+            wn = "win%d%s" % (t, b)
+            op("V", gcost(128), [wn + "." + j for j in "z01248"] + ["rp", "pass" + b], ("Rm" + b,),
+               lambda e, q=q, w=T[wn], c0=c0: e.tensor_tensor(q["Rm"][:], w[:, 0:2048].indirect(T.rp[:, c0:c0 + 8]), q["pass"][:], A.mult), tag="Rm")
+            if not last:
+                def rev(e, p3=p3, q=q):
+                    e.matmul(p3[:, 0:128], T.J32[:], q["cm"][:], True, False)
+                    return e.matmul(p3[:, 0:128], T.J32[:], q["Rm"][:], False, True)
+                P(1024, ("J0", "cm" + b, "Rm" + b), rev, (bk[3],), tag="rev")
+                ts = slice(t * 128, t * 128 + 128)
+                sr = T["sr" + b][:, ts]; su = T["su" + b][:, ts]
+                C(128, (), ("sr%d%s" % (t, b),), lambda e, d=sr, p3=p3: e.activation(d, p3[:, 0:128], F.Copy), (bk[3],), tag="revc")
+                pend["r" + b] = op("G", 1.0, ("sr%d%s" % (t, b),), (), ("send", sr, "win%d%s" % (t + 1, b), "ar%d%s" % (t + 1, b), peer[b][0]), sem="snd", tag="sendr")
+
+            def nat1(e, p2=p2, q=q):
+                e.matmul(p2[:, 0:128], T.I32[:], q["cm"][:], True, False)
+                return e.matmul(p2[:, 0:128], T.I32[:], q["Rm"][:], False, False)
+            P(1024, ("I32", "cm" + b, "Rm" + b), nat1, (bk[2],), tag="nat1")
+
+            def kc(e, p0=p0):
+                e.matmul(p0[:, 256:384], T.row16[0:1, :], ON[0:1, 0:128], True, False)
+                return e.matmul(p0[:, 256:384], ON[0:1, 0:128], T.rowi[0:1, :], False, False)
+            P(256, ("row16", "ones", "rowi"), kc, (bk[0],), tag="kc")
+
+            def kd(e, p0=p0, AD=AD):
+                for i in range(16):
+                    r = e.matmul(p0[:, 256 + i:384:16], AD[:, i:2048:16], T.K8[:], False, i == 15)
+                return r
+            P(1024, ["AD" + j for j in q4] + ["K8"], kd, (bk[0],), tag="key")
+            V(128, 1, ("Rk",), ("pm" + b,), lambda e, d=pn, p0=p0: e.tensor_tensor_scan(d[:, 0:128], T.Rk[:], p0[:, 256:384], 0.0, A.max, A.min), (bk[0],), tag="scan")
+            V(128, 1, ("Rk", "pm" + b), ("mn" + b,), lambda e, d=pn: e.tensor_tensor_scan(d[:, 255:127:-1], T.Rk[:], d[:, 127::-1], 0.0, A.max, A.min), tag="scr")
+            if not last:
+                V(128, 2, ("mn" + b, "mask"), ("Km" + b,), lambda e, q=q, d=pn: e.tensor_tensor(q["Km"][:], d[:, 128:256], T.mask[:], A.mult), tag="Km")
+            V(128, 1, ("mn" + b,), ("OH" + b,), lambda e, q=q, d=pn, p0=p0: e.tensor_tensor(q["OH"][:], p0[:, 256:384], d[:, 128:256], A.is_equal), (bk[0],), tag="OH")
+            if not last:
+                P(256, ("Km" + b, "Bd32"), lambda e, q=q, p0=p0: e.matmul(p0[:, 384:392], q["Km"][:], T.Bd32[:, 0:128:16], True, True), (bk[0],), tag="Kp")
+            P(128, ("OH" + b, "Id"), lambda e, q=q, p1=p1: e.matmul(p1[:, 0:128], q["OH"][:], T.Id[:], True, True), (bk[1],), tag="OHT")
+            V(128, 1, ("c32" + b,), ("OHc" + b,), lambda e, q=q, p1=p1: e.tensor_tensor(q["OHc"][:], q["c32"][:], p1[:, 0:128], A.mult), (bk[1],), tag="OHc")
+            P(512, ("E32", "OHc" + b), lambda e, q=q, p2=p2: e.matmul(p2[:, 0:128], T.E32[:, 15:143], q["OHc"][:], False, True), (bk[2],), tag="nat2")
+            if last:
+                s = slice(0, 128) if b == "A" else slice(128, 256)
+                ys = T["ys" + b]
+                V(128, 1, (), ("yls" + b,), lambda e, d=ys, p2=p2: e.tensor_copy(d[:, 0:128], p2[:, 0:128]), (bk[2],), tag="yl")
+                C(128, zk, ("yzs" + b,), lambda e, d=ys, Zx=Zx: e.activation(d[:, 128:256], Zx[:, 0:2048:16], F.Copy), tag="yz")
+                DMA("S", 2.0, ("yzs" + b,), (), T.yz[:, s], ys[:, 128:256], "out", tag="out")
+                DMA("S", 2.0, ("yls" + b,), (), T.yl[:, s], ys[:, 0:128], "out", tag="out")
+            else:
+                V(128, 1, (), ("su%d%s" % (t, b),), lambda e, d=su, p2=p2: e.tensor_copy(d, p2[:, 0:128]), (bk[2],), tag="su")
+                pend["u" + b] = op("G", 1.0, ("su%d%s" % (t, b),), (), ("send", su, "lu%d%s" % (t + 1, b), "au%d%s" % (t + 1, b), peer[b][0]), sem="snd", tag="sendu")
+                V(8, 1, (), ("ki" + b,), lambda e, q=q, p0=p0: e.tensor_copy(q["ki"][:, 0:8], p0[:, 384:392]), (bk[0],), tag="k1")
+                V(8, 1, ("ki" + b,), ("kj" + b,), lambda e, q=q: e.tensor_scalar(q["ki"][:, 8:16], q["ki"][:, 0:8], 4095, None, A.bitwise_and), tag="k2")
+                V(8, 1, ("kj" + b,), ("ku" + b,), lambda e, q=q: e.tensor_copy(q["ku"][:], q["ki"][:, 8:16]), tag="k3")
+                op("V", gcost(128), ["ku" + b] + ["D" + j for j in q4], ("yh" + b,),
+                   lambda e, q=q, D=D: e.tensor_scalar(q["yh"][:], D[:, 0:2048].indirect(q["ku"][:]), 0.5, -0.25, A.mult, A.add), tag="yh")
+                V(128, 1, ("yh" + b,), ("Y" + b,), lambda e, q=q, p3=p3: e.tensor_tensor(q["Y"][:], q["yh"][:], p3[:, 384:512], A.add), (bk[3],), tag="Y")
+                op("V", 0.06 + 128 * 3.5 * CY, ("Y" + b, "rp"), ("X",),
+                   lambda e, q=q, c0=c0: e.tensor_copy(T.X[:, 0:8192].indirect(T.rp[:, 16 + c0:24 + c0]), q["Y"][:]), tag="scat")
+    return ops, lanes, peer
+
+
+def schedule(ops):
+    n = len(ops)
+    succ = [[] for _ in range(n)]
+    for o in ops:
+        for d in o["wait"] | o["order"]: succ[d].append(o["i"])
+    pr = [0.0] * n
+    for i in range(n - 1, -1, -1):
+        pr[i] = ops[i]["c"] + max([pr[s] + (WAKE if ops[s]["q"] != ops[i]["q"] else .02) for s in succ[i]], default=0.0)
+    need = [len(o["wait"] | o["order"]) for o in ops]
+    ready, fin, avail, order = {}, [0.0] * n, {}, []
+    rt = [0.0] * n
+    for i in range(n):
+        if not need[i]: ready[i] = 0.0
+    while ready:
+        st = {}
+        for i, r in ready.items():
+            q = ops[i]["q"]; q = "A" if q == "AD" else q
+            st[i] = max(r, avail.get(q, 0.0)) if q != "R" else r
+        best = {}
+        for i in st:
+            q = ops[i]["q"]
+            if q not in best or st[i] < best[q]: best[q] = st[i]
+        q0 = min(best, key=lambda q: best[q])
+        cand = [i for i in st if ops[i]["q"] == q0 and st[i] <= best[q0] + LOOK[q0]]
+        i = max(cand, key=lambda k: (pr[k] + PRI.get(ops[k]["tag"], 0.0), -k))
+        o = ops[i]; q = "A" if o["q"] == "AD" else o["q"]
+        s = st[i]
+        fin[i] = s + o["c"]
+        if q != "R": avail[q] = s + (0.1 if o["q"] in ("AD", "S") else o["c"])
+        o["s"] = s
+        order.append(i)
+        del ready[i]
+        for k in succ[i]:
+            need[k] -= 1
+            wk = WAKE if ops[k]["q"] != o["q"] else .05
+            rt[k] = max(rt[k], fin[i] + wk)
+            if not need[k]: ready[k] = rt[k]
+    return order, max(fin)
+
+
+def rank_program(g, core, T, topo):
+    if T.rank_of(core) is None:
+        return
+    ops, lanes, peer = make_ops(core, T, topo)
+    order, est = schedule(ops)
+    eng = {"V": g.vector, "A": g.scalar, "T": g.tensor, "G": g, "S": g.sync, "AD": g.scalar}
+    qsem = {"V": "qV", "A": "qA", "T": "qT", "G": "qG"}
+    cnt, known, snap, done = {}, {}, {}, {}
+    sent = 0
+    for i in order:
+        o = ops[i]
+        if o["q"] == "R":
+            done[i] = (o["sem"], o["n"]); snap[i] = {o["sem"]: o["n"]}
+            continue
+        qn = "A" if o["q"] == "AD" else o["q"]
+        e = eng[o["q"]]
+        kn = known.setdefault(qn, {})
+        for d in sorted(o["wait"], key=lambda d: -ops[d].get("s", 0.0)):
+            s, v = done[d]
+            if kn.get(s, 0) >= v: continue
+            e.wait_ge(T.sem[s], v)
+            for k, x in snap[d].items():
+                if kn.get(k, 0) < x: kn[k] = x
+        if o["sem"] == "snd":
+            _, src, dst, sem, to = o["fn"]
+            ln = lanes(core, to)
+            rid, pid, _ = topo.addr(to)
+            g.remote_dma(out_ap=T[dst][:, 0:128], in_ap=src, remote_sem=T.sem[sem], local_sem=T.sem.snd, pid=pid, routing_id=rid,
+                         dma_engine_mask=sum(1 << x for x in ln))
+            sent += len(ln)
+            done[i] = ("snd", sent); snap[i] = dict(kn)
+        else:
+            r = o["fn"](e)
+            if o["q"] in ("S", "AD"):
+                r.then_inc(T.sem[o["sem"]], 16)
+                done[i] = (o["sem"], o["n"]); cnt[o["sem"]] = o["n"]
+            else:
+                s = qsem[o["q"]]
+                cnt[s] = cnt.get(s, 0) + 1
+                r.then_inc(T.sem[s], 1)
+                done[i] = (s, cnt[s])
+            snap[i] = dict(kn); snap[i][done[i][0]] = done[i][1]
+    for s, v in cnt.items():
+        g.wait_ge(T.sem[s], v)
+    g.wait_ge(T.sem.snd, sent)
+    for o in ops:
+        if o["q"] == "R": g.wait_ge(T.sem[o["sem"]], o["n"])

@@ -4,62 +4,57 @@ A = AluOpType
 F = ActivationFunctionType
 RO = 4
 BF, F32, I32, U16 = "bfloat16", "float32", "int32", "uint16"
+MAGIC = 12582912.0
 
 SCRATCH = {}
+for _n in ("p0A", "p1A", "p2A", "p0B", "p1B", "p2B", "z0", "z1"):
+    SCRATCH[_n] = ("psum", [128, 512], F32)
 for _b in "AB":
-    for _n in ("p0", "p1", "p2", "p3"):
-        SCRATCH[_n + _b] = ("psum", [128, 512], F32)
-for _b in "AB":
-    for _n in ("G", "M", "H", "Zx", "D", "AD"):
+    for _n in ("G", "M", "H", "Gc", "P"):
         SCRATCH[_n + _b] = ("sbuf", [128, 2048], BF)
-    for _n, _d in (("Si", I32), ("Sm", I32), ("us", F32), ("Lp", F32), ("t32", I32), ("c32", I32), ("Wm", F32),
-                   ("cm", F32), ("Rm", F32), ("OHc", F32), ("Km", F32), ("yh", I32), ("pass", BF),
-                   ("OH", BF), ("Y", BF), ("zo", U16), ("cu", U16), ("ej", BF)):
+    for _n, _d in (("us", F32), ("Lp", F32), ("t32", I32), ("c32", I32), ("Wm", BF), ("Ws", F32), ("cm", F32), ("OHc", F32),
+                   ("Km", F32), ("pm", F32), ("mn", F32), ("Y", I32), ("pass", BF), ("q", BF), ("OH", BF), ("Z", BF), ("Zt", BF),
+                   ("Zh", F32), ("cu", U16), ("ej", BF)):
         SCRATCH[_n + _b] = ("sbuf", [128, 128], _d)
-    SCRATCH["pn" + _b] = ("sbuf", [128, 256], F32)
     SCRATCH["ys" + _b] = ("sbuf", [128, 256], F32)
     SCRATCH["ki" + _b] = ("sbuf", [128, 16], I32)
     SCRATCH["ku" + _b] = ("sbuf", [128, 8], U16)
+    SCRATCH["zo" + _b] = ("sbuf", [128, 16], U16)
     SCRATCH["su" + _b] = ("sbuf", [128, 384], U16)
-    SCRATCH["sr" + _b] = ("sbuf", [128, 384], F32)
-    for _t in range(RO):
-        SCRATCH["win%d%s" % (_t, _b)] = ("sbuf", [128, 2048], F32)
-        SCRATCH["lu%d%s" % (_t, _b)] = ("sbuf", [128, 128], U16)
-for _n, _s, _d in (("X", [128, 8192], BF), ("R", [128, 1024], BF), ("Rk", [128, 128], F32), ("ones", [128, 256], BF),
-                   ("E", [128, 144], BF), ("Bd", [128, 128], BF), ("Id", [128, 128], BF), ("Sh", [128, 128], BF),
-                   ("selM", [128, 128], BF), ("Bn", [128, 128], BF), ("Wn", [128, 128], BF), ("Qe", [128, 128], BF),
-                   ("R16", [128, 128], BF), ("mask", [128, 128], BF), ("K8", [128, 8], BF), ("wE", [128, 144], BF),
-                   ("row16", [128, 128], BF), ("rowi", [128, 128], BF), ("Bd32", [128, 128], F32), ("Bu32", [128, 128], F32),
-                   ("I32", [128, 128], F32), ("J32", [128, 128], F32), ("E32", [128, 144], F32), ("z8", [128, 16], F32),
-                   ("cols", [128, 16], F32), ("wi", [128, 1], I32), ("kni", [128, 1], I32), ("limi", [128, 4], I32),
-                   ("limf", [128, 4], F32), ("tub", [128, 256], I32), ("tubf", [128, 256], F32), ("pi", [128, 32], I32),
-                   ("cvb", [128, 32], I32), ("cv", [128, 32], I32), ("zt", [128, 1920], F32), ("Wi", [128, 16], I32),
-                   ("nu", [128, 32], I32), ("nv", [128, 32], I32), ("rp", [128, 32], U16), ("ei", [128, 2], I32),
-                   ("ec", [128, 2], F32), ("one32", [128, 128], F32)):
-    SCRATCH[_n] = ("sbuf", _s, _d)
+    SCRATCH["nw" + _b] = ("sbuf", [128, 512], F32)
+    SCRATCH["lu" + _b] = ("sbuf", [128, 512], U16)
+    SCRATCH["lf" + _b] = ("sbuf", [128, 512], F32)
+    SCRATCH["win" + _b] = ("sbuf", [128, 2048], F32)
+    SCRATCH["rows" + _b] = ("dram", [8, 16, 128], F32)
+for _n, _s, _d in (("X", 8192, BF), ("R", 512, BF), ("Rk", 128, F32), ("ones", 256, BF), ("Exp", 2048, BF),
+                   ("E", 144, BF), ("E2", 144, BF), ("wE", 144, BF), ("wD", 144, BF), ("nE", 144, BF), ("E32", 144, F32),
+                   ("Bd", 128, BF), ("Id", 128, BF), ("Ih", 128, BF), ("In", 128, BF), ("Im", 128, BF), ("Bn", 128, BF), ("Qe", 128, BF),
+                   ("R16", 128, BF), ("mask", 128, BF), ("K8", 16, BF), ("sel", 16, BF), ("CV", 16, BF), ("cr", 256, BF),
+                   ("row16", 128, BF), ("rowi", 128, BF), ("Bd32", 128, F32), ("Bq32", 128, F32), ("I32", 128, F32),
+                   ("z8", 16, F32), ("cols", 16, F32), ("wi", 1, I32), ("kni", 1, I32), ("limi", 4, I32), ("limf", 4, F32),
+                   ("tub", 256, I32), ("pi", 48, I32), ("cvb", 48, I32), ("cv", 32, I32), ("cidx", 8, U16), ("Wi", 16, I32),
+                   ("nu", 16, I32), ("nv", 16, I32), ("rp", 16, U16), ("ei", 2, I32), ("ec", 2, F32)):
+    SCRATCH[_n] = ("sbuf", [128, _s], _d)
 
 SEMAPHORES = ["qV", "qA", "qT", "qG", "lX", "ltub", "lwt", "lkn", "llim", "snd", "out"]
 for _b in "AB":
-    SEMAPHORES += [_n + "%d%s" % (_t, _b) for _n in "wz" for _t in range(RO)]
-    SEMAPHORES += ["au%d%s" % (_t, _b) for _t in range(1, RO)] + ["ar%d%s" % (_t, _b) for _t in range(1, RO)]
+    SEMAPHORES += [_n + "%d%s" % (_t, _b) for _n in "wr" for _t in range(RO)]
+    SEMAPHORES += ["au%d%s" % (_t, _b) for _t in range(1, RO)] + ["af%d%s" % (_t, _b) for _t in range(1, RO)]
 
-CY = 0.83e-3 * 1.2
-PEC = 0.75e-3 * 1.2
+CY = 0.83e-3 * 1.15
+PEC = 0.42e-3 * 1.15
 GA = 1.5
-WAKE = 0.12
-PRI = dict(Abs0A=107,Abs0B=-224,Abs1A=-94,Abs1B=-31,Abs2A=-372,Abs2B=-627,Abs3A=322,Abs3B=-436,B=-69,CP0A=-224,CP0B=-356,
-    CP1A=-370,CP1B=317,EA=254,EB=21,EaccA=523,EaccB=-161,G10A=387,G10B=-448,G11A=208,G11B=307,G20A=219,G20B=-180,G21A=-381,
-    G21B=485,G22A=-937,G22B=216,G23A=41,G23B=40,KmA=913,KmB=-364,KpA=588,KpB=-12,LpA=-95,LpB=83,OHA=-510,OHB=54,OHTA=681,
-    OHTB=168,OHcA=-216,OHcB=350,RmA=207,RmB=-136,S0A=523,S0B=90,S1A=679,S1B=279,SC0A=-114,SC0B=-22,SC1A=694,SC1B=-272,SqA=751,
-    SqB=-6,WexpA=-632,WexpB=474,WmA=520,WmB=-166,WpA=203,WpB=248,YA=240,YB=39,ZcA=728,ZcB=-69,Zx0A=-97,Zx0B=129,Zx1A=-141,
-    Zx1B=-374,Zx2A=-274,Zx2B=-130,Zx3A=-34,Zx3B=-221,cmA=3,cmB=334,cnt0A=125,cnt0B=-25,cnt1A=316,cnt1B=678,e1=-192,e2=11,
-    e3=-250,k1A=-245,k1B=232,k2A=196,k2B=-74,k3A=125,k3B=377,kcA=-561,kcB=-194,keyA=126,keyB=649,nat1A=100,nat1B=230,nat2A=312,
-    nat2B=509,npassA=-309,npassB=320,outA=413,outB=538,passA=566,passB=232,revA=113,revB=-114,revcA=-31,revcB=-222,s4A=382,
-    s4B=582,s5A=187,s5B=567,s6A=-629,s6B=-145,s7A=103,s7B=640,s8A=345,s8B=-104,scanA=65,scanB=526,scatA=-30,scatB=-3,scrA=-60,
-    scrB=-65,selA=866,selB=472,sendrA=70,sendrB=-10,senduA=211,senduB=505,suA=-195,suB=126,uA=823,uB=451,usA=-23,usB=-153,
-    w1A=-76,w1B=20,w2=-71,w3=-305,w4=196,w5=557,yhA=-410,yhB=199,ylA=-41,ylB=-98,yzA=-366,yzB=306,zoA=518,zoB=141)
-LOOK = {"V": 0.0, "A": 0.0, "T": 0.2, "G": 0.0, "S": 0.0, "AD": 0.0, "R": 0.0}
-G1Q = {("A", 0): "A", ("A", 1): "V", ("B", 0): "A", ("B", 1): "A"}
+WAKE = 0.1
+FLY = 3.0
+SELF = 0.05
+ISSUE = 0.1
+PASSES = 6
+G1Q = {"A": "AVAV", "B": "AAAA"}
+G2Q = {"A": "AAAA", "B": "AAAA"}
+CPQ = {"A": "VVVV", "B": "AAAA"}
+MXQ = {"A": "VVVV", "B": "VVVV"}
+OPQ = {"pass": "V", "Z": "A", "mn": "A", "late": "V"}
+PLAN = []
 
 
 def vcost(n, f=1.0): return 0.05 + max(64, n * f) * CY
@@ -111,6 +106,13 @@ def make_ops(core, T, topo):
     def DMA(q, cost, reads, writes, out, in_, sem, tag=""):
         return op(q, cost, reads, writes, lambda e: e.dma_start(out, in_), sem=sem, tag=tag)
 
+    def gather(q, n, reads, writes, out, src, scale=None, tag=""):
+        if q == "A":
+            fn = (lambda e: e.activation(out, src, F.Copy)) if scale is None else (lambda e: e.activation(out, src, F.Copy, scale=scale))
+        else:
+            fn = (lambda e: e.tensor_copy(out, src)) if scale is None else (lambda e: e.tensor_scalar(out, src, scale, None, A.mult))
+        return op(q, gcost(n), reads, writes, fn, tag=tag)
+
     rank = T.rank_of(core)
     ncore = len(T.cores)
     peer = {"A": (T.cores[(rank + 1) % ncore], T.cores[(rank - 1) % ncore]),
@@ -119,288 +121,330 @@ def make_ops(core, T, topo):
     def lanes(s, d):
         return topo.engines(s, d)[:8]
 
-    DMA("AD", 2.0, (), ("tub",), T.tub[:], T.tube[:], "ltub")
-    DMA("AD", 2.0, (), ("wi",), T.wi[:], T.wt[:], "lwt")
-    DMA("AD", 2.0, (), ("kni",), T.kni[:], T.kn[:], "lkn")
-    DMA("AD", 2.0, (), ("limi",), T.limi[:], T.lim[:], "llim")
+    half = {"A": slice(0, 128), "B": slice(128, 256)}
+
+    small = [DMA("S", 2.0, (), ("tub",), T.tub[:], T.tube[:], "ltub"), DMA("AD", 2.0, (), ("wi",), T.wi[:], T.wt[:], "lwt"),
+             DMA("AD", 2.0, (), ("kni",), T.kni[:], T.kn[:], "lkn"), DMA("S", 2.0, (), ("limi",), T.limi[:], T.lim[:], "llim")]
     DMA("S", 11.0, (), ("X",), T.X[:], T.field[:], "lX")
-    V(256, .5, (), ("ones",), lambda e: e.memset(T.ones[:], 1.0))
-    V(128, 1, (), ("one32",), lambda e: e.memset(T.one32[:], 1.0))
-    ON, O3 = T.ones, T.one32
+    for i in small: ops[i]["first"] = True
+    ON, col, cr = T.ones, T.cols, T.cr
+    V(256, .5, (), ("ones",), lambda e: e.memset(ON[:], 1.0))
     Gc(128, ("ones",), ("Bd0",), lambda e: e.affine_select(T.Bd[:], ON[:, 0:128], [[-16, 8], [0, 16]], A.is_ge, 0.0, 0, 1))
     Gc(128, ("Bd0",), ("Bd",), lambda e: e.affine_select(T.Bd[:], T.Bd[:], [[16, 8], [0, 16]], A.is_ge, 0.0, 15, -1))
     Gc(128, ("ones",), ("Id",), lambda e: e.affine_select(T.Id[:], ON[:, 0:128], [[-1, 128]], A.is_equal, 0.0, 0, 1))
-    Gc(8, ("one32",), ("z8",), lambda e: e.affine_select(T.z8[:, 0:8], O3[:, 0:8], [[-16, 8]], A.is_equal, 0.0, 0, 1))
-    Gc(128, ("one32",), ("J0",), lambda e: e.affine_select(T.J32[:], O3[:], [[-16, 8], [1, 16]], A.is_equal, 0.0, -16, 1))
-    Gc(8, ("one32",), ("z15",), lambda e: e.affine_select(T.z8[:, 8:16], O3[:, 0:8], [[-16, 8]], A.is_equal, 0.0, -15, 1))
+    Gc(8, ("ones",), ("z8",), lambda e: e.affine_select(T.z8[:, 0:8], ON[:, 0:8], [[-16, 8]], A.is_equal, 0.0, 0, 1))
+    Gc(8, ("ones",), ("z15",), lambda e: e.affine_select(T.z8[:, 8:16], ON[:, 0:8], [[-16, 8]], A.is_equal, 0.0, -15, 1))
     Gc(144, ("ones",), ("E0",), lambda e: e.affine_select(T.E[:], ON[:, 0:144], [[0, 9], [1, 16]], A.is_equal, 0.0, -15, 0))
     Gc(144, ("E0",), ("E1",), lambda e: e.affine_select(T.E[:], T.E[:], [[-16, 9], [0, 16]], A.is_ge, 0.0, 0, 1))
     Gc(144, ("E1",), ("E",), lambda e: e.affine_select(T.E[:], T.E[:], [[16, 9], [0, 16]], A.is_ge, 0.0, 15, -1))
-    Gc(128, ("ones",), ("Sh",), lambda e: e.affine_select(T.Sh[:], ON[:, 0:128], [[-1, 128]], A.is_equal, 0.0, -1, 1))
     Gc(128, ("ones",), ("R16",), lambda e: e.affine_select(T.R16[:], ON[:, 0:128], [[0, 8], [1, 16]], A.is_equal, 0.0, 0, -1))
     Gc(128, (), ("row16",), lambda e: e.iota(T.row16[:], [[16, 128]], 0, 0, allow_small_or_imprecise_dtypes=True))
     Gc(128, (), ("rowi",), lambda e: e.iota(T.rowi[:], [[0, 8], [1, 16]], 0, 0, allow_small_or_imprecise_dtypes=True))
-    Gc(32, (), ("pi",), lambda e: e.iota(T.pi[:], [[0, 32]], 0, 1))
-    Gc(16, (), ("cvb0",), lambda e: e.iota(T.cvb[:, 0:16], [[0, 2], [16, 8]], 0, 0))
-    Gc(16, (), ("cvb1",), lambda e: e.iota(T.cvb[:, 16:32], [[512, 16]], 0, 0))
+    Gc(32, (), ("pi",), lambda e: e.iota(T.pi[:, 0:32], [[0, 32]], 0, 1))
+    Gc(8, (), ("cvb0",), lambda e: e.iota(T.cvb[:, 0:8], [[256, 8]], 0, 0))
+    Gc(8, (), ("cvb1",), lambda e: e.iota(T.cvb[:, 8:16], [[16, 8]], 0, 0))
+    Gc(16, (), ("cvb2",), lambda e: e.iota(T.cvb[:, 16:32], [[512, 16]], 0, 0))
+    Gc(8, (), ("cvb3",), lambda e: e.iota(T.cvb[:, 32:40], [[16, 8]], 15, 0))
+    V(2048, .5, (), ("Exp0",), lambda e: e.memset(T.Exp[:], 1.0))
+    Gc(2048, ("Exp0",), ("Exp",), lambda e: e.affine_select(T.Exp[:], T.Exp[:], [[-1, 128], [0, 16]], A.is_equal, 0.0, 0, 1))
+    V(2048, .5, (), ["HA%d" % j for j in range(4)], lambda e: e.memset(T.HA[:], 0.0))
     for b in "AB":
-        s = slice(0, 128) if b == "A" else slice(128, 256)
-        V(128, 1, ("tub",), ("lu0" + b,), lambda e, b=b, s=s: e.tensor_copy(T["lu0" + b][:], T.tub[:, s]))
-    V(256, 1, ("tub",), ("tubf",), lambda e: e.tensor_copy(T.tubf[:], T.tub[:]))
-    for b in "AB":
-        s = slice(0, 128) if b == "A" else slice(128, 256)
-        P(512, ("J0", "tubf"), lambda e, b=b, s=s: e.matmul(T["p3" + b][:, 0:128], T.J32[:], T.tubf[:, s], True, True), ("3" + b,))
-        C(128, (), ("win0%s.0" % b,), lambda e, b=b: e.activation(T["win0" + b][:, 0:128], T["p3" + b][:, 0:128], F.Copy), ("3" + b,))
-    V(1920, 1, (), ("zt",), lambda e: e.memset(T.zt[:], 0.0))
-    for t in range(RO):
-        for b in "AB":
-            DMA("S", 2.0, ("zt",), ("win%d%s.z" % (t, b),), T["win%d%s" % (t, b)][112:128, 128:2048], T.zt[112:128, :], "z%d%s" % (t, b))
-    col = T.cols
+        V(128, 1, ("tub",), ("lf0" + b,), lambda e, b=b: e.tensor_copy(T["lf" + b][:, 0:128], T.tub[:, half[b]]))
+        V(128, 1, ("tub",), ("lu0" + b,), lambda e, b=b: e.tensor_copy(T["lu" + b][:, 0:128], T.tub[:, half[b]]))
+        C(2048, ["HA%d" % j for j in range(4)], ["win%s%d" % (b, j) for j in range(16)], lambda e, b=b: e.activation(T["win" + b][:], T.HA[:], F.Copy))
     V(8, 1, ("z8",), ("c0",), lambda e: e.tensor_reduce(col[:, 0:1], T.z8[:, 0:8], AxisListType.X, A.add))
     V(8, 1, ("z15",), ("c2",), lambda e: e.tensor_reduce(col[:, 2:3], T.z8[:, 8:16], AxisListType.X, A.add, negate=True))
     V(1, 1, ("c0",), ("c1",), lambda e: e.tensor_scalar(col[:, 1:2], col[:, 0:1], -1.0, 1.0, A.mult, A.add))
-    V(1, 1, ("c0",), ("c3",), lambda e: e.tensor_scalar(col[:, 3:4], col[:, 0:1], -7.0, 6.0, A.mult, A.add))
-    V(1, 1, ("c0",), ("c8",), lambda e: e.tensor_scalar(col[:, 8:9], col[:, 0:1], 2048.0, -128.0, A.mult, A.add))
     V(1, 1, ("wi",), ("c4",), lambda e: e.tensor_copy(col[:, 4:5], T.wi[:]))
     V(1, 1, ("kni",), ("c5",), lambda e: e.tensor_scalar(col[:, 5:6], T.kni[:], 8.0, None, A.mult))
-    V(1, 1, ("c5",), ("c9",), lambda e: e.tensor_tensor(col[:, 9:10], col[:, 5:6], col[:, 5:6], A.mult))
-    V(1, 1, ("c9",), ("c6",), lambda e: e.tensor_scalar(col[:, 6:7], col[:, 9:10], -1.0, None, A.mult))
+    V(1, 1, ("c5",), ("c6",), lambda e: e.tensor_scalar(col[:, 6:7], col[:, 5:6], col[:, 5:6], -1.0, A.mult, A.mult))
+    V(1, 1, ("c5",), ("c8",), lambda e: e.tensor_scalar(col[:, 8:9], col[:, 5:6], 2047.5, None, A.add))
     V(4, 1, ("limi",), ("limf",), lambda e: e.tensor_copy(T.limf[:], T.limi[:]))
+    V(1, 1, ("limf",), ("thr",), lambda e: e.tensor_copy(col[:, 7:8], T.limf[:, 0:1]))
+    sigmoid = "A" in CPQ["A"] + CPQ["B"]
+
+    def nthr():
+        if sigmoid: V(1, 1, ("thr",), ("nthr",), lambda e: e.tensor_scalar(col[:, 9:10], col[:, 7:8], -256.0, 128.0, A.mult, A.add), tag="e4")
+    nthr()
+    if sigmoid or OPQ["pass"] == "A":
+        C(1400, ("ones",), ("ejA",), lambda e: e.activation(T.ejA[:], ON[:, 0:128], F.Sigmoid))
+    V(128, .5, ("Id",), ("Im",), lambda e: e.tensor_scalar(T.Im[:], T.Id[:], -1.0, None, A.mult))
+    V(1, 1, (), ("E20",), lambda e: e.memset(T.E2[:, 0:1], 0.0))
+    V(143, 2, ("E",), ("E21",), lambda e: e.tensor_tensor(T.E2[:, 1:144], T.E[:, 1:144], T.E[:, 0:143], A.subtract))
     V(144, .5, ("E", "c4"), ("wE",), lambda e: e.tensor_scalar(T.wE[:], T.E[:], col[:, 4:5], None, A.mult))
-    V(1024, .5, (), ("R0",), lambda e: e.memset(T.R[:], 0.0))
-    V(64, .5, ("R0",), ("R",), lambda e: e.memset(T.R[:, 0:1024:16], 255.0))
-    V(128, 2, ("Sh", "Bd"), ("ShB",), lambda e: e.tensor_tensor(T.Sh[:], T.Sh[:], T.Bd[:], A.mult))
-    V(128, 2, ("Id", "ShB"), ("selM",), lambda e: e.tensor_tensor(T.selM[:], T.Id[:], T.Sh[:], A.subtract))
+    V(144, .5, ("E20", "E21", "c4"), ("wD",), lambda e: e.tensor_scalar(T.wD[:], T.E2[:], col[:, 4:5], None, A.mult))
+    V(144, .5, ("E",), ("nE",), lambda e: e.tensor_scalar(T.nE[:], T.E[:], -16384.0, None, A.mult))
+    V(144, 1, ("E",), ("E32",), lambda e: e.tensor_copy(T.E32[:], T.E[:]))
+    V(512, .5, (), ("R0",), lambda e: e.memset(T.R[:], 0.0))
+    V(32, .5, ("R0",), ("R",), lambda e: e.memset(T.R[:, 0:512:16], 255.0))
     V(128, .5, ("Bd", "c1"), ("Bn",), lambda e: e.tensor_scalar(T.Bn[:], T.Bd[:], col[:, 1:2], None, A.mult))
     V(128, 1, ("Bd",), ("Bd32",), lambda e: e.tensor_copy(T.Bd32[:], T.Bd[:]))
-    V(128, 1, ("Bd",), ("Bu32",), lambda e: e.tensor_scalar(T.Bu32[:], T.Bd[:], 2048.0, None, A.mult))
-    V(128, .5, ("Bd", "c8"), ("Wn",), lambda e: e.tensor_scalar(T.Wn[:], T.Bd[:], col[:, 8:9], None, A.mult))
+    V(128, 1, ("Bd",), ("Bq32",), lambda e: e.tensor_scalar(T.Bq32[:], T.Bd[:], 1.0 / 4096, None, A.mult))
     V(128, .5, ("ones", "c2"), ("Qe",), lambda e: e.tensor_scalar(T.Qe[:], ON[:, 0:128], col[:, 2:3], None, A.mult))
-    P(128, ("R16",), lambda e: e.matmul(T.p2A[:, 0:128], T.R16[:], T.R16[:], True, True), ("2A",))
-    V(128, 1, (), ("mask",), lambda e: e.tensor_copy(T.mask[:], T.p2A[:, 0:128]), ("2A",))
-    V(8, 1, ("Bd",), ("K8",), lambda e: e.tensor_scalar(T.K8[:], T.Bd[:, 0:128:16], 4096.0, None, A.mult))
-    V(128, 1, ("Id", "c1"), ("I32",), lambda e: e.tensor_scalar(T.I32[:], T.Id[:], col[:, 1:2], None, A.mult))
-    V(144, 1, ("E",), ("E32",), lambda e: e.tensor_copy(T.E32[:], T.E[:]))
-    V(128, 1, (), ("Rk0",), lambda e: e.memset(T.Rk[:], 0.0))
+    V(128, .5, ("Id",), ("Ih",), lambda e: e.tensor_scalar(T.Ih[:], T.Id[:], 0.5, None, A.mult))
+    V(128, .5, ("Id",), ("In",), lambda e: e.tensor_scalar(T.In[:], T.Id[:], -4096.0, None, A.mult))
+    V(128, 1, ("Id",), ("I32",), lambda e: e.tensor_copy(T.I32[:], T.Id[:]))
+    P(128, ("R16",), lambda e: e.matmul(T.z0[:, 0:128], T.R16[:], T.R16[:], True, True), ("z0",))
+    V(128, 1, (), ("mask",), lambda e: e.tensor_copy(T.mask[:], T.z0[:, 0:128]), ("z0",))
+    V(8, 1, ("Bd",), ("K8a",), lambda e: e.tensor_scalar(T.K8[:, 0:8], T.Bd[:, 0:128:16], 8192.0, None, A.mult))
+    V(8, 1, ("Bd",), ("K8b",), lambda e: e.tensor_scalar(T.K8[:, 8:16], T.Bd[:, 0:128:16], -4096.0, None, A.mult))
+    V(8, 1, ("Bd",), ("sela",), lambda e: e.tensor_copy(T.sel[:, 0:8], T.Bd[:, 0:128:16]))
+    V(8, 1, ("Bd",), ("selb",), lambda e: e.tensor_scalar(T.sel[:, 8:16], T.Bd[:, 0:128:16], 128.0, None, A.mult))
+    V(128, 1, (), ("Rk0",), lambda e: e.memset(T.Rk[:], -33554432.0))
     V(8, 1, ("Rk0",), ("Rk",), lambda e: e.memset(T.Rk[:, 0:128:16], 33554432.0))
-    V(32, 1, ("pi",), ("pi2",), lambda e: e.tensor_scalar(T.pi[:], T.pi[:], 15, None, A.bitwise_and))
-    V(16, 1, ("pi2",), ("pi3",), lambda e: e.tensor_scalar(T.pi[:, 16:32], T.pi[:, 16:32], 32, None, A.mult))
-    V(32, 2, ("pi2", "pi3", "cvb0", "cvb1"), ("cv",), lambda e: e.tensor_tensor(T.cv[:], T.pi[:], T.cvb[:], A.add))
-    V(1, 1, ("limf",), ("thr",), lambda e: e.tensor_copy(col[:, 7:8], T.limf[:, 0:1]))
+    V(128, .5, (), ("cr0",), lambda e: e.memset(cr[0:2, 0:128], 0.0))
+    V(8, .5, ("cr0",), ("cr1",), lambda e: e.memset(cr[0:2, 0:128:16], 0.5))
+    V(8, .5, ("cr1",), ("crS",), lambda e: e.memset(cr[0:1, 0:128:16], -2048.0))
+    V(128, .5, (), ("cr2",), lambda e: e.memset(cr[0:1, 128:256], 90112.0))
+    V(8, .5, ("cr2",), ("crX",), lambda e: e.memset(cr[0:1, 128:256:16], -1048576.0))
+    V(32, 1, ("pi",), ("pi2",), lambda e: e.tensor_scalar(T.pi[:, 0:32], T.pi[:, 0:32], 15, None, A.bitwise_and))
+    V(8, 1, ("pi2",), ("pi3",), lambda e: e.tensor_scalar(T.pi[:, 0:8], T.pi[:, 0:8], 16, None, A.mult))
+    V(16, 1, ("pi2",), ("pi4",), lambda e: e.tensor_scalar(T.pi[:, 16:32], T.pi[:, 16:32], 32, None, A.mult))
+    V(32, 2, ("pi3", "pi4", "cvb0", "cvb1", "cvb2"), ("cv",), lambda e: e.tensor_tensor(T.cv[:], T.pi[:, 0:32], T.cvb[:, 0:32], A.add))
+    V(16, 1, ("cv",), ("CV",), lambda e: e.tensor_copy(T.CV[:], T.cv[:, 0:16]))
+    V(8, 1, ("cvb3",), ("cidx",), lambda e: e.tensor_copy(T.cidx[:], T.cvb[:, 32:40]))
 
     pend = {}
-    for t in range(RO):
-        last = t == RO - 1
+
+    def window(t, b):
+        ts = slice(t * 128, t * 128 + 128)
         if t:
-            for b in "AB":
-                src = peer[b][1]
-                op("R", 2.2, (), ("lu%d%s" % (t, b),), None, sem="au%d%s" % (t, b), cnt=len(lanes(src, core)), sched=(pend["u" + b],))
-                op("R", 2.2, (), ("win%d%s.0" % (t, b),), None, sem="ar%d%s" % (t, b), cnt=len(lanes(src, core)), sched=(pend["r" + b],))
-        for k in (1, 2, 4, 8):
-            for b in "AB":
-                w = T["win%d%s" % (t, b)]; n = "win%d%s." % (t, b)
-                rd = [n + "z", n + "0"] + [n + str(j) for j in (1, 2, 4) if j < k]
-                DMA("S", 2.0 + k * .06, rd, (n + str(k),), w[0:128 - k, 128 * k:256 * k], w[k:128, 0:128 * k], "w%d%s" % (t, b))
-        for b in "AB":
-            cur[0] = b
-            bk = [str(j) + b for j in range(4)]
-            p0, p1, p2, p3 = T["p0" + b], T["p1" + b], T["p2" + b], T["p3" + b]
-            lu = T["lu%d%s" % (t, b)]; luk = "lu%d%s" % (t, b)
-            tl = {n: T[n + b] for n in ("G", "M", "H", "Si", "Sm", "us", "Lp", "t32", "c32", "Wm", "pass", "zo", "cu", "ej", "Zx")}
-            G, M, H, Zx = tl["G"], tl["M"], tl["H"], tl["Zx"]
-            V(128, 1, (luk, "c6"), ("Lp" + b,), lambda e, d=tl["Lp"], s=lu: e.tensor_scalar(d[:], s[:], 16.0, col[:, 6:7], A.mult, A.add), tag="Lp")
-            for h in (0, 1):
-                f = slice(h * 1024, h * 1024 + 1024); o = slice(h * 64, h * 64 + 64)
-                gk, mk, hk = "G%s%d" % (b, h), "M%s%d" % (b, h), "H%s%d" % (b, h)
-                if G1Q[(b, h)] == "A":
-                    op("A", gcost(1024), ("X", luk), (gk,), lambda e, G=G, f=f, o=o, lu=lu: e.activation(G[:, f], T.X[:, 0:8192].indirect(lu[:, o]), F.Copy), tag="G1%d" % h)
-                else:
-                    op("V", gcost(1024), ("X", luk), (gk,), lambda e, G=G, f=f, o=o, lu=lu: e.tensor_copy(G[:, f], T.X[:, 0:8192].indirect(lu[:, o])), tag="G1%d" % h)
-                V(1024, .5, (gk, "R"), (mk,), lambda e, G=G, M=M, f=f: e.tensor_tensor_scan(M[:, f], T.R[:], G[:, f], 0.0, A.max, A.min), tag="SC%d" % h)
-                V(1024, .5, (mk, "thr"), (hk,), lambda e, H=H, M=M, f=f: e.tensor_scalar(H[:, f], M[:, f], col[:, 7:8], None, A.is_ge), tag="CP%d" % h)
+            op("R", FLY, (), ("lf%d%s" % (t, b),), None, sem="af%d%s" % (t, b), cnt=len(lanes(peer[b][1], core)), sched=(pend["f" + b],))
+        DMA("S", 2.0, ("lf%d%s" % (t, b),), ("rows" + b,), T["rows" + b][:], T["lf" + b][:, ts], "r%d%s" % (t, b), tag="D1")
+        for j in range(1, 16):
+            DMA("S", 2.5, ("rows" + b,), ("win%s%d" % (b, j),), T["win" + b][j:128:16, 128 * j:2048], T["rows" + b][:, 1:17 - j, :],
+                "w%d%s" % (t, b), tag="Dj")
 
-                def mm8(e, dst, w, src, i0, h=h, o=o):
-                    for i in range(i0, i0 + 8):
-                        r = e.matmul(dst[:, o], w[:, 15 - i:143 - i], src[:, h * 1024 + i:h * 1024 + 1024:16], i == 0, i == 15)
-                    return r
-                for i0 in (0, 8):
-                    P(512, (gk, "wE"), lambda e, d=p1, s=G, f=mm8, i0=i0: f(e, d, T.wE, s, i0), (bk[1],), tag="S%d" % h)
-                for i0 in (0, 8):
-                    P(512, (hk, "E"), lambda e, d=p0, s=H, f=mm8, i0=i0: f(e, d, T.E, s, i0), (bk[0],), tag="cnt%d" % h)
-            V(128, 1, (), ("Si" + b,), lambda e, d=tl["Si"], s=p1: e.tensor_copy(d[:], s[:, 0:128]), (bk[1],), tag="s7")
-            V(128, 1, ("Si" + b,), ("Sm" + b,), lambda e, d=tl["Sm"], s=tl["Si"]: e.tensor_scalar(d[:], s[:], 4095, None, A.bitwise_and), tag="s8")
-            V(128, 1, ("c3",), ("pass" + b,), lambda e, d=tl["pass"], s=p0: e.tensor_scalar(d[:], s[:, 0:128], col[:, 3:4], None, A.is_ge), (bk[0],), tag="pass")
-
-            def selnoff(e, p2=p2, ps=tl["pass"]):
-                e.matmul(p2[:, 0:128], T.selM[:], ps[:], True, True)
-                e.matmul(p2[:, 128:256], ON[0:1, 0:128], T.row16[0:1, :], True, False)
-                return e.matmul(p2[:, 128:256], T.Bn[:], ps[:], False, True)
-            P(384, ("pass" + b, "selM", "Bn", "ones", "row16"), selnoff, (bk[2],), tag="sel")
-            V(128, 1, ("Sm" + b,), ("us" + b,), lambda e, d=tl["us"], s=tl["Sm"], p2=p2: e.tensor_tensor(d[:], s[:], p2[:, 0:128], A.mult), (bk[2],), tag="us")
-            V(128, 1, (), ("zo" + b,), lambda e, d=tl["zo"], p2=p2: e.tensor_copy(d[:], p2[:, 128:256]), (bk[2],), tag="zo")
-            P(512, ("us" + b, "Bd32"), lambda e, d=p3, s=tl["us"]: e.matmul(d[:, 0:128], T.Bd32[:], s[:], True, True), (bk[3],), tag="u")
-            C(128, ("c5",), (), lambda e, d=p3: e.activation(d[:, 128:256], d[:, 0:128], F.Square, bias=col[:, 5:6]), (bk[3],), tag="Sq")
-            V(128, 1, ("Lp" + b,), ("t32" + b,), lambda e, d=tl["t32"], p3=p3, l=tl["Lp"]: e.tensor_tensor(d[:], p3[:, 128:256], l[:], A.add), (bk[3],), tag="s4")
-            V(128, 1, ("t32" + b,), ("c32" + b,), lambda e, d=tl["c32"], s=tl["t32"]: e.tensor_scalar(d[:], s[:], 4, 8191, A.arith_shift_right, A.bitwise_and), tag="s5")
-            V(128, 1, ("c32" + b,), ("cu" + b,), lambda e, d=tl["cu"], s=tl["c32"]: e.tensor_copy(d[:], s[:]), tag="s6")
-            for h4 in range(4):
-                f = slice(h4 * 512, h4 * 512 + 512); o = slice(h4 * 32, h4 * 32 + 32)
-                op("A", gcost(512), ("zo" + b, "M%s0" % b, "M%s1" % b), ("Zx%s%d" % (b, h4),),
-                   lambda e, d=Zx, M=M, z=tl["zo"], f=f, o=o: e.activation(d[:, f], M[:, 0:2048].indirect(z[:, o]), F.Copy), tag="Zx%d" % h4)
-            C(128, ("pass" + b,), (), lambda e, d=p3, s=tl["pass"]: e.activation(d[:, 256:384], s[:], F.Copy, bias=1.0, scale=-1.0), (bk[3],), tag="npass")
-
-            def wexp(e, p1=p1, ps=tl["pass"], us=tl["us"], last=last):
-                r = e.matmul(p1[:, 128:256], ps[:], T.Wn[:], True, last)
-                if not last:
-                    r = e.matmul(p1[:, 128:256], us[:], T.Bu32[:], False, True)
-                return r
-            P(640, ("pass" + b, "us" + b, "Wn", "Bu32"), wexp, (bk[1],), tag="Wexp")
-            V(128, 1, ("mask",), ("Wm" + b,), lambda e, d=tl["Wm"], p1=p1: e.tensor_tensor(d[:], p1[:, 128:256], T.mask[:], A.mult), (bk[1],), tag="Wm")
-            P(256, ("Wm" + b, "Bd32"), lambda e, p1=p1, s=tl["Wm"]: e.matmul(p1[:, 256:264], s[:], T.Bd32[:, 0:128:16], True, True), (bk[1],), tag="Wp")
-            c0 = 0 if b == "A" else 8
-            V(8, 1, (), ("Wi" + b,), lambda e, p1=p1, c0=c0: e.tensor_copy(T.Wi[:, c0:c0 + 8], p1[:, 256:264]), (bk[1],), tag="w1")
-            if not last:
-                P(128, ("Qe", "pass" + b), lambda e, d=p0, s=tl["pass"]: e.matmul(d[:, 128:256], T.Qe[:], s[:], True, True), (bk[0],), tag="E")
-                ec = T.ec[:, 0:1] if b == "A" else T.ec[:, 1:2]
-                C(128, (), ("ec" + b, "ej" + b), lambda e, d=tl["ej"], s=p0, c=ec: e.activation(d[:], s[:, 128:256], F.Copy, accum_out=c), (bk[0],), tag="Eacc")
-        cur[0] = ""
-        V(16, 1, ("WiA", "WiB"), ("nu0",), lambda e: e.tensor_scalar(T.nu[:, 0:16], T.Wi[:], 2047, None, A.bitwise_and), tag="w2")
-        if last:
-            V(16, 2, ("nu0", "cv"), ("nv",), lambda e: e.tensor_tensor(T.nv[:, 0:16], T.nu[:, 0:16], T.cv[:, 0:16], A.add), tag="w4")
-            V(16, 1, ("nv",), ("rp",), lambda e: e.tensor_copy(T.rp[:, 0:16], T.nv[:, 0:16]), tag="w5")
-        else:
-            V(16, 1, ("WiA", "WiB"), ("nu1",), lambda e: e.tensor_scalar(T.nu[:, 16:32], T.Wi[:], 11, 31, A.arith_shift_right, A.bitwise_and), tag="w3")
-            V(32, 2, ("nu0", "nu1", "cv"), ("nv",), lambda e: e.tensor_tensor(T.nv[:], T.nu[:], T.cv[:], A.add), tag="w4")
-            V(32, 1, ("nv",), ("rp",), lambda e: e.tensor_copy(T.rp[:], T.nv[:]), tag="w5")
-            V(1, 1, ("ecA", "ecB"), ("ei",), lambda e: e.tensor_tensor(T.ei[:, 0:1], T.ec[:, 0:1], T.ec[:, 1:2], A.add), tag="e1")
-            V(1, 1, ("ei",), ("ej2",), lambda e: e.tensor_scalar(T.ei[:, 1:2], T.ei[:, 0:1], 7, None, A.bitwise_and), tag="e2")
-            V(1, 2, ("ej2", "limf"), ("thr",), lambda e, t=t: e.tensor_tensor(col[:, 7:8], T.ei[:, 1:2], T.limf[:, t + 1:t + 2], A.add), tag="e3")
-        for b in "AB":
-            cur[0] = b
-            D, AD, Zx, cu = T["D" + b], T["AD" + b], T["Zx" + b], T["cu" + b]
-            for h in range(4):
-                f = slice(h * 512, h * 512 + 512); o = slice(h * 32, h * 32 + 32)
-                op("V", gcost(512), ("X", "cu" + b, "Zx%s%d" % (b, h)), ("D%s%d" % (b, h),),
-                   lambda e, D=D, Zx=Zx, cu=cu, f=f, o=o: e.tensor_tensor(D[:, f], T.X[:, 0:8192].indirect(cu[:, o]), Zx[:, f], A.subtract), tag="G2%d" % h)
-                C(512, ("D%s%d" % (b, h),), ("AD%s%d" % (b, h),), lambda e, D=D, AD=AD, f=f: e.activation(AD[:, f], D[:, f], F.Abs), tag="Abs%d" % h)
-        for b in "AB":
-            cur[0] = b
-            bk = [str(j) + b for j in range(4)]
-            p0, p1, p2, p3 = T["p0" + b], T["p1" + b], T["p2" + b], T["p3" + b]
-            D, AD, Zx, pn = T["D" + b], T["AD" + b], T["Zx" + b], T["pn" + b]
-            q4 = [b + str(j) for j in range(4)]
-            zk = ["Zx" + j for j in q4]
-            q = {n: T[n + b] for n in ("cm", "Rm", "OHc", "Km", "yh", "pass", "OH", "Y", "c32", "ki", "ku")}
-            c0 = 0 if b == "A" else 8
-            V(128, 1, ("c32" + b,), ("cm" + b,), lambda e, q=q, p3=p3: e.tensor_tensor(q["cm"][:], q["c32"][:], p3[:, 256:384], A.mult), (bk[3],), tag="cm")
-            if not last:
-                C(128, zk, (), lambda e, d=p3, Zx=Zx: e.activation(d[:, 384:512], Zx[:, 0:2048:16], F.Copy), (bk[3],), tag="Zc")
-            wn = "win%d%s" % (t, b)
-            op("V", gcost(128), [wn + "." + j for j in "z01248"] + ["rp", "pass" + b], ("Rm" + b,),
-               lambda e, q=q, w=T[wn], c0=c0: e.tensor_tensor(q["Rm"][:], w[:, 0:2048].indirect(T.rp[:, c0:c0 + 8]), q["pass"][:], A.mult), tag="Rm")
-            if not last:
-                def rev(e, p3=p3, q=q):
-                    e.matmul(p3[:, 0:128], T.J32[:], q["cm"][:], True, False)
-                    return e.matmul(p3[:, 0:128], T.J32[:], q["Rm"][:], False, True)
-                P(1024, ("J0", "cm" + b, "Rm" + b), rev, (bk[3],), tag="rev")
-                ts = slice(t * 128, t * 128 + 128)
-                sr = T["sr" + b][:, ts]; su = T["su" + b][:, ts]
-                C(128, (), ("sr%d%s" % (t, b),), lambda e, d=sr, p3=p3: e.activation(d, p3[:, 0:128], F.Copy), (bk[3],), tag="revc")
-                pend["r" + b] = op("G", 1.0, ("sr%d%s" % (t, b),), (), ("send", sr, "win%d%s" % (t + 1, b), "ar%d%s" % (t + 1, b), peer[b][0]), sem="snd", tag="sendr")
-
-            def nat1(e, p2=p2, q=q):
-                e.matmul(p2[:, 0:128], T.I32[:], q["cm"][:], True, False)
-                return e.matmul(p2[:, 0:128], T.I32[:], q["Rm"][:], False, False)
-            P(1024, ("I32", "cm" + b, "Rm" + b), nat1, (bk[2],), tag="nat1")
-
-            def kc(e, p0=p0):
-                e.matmul(p0[:, 256:384], T.row16[0:1, :], ON[0:1, 0:128], True, False)
-                return e.matmul(p0[:, 256:384], ON[0:1, 0:128], T.rowi[0:1, :], False, False)
-            P(256, ("row16", "ones", "rowi"), kc, (bk[0],), tag="kc")
-
-            def kd(e, p0=p0, AD=AD):
-                for i in range(16):
-                    r = e.matmul(p0[:, 256 + i:384:16], AD[:, i:2048:16], T.K8[:], False, i == 15)
-                return r
-            P(1024, ["AD" + j for j in q4] + ["K8"], kd, (bk[0],), tag="key")
-            V(128, 1, ("Rk",), ("pm" + b,), lambda e, d=pn, p0=p0: e.tensor_tensor_scan(d[:, 0:128], T.Rk[:], p0[:, 256:384], 0.0, A.max, A.min), (bk[0],), tag="scan")
-            V(128, 1, ("Rk", "pm" + b), ("mn" + b,), lambda e, d=pn: e.tensor_tensor_scan(d[:, 255:127:-1], T.Rk[:], d[:, 127::-1], 0.0, A.max, A.min), tag="scr")
-            if not last:
-                V(128, 2, ("mn" + b, "mask"), ("Km" + b,), lambda e, q=q, d=pn: e.tensor_tensor(q["Km"][:], d[:, 128:256], T.mask[:], A.mult), tag="Km")
-            V(128, 1, ("mn" + b,), ("OH" + b,), lambda e, q=q, d=pn, p0=p0: e.tensor_tensor(q["OH"][:], p0[:, 256:384], d[:, 128:256], A.is_equal), (bk[0],), tag="OH")
-            if not last:
-                P(256, ("Km" + b, "Bd32"), lambda e, q=q, p0=p0: e.matmul(p0[:, 384:392], q["Km"][:], T.Bd32[:, 0:128:16], True, True), (bk[0],), tag="Kp")
-            P(128, ("OH" + b, "Id"), lambda e, q=q, p1=p1: e.matmul(p1[:, 0:128], q["OH"][:], T.Id[:], True, True), (bk[1],), tag="OHT")
-            V(128, 1, ("c32" + b,), ("OHc" + b,), lambda e, q=q, p1=p1: e.tensor_tensor(q["OHc"][:], q["c32"][:], p1[:, 0:128], A.mult), (bk[1],), tag="OHc")
-            P(512, ("E32", "OHc" + b), lambda e, q=q, p2=p2: e.matmul(p2[:, 0:128], T.E32[:, 15:143], q["OHc"][:], False, True), (bk[2],), tag="nat2")
-            if last:
-                s = slice(0, 128) if b == "A" else slice(128, 256)
-                ys = T["ys" + b]
-                V(128, 1, (), ("yls" + b,), lambda e, d=ys, p2=p2: e.tensor_copy(d[:, 0:128], p2[:, 0:128]), (bk[2],), tag="yl")
-                C(128, zk, ("yzs" + b,), lambda e, d=ys, Zx=Zx: e.activation(d[:, 128:256], Zx[:, 0:2048:16], F.Copy), tag="yz")
-                DMA("S", 2.0, ("yzs" + b,), (), T.yz[:, s], ys[:, 128:256], "out", tag="out")
-                DMA("S", 2.0, ("yls" + b,), (), T.yl[:, s], ys[:, 0:128], "out", tag="out")
+    def front(t, b):
+        last = t == RO - 1
+        ts = slice(t * 128, t * 128 + 128)
+        b0, b1, b2 = "0" + b, "1" + b, "2" + b
+        p0, p1, p2 = T["p0" + b], T["p1" + b], T["p2" + b]
+        lu = T["lu" + b]; luk = "lu%d%s" % (t, b)
+        q = {n: T[n + b] for n in ("G", "M", "H", "us", "Lp", "t32", "c32", "Wm", "Ws", "pass", "zo", "cu", "ej", "q", "Z", "Zt", "Zh", "cm")}
+        G, M, H = q["G"], q["M"], q["H"]
+        if t:
+            op("R", FLY, (), (luk,), None, sem="au%d%s" % (t, b), cnt=len(lanes(peer[b][1], core)), sched=(pend["u" + b],))
+        V(128, 1, (luk, "c6"), ("Lp" + b,), lambda e: e.tensor_scalar(q["Lp"][:], lu[:, ts], 16.0, col[:, 6:7], A.mult, A.add), tag="Lp")
+        for j in range(4):
+            f = slice(j * 512, j * 512 + 512); o = slice(t * 128 + j * 32, t * 128 + j * 32 + 32)
+            gather(G1Q[b][j], 512, ("X", luk), ("G%s%d" % (b, j),), G[:, f], T.X[:, 0:8192].indirect(lu[:, o]), tag="G1")
+            V(512, .5, ("G%s%d" % (b, j), "R"), ("M%s%d" % (b, j),),
+              lambda e, f=f: e.tensor_tensor_scan(M[:, f], T.R[:, 0:512], G[:, f], 0.0, A.max, A.min), tag="SC")
+            if CPQ[b][j] == "V":
+                V(512, .5, ("M%s%d" % (b, j), "thr"), ("H%s%d" % (b, j),),
+                  lambda e, f=f: e.tensor_scalar(H[:, f], M[:, f], col[:, 7:8], None, A.is_ge), tag="CP")
             else:
-                V(128, 1, (), ("su%d%s" % (t, b),), lambda e, d=su, p2=p2: e.tensor_copy(d, p2[:, 0:128]), (bk[2],), tag="su")
-                pend["u" + b] = op("G", 1.0, ("su%d%s" % (t, b),), (), ("send", su, "lu%d%s" % (t + 1, b), "au%d%s" % (t + 1, b), peer[b][0]), sem="snd", tag="sendu")
-                V(8, 1, (), ("ki" + b,), lambda e, q=q, p0=p0: e.tensor_copy(q["ki"][:, 0:8], p0[:, 384:392]), (bk[0],), tag="k1")
-                V(8, 1, ("ki" + b,), ("kj" + b,), lambda e, q=q: e.tensor_scalar(q["ki"][:, 8:16], q["ki"][:, 0:8], 4095, None, A.bitwise_and), tag="k2")
-                V(8, 1, ("kj" + b,), ("ku" + b,), lambda e, q=q: e.tensor_copy(q["ku"][:], q["ki"][:, 8:16]), tag="k3")
-                op("V", gcost(128), ["ku" + b] + ["D" + j for j in q4], ("yh" + b,),
-                   lambda e, q=q, D=D: e.tensor_scalar(q["yh"][:], D[:, 0:2048].indirect(q["ku"][:]), 0.5, -0.25, A.mult, A.add), tag="yh")
-                V(128, 1, ("yh" + b,), ("Y" + b,), lambda e, q=q, p3=p3: e.tensor_tensor(q["Y"][:], q["yh"][:], p3[:, 384:512], A.add), (bk[3],), tag="Y")
-                op("V", 0.06 + 128 * 3.5 * CY, ("Y" + b, "rp"), ("X",),
-                   lambda e, q=q, c0=c0: e.tensor_copy(T.X[:, 0:8192].indirect(T.rp[:, 16 + c0:24 + c0]), q["Y"][:]), tag="scat")
+                C(512, ("M%s%d" % (b, j), "nthr"), ("H%s%d" % (b, j),),
+                  lambda e, f=f: e.activation(H[:, f], M[:, f], F.Sigmoid, bias=col[:, 9:10], scale=256.0), tag="CP")
+            if j & 1:
+                h = j // 2; o = slice(h * 64, h * 64 + 64)
+
+                def sums(e, dst, row, ws, src, h=h, o=o):
+                    e.matmul(dst[:, o], row, ON[0:row.shape[0], 0:64], True, False)
+                    for i in range(16):
+                        r = e.matmul(dst[:, o], ws[i][:, 15 - i:143 - i], src[:, h * 1024 + i:h * 1024 + 1024:16], False, i == 15)
+                    return r
+                P(1088, ("G%s%d" % (b, j - 1), "G%s%d" % (b, j), "wE", "wD", "crS", "ones"),
+                  lambda e, f=sums: f(e, p1, cr[0:2, 0:128], [T.wD] * 15 + [T.wE], G), (b1,), tag="dS")
+                P(1088, ("H%s%d" % (b, j - 1), "H%s%d" % (b, j), "nE", "crX", "ones"),
+                  lambda e, f=sums: f(e, p0, cr[0:1, 128:256], [T.nE] * 16, H), (b0,), tag="cnt")
+        mk = ["M%s%d" % (b, j) for j in range(4)]
+        if OPQ["pass"] == "V":
+            V(128, 1, (), ("pass" + b,), lambda e: e.tensor_scalar(q["pass"][:], p0[:, 0:128], 0.0, None, A.is_lt), (b0,), tag="pass")
+        else:
+            C(128, (), ("pass" + b,), lambda e: e.activation(q["pass"][:], p0[:, 0:128], F.Sigmoid, scale=-1.0), (b0,), tag="pass")
+        V(128, 1, ("pass" + b,), ("us" + b,), lambda e: e.tensor_tensor(q["us"][:], q["pass"][:], p1[:, 0:128], A.mult), (b1,), tag="us")
+        P(128, ("pass" + b, "Bn"), lambda e: e.matmul(p0[:, 128:256], q["pass"][:], T.Bn[:], True, True), (b0,), tag="mT")
+        P(512, ("us" + b, "Bq32"), lambda e: e.matmul(p1[:, 384:512], T.Bq32[:], q["us"][:], True, True), (b1,), tag="x")
+        P(512, ("us" + b, "Bd32"), lambda e: e.matmul(p2[:, 128:256], T.Bd32[:], q["us"][:], True, False), (b2,), tag="u1")
+        V(128, 1, ("mask",), ("Wm" + b,), lambda e: e.tensor_tensor(q["Wm"][:], p0[:, 128:256], T.mask[:], A.mult), (b0,), tag="Wm")
+        V(128, 1, (), ("q" + b,), lambda e: e.tensor_scalar(q["q"][:], p1[:, 384:512], MAGIC, MAGIC, A.add, A.subtract), (b1,), tag="q")
+
+        def mP(e):
+            e.matmul(p0[:, 384:400], T.Id[:], T.CV[:], True, False)
+            return e.matmul(p0[:, 384:400], q["Wm"][:], T.sel[:], False, True)
+        P(128, ("Wm" + b, "Id", "CV", "sela", "selb"), mP, (b0,), tag="mP")
+        P(128, ("q" + b, "In"), lambda e: e.matmul(p2[:, 128:256], T.In[:], q["q"][:], False, True), (b2,), tag="u2")
+        V(16, 1, (), ("zo" + b,), lambda e: e.tensor_copy(q["zo"][:], p0[:, 384:400]), (b0,), tag="zo")
+        C(128, ("c8",), (), lambda e: e.activation(p2[:, 256:384], p2[:, 128:256], F.Square, bias=col[:, 8:9]), (b2,), tag="Sq")
+        gather(OPQ["Z"], 128, ["zo" + b] + mk, ("Z" + b,), q["Z"][:], M[:, 0:2048].indirect(q["zo"][:, 0:8]), tag="Z")
+        V(128, 1, ("Lp" + b,), ("t32" + b,), lambda e: e.tensor_tensor(q["t32"][:], p2[:, 256:384], q["Lp"][:], A.add), (b2,), tag="t32")
+        V(128, 1, ("t32" + b,), ("c32" + b,), lambda e: e.tensor_scalar(q["c32"][:], q["t32"][:], 4, 8191, A.arith_shift_right, A.bitwise_and), tag="c32")
+        V(128, 1, ("c32" + b,), ("cu" + b,), lambda e: e.tensor_copy(q["cu"][:], q["c32"][:]), tag="cu")
+        P(128, ("Z" + b, "Ih"), lambda e: e.matmul(p1[:, 256:384], q["Z"][:], T.Ih[:], True, True), (b1,), tag="Ztr")
+        C(128, (), ("Zt" + b,), lambda e: e.activation(q["Zt"][:], p1[:, 256:384], F.Copy), (b1,), tag="Zt")
+        V(128, 1, ("c32" + b,), ("cm" + b,), lambda e: e.tensor_tensor(q["cm"][:], q["c32"][:], p0[:, 0:128], A.min), (b0,), tag="cm")
+        nw = T["nw" + b][:, ts]
+        op("V", gcost(128), ["win%s%d" % (b, j) for j in range(16)] + ["zo" + b, "cm" + b], ("nw%d%s" % (t, b),),
+           lambda e: e.tensor_tensor(nw, T["win" + b][:, 0:2048].indirect(q["zo"][:, 8:16]), q["cm"][:], A.max), tag="nw")
+        P(512, ("I32", "nw%d%s" % (t, b)), lambda e: e.matmul(p2[:, 0:128], T.I32[:], nw, True, False), (b2,), tag="nat1")
+        if last:
+            C(128, ("Z" + b,), ("yzs" + b,), lambda e: e.activation(T["ys" + b][:, 128:256], q["Z"][:], F.Copy), tag="yz")
+            DMA("S", 2.0, ("yzs" + b,), (), T.yz[:, half[b]], T["ys" + b][:, 128:256], "out", tag="out")
+            return
+        nxt = slice(t * 128 + 128, t * 128 + 256)
+        pend["f" + b] = op("G", 0.8, ("nw%d%s" % (t, b),), (), ("send", nw, T["lf" + b][:, nxt], "af%d%s" % (t + 1, b), peer[b][0]), sem="snd", tag="sendf")
+        C(128, ("Z" + b,), ("Zh" + b,), lambda e: e.activation(q["Zh"][:], q["Z"][:], F.Copy, bias=-0.25, scale=0.5), tag="Zh")
+        P(512, ("us" + b, "Bd32"), lambda e: e.matmul(p1[:, 128:256], q["us"][:], T.Bd32[:], True, True), (b1,), tag="sT")
+        V(128, 1, ("mask",), ("Ws" + b,), lambda e: e.tensor_tensor(q["Ws"][:], p1[:, 128:256], T.mask[:], A.mult), (b1,), tag="Ws")
+        P(256, ("Ws" + b, "Bd32"), lambda e: e.matmul(p1[:, 0:8], q["Ws"][:], T.Bd32[:, 0:128:16], True, True), (b1,), tag="sP")
+        c0 = 0 if b == "A" else 8
+        V(8, 1, (), ("Wi" + b,), lambda e: e.tensor_scalar(T.Wi[:, c0:c0 + 8], p1[:, 0:8], 2047.5, None, A.add), (b1,), tag="w1")
+        P(128, ("Qe", "pass" + b), lambda e: e.matmul(p0[:, 128:256], T.Qe[:], q["pass"][:], True, True), (b0,), tag="E")
+        ec = T.ec[:, 0:1] if b == "A" else T.ec[:, 1:2]
+        C(128, (), ("ec" + b, "ej" + b), lambda e: e.activation(q["ej"][:], p0[:, 128:256], F.Copy, accum_out=ec), (b0,), tag="Eacc")
+
+    def joint(t):
+        V(16, 1, ("WiA", "WiB"), ("nu",), lambda e: e.tensor_scalar(T.nu[:], T.Wi[:], 31, None, A.bitwise_and), tag="w2")
+        V(16, 2, ("nu", "cv"), ("nv",), lambda e: e.tensor_tensor(T.nv[:], T.nu[:], T.cv[:, 16:32], A.add), tag="w3")
+        V(16, 1, ("nv",), ("rp",), lambda e: e.tensor_copy(T.rp[:], T.nv[:]), tag="w4")
+        V(1, 1, ("ecA", "ecB"), ("ei",), lambda e: e.tensor_tensor(T.ei[:, 0:1], T.ec[:, 0:1], T.ec[:, 1:2], A.add), tag="e1")
+        V(1, 1, ("ei",), ("ej2",), lambda e: e.tensor_scalar(T.ei[:, 1:2], T.ei[:, 0:1], 7, None, A.bitwise_and), tag="e2")
+        V(1, 2, ("ej2", "limf"), ("thr",), lambda e: e.tensor_tensor(col[:, 7:8], T.ei[:, 1:2], T.limf[:, t + 1:t + 2], A.add), tag="e3")
+        nthr()
+
+    zn = [0]
+
+    def middle(t, b):
+        Gh, Pm, cu, Zt = T["Gc" + b], T["P" + b], T["cu" + b], T["Zt" + b]
+        for j in range(4):
+            f = slice(j * 512, j * 512 + 512); o = slice(j * 32, j * 32 + 32)
+            z = "z%d" % (zn[0] & 1); zn[0] += 1
+            gather(G2Q[b][j], 512, ("X", "cu" + b), ("Gc%s%d" % (b, j),), Gh[:, f], T.X[:, 0:8192].indirect(cu[:, o]), 0.5, tag="G2")
+            onv = MXQ[b][j] == "V"
+            P(512, ("Zt" + b, "Exp"), lambda e, z=z, f=f, onv=onv: e.matmul(T[z][:], Zt[:], T.Exp[:, f], True, onv), (z,), tag="Zx")
+            if onv:
+                V(512, 1, ("Gc%s%d" % (b, j),), ("P%s%d" % (b, j),), lambda e, z=z, f=f: e.tensor_tensor(Pm[:, f], Gh[:, f], T[z][:], A.max), (z,), tag="max")
+            else:
+                P(512, ("Gc%s%d" % (b, j), "Im"), lambda e, z=z, f=f: e.matmul(T[z][:], T.Im[:], Gh[:, f], False, True), (z,), tag="Zd")
+                C(512, (), ("P%s%d" % (b, j),), lambda e, z=z, f=f: e.activation(Pm[:, f], T[z][:], F.Relu, scale=-1.0), (z,), tag="max")
+
+    def back(t, b):
+        last = t == RO - 1
+        b0, b1, b2 = "0" + b, "1" + b, "2" + b
+        p0, p1, p2 = T["p0" + b], T["p1" + b], T["p2" + b]
+        q = {n: T[n + b] for n in ("Gc", "P", "OHc", "Km", "pm", "mn", "OH", "Y", "c32", "ki", "ku", "Zh")}
+        gk = ["Gc%s%d" % (b, j) for j in range(4)]
+        c0 = 0 if b == "A" else 8
+
+        def kc(e):
+            e.matmul(p0[:, 256:384], T.row16[0:1, :], ON[0:1, 0:128], True, False)
+            return e.matmul(p0[:, 256:384], ON[0:1, 0:128], T.rowi[0:1, :], False, False)
+
+        def kd(e, src, w, stop):
+            for i in range(16):
+                r = e.matmul(p0[:, 256 + i:384:16], src[:, i:2048:16], w, False, stop and i == 15)
+            return r
+        P(256, ("row16", "ones", "rowi"), kc, (b0,), tag="kc")
+        P(1024, gk + ["K8b"], lambda e: kd(e, q["Gc"], T.K8[:, 8:16], False), (b0,), tag="keyG")
+        P(1024, ["P%s%d" % (b, j) for j in range(4)] + ["K8a"], lambda e: kd(e, q["P"], T.K8[:, 0:8], True), (b0,), tag="keyP")
+        V(128, 1, ("Rk",), ("pm" + b,), lambda e: e.tensor_tensor_scan(q["pm"][:], T.Rk[:], p0[:, 256:384], 0.0, A.max, A.min), (b0,), tag="scan")
+        least = q["pm"][:, 0:128].indirect(T.cidx[:])
+        if not last:
+            op("V", gcost(128), ("pm" + b, "cidx", "mask"), ("Km" + b,), lambda e: e.tensor_tensor(q["Km"][:], least, T.mask[:], A.mult), tag="Km")
+        gather(OPQ["mn"], 128, ("pm" + b, "cidx"), ("mn" + b,), q["mn"][:], least, tag="mn")
+        V(128, 1, ("mn" + b,), ("OH" + b,), lambda e: e.tensor_tensor(q["OH"][:], p0[:, 256:384], q["mn"][:], A.is_equal), (b0,), tag="OH")
+        if not last:
+            P(256, ("Km" + b, "Bd32"), lambda e: e.matmul(p1[:, 384:392], q["Km"][:], T.Bd32[:, 0:128:16], True, True), (b1,), tag="Kp")
+            V(8, 1, (), ("ki" + b,), lambda e: e.tensor_copy(q["ki"][:, 0:8], p1[:, 384:392]), (b1,), tag="k1")
+        P(128, ("OH" + b, "Id"), lambda e: e.matmul(p1[:, 0:128], q["OH"][:], T.Id[:], True, True), (b1,), tag="OHT")
+        V(128, 1, ("c32" + b,), ("OHc" + b,), lambda e: e.tensor_tensor(q["OHc"][:], q["c32"][:], p1[:, 0:128], A.mult), (b1,), tag="OHc")
+        P(512, ("E32", "OHc" + b), lambda e: e.matmul(p2[:, 0:128], T.E32[:, 15:143], q["OHc"][:], False, True), (b2,), tag="nat2")
+        if last:
+            ys = T["ys" + b]
+            V(128, 1, (), ("yls" + b,), lambda e: e.tensor_copy(ys[:, 0:128], p2[:, 0:128]), (b2,), tag="yl")
+            DMA("S", 2.0, ("yls" + b,), (), T.yl[:, half[b]], ys[:, 0:128], "out", tag="out")
+            return
+        su = T["su" + b][:, t * 128:t * 128 + 128]
+        V(128, 1, (), ("su%d%s" % (t, b),), lambda e: e.tensor_copy(su, p2[:, 0:128]), (b2,), tag="su")
+        pend["u" + b] = op("G", 0.8, ("su%d%s" % (t, b),), (),
+                           ("send", su, T["lu" + b][:, t * 128 + 128:t * 128 + 256], "au%d%s" % (t + 1, b), peer[b][0]), sem="snd", tag="sendu")
+        V(8, 1, ("ki" + b,), ("kj" + b,), lambda e: e.tensor_scalar(q["ki"][:, 8:16], q["ki"][:, 0:8], 2047, None, A.bitwise_and), tag="k2")
+        V(8, 1, ("kj" + b,), ("ku" + b,), lambda e: e.tensor_copy(q["ku"][:], q["ki"][:, 8:16]), tag="k3")
+        op("V", gcost(128), ["ku" + b, "Zh" + b] + gk, ("Y" + b,),
+           lambda e: e.tensor_tensor(q["Y"][:], q["Gc"][:, 0:2048].indirect(q["ku"][:]), q["Zh"][:], A.add), tag="Y")
+
+    def scatter(b):
+        c0 = 0 if b == "A" else 8
+        op("V", 0.06 + 128 * 3.5 * CY, ("Y" + b, "rp"), ("X",),
+           lambda e: e.tensor_copy(T.X[:, 0:8192].indirect(T.rp[:, c0:c0 + 8]), T["Y" + b][:]), tag="scat")
+
+    for t in range(RO):
+        for step in (window, front, None, middle, back):
+            for b in "AB":
+                cur[0] = b
+                if step: step(t, b)
+            cur[0] = ""
+            if step is None and t < RO - 1: joint(t)
+        if t < RO - 1:
+            for b in "AB":
+                cur[0] = b
+                scatter(b)
     return ops, lanes, peer
 
 
 def schedule(ops):
     n = len(ops)
+    pred = [sorted(o["wait"] | o["order"]) for o in ops]
     succ = [[] for _ in range(n)]
-    for o in ops:
-        for d in o["wait"] | o["order"]: succ[d].append(o["i"])
-    pr = [0.0] * n
-    for i in range(n - 1, -1, -1):
-        pr[i] = ops[i]["c"] + max([pr[s] + (WAKE if ops[s]["q"] != ops[i]["q"] else .02) for s in succ[i]], default=0.0)
-    need = [len(o["wait"] | o["order"]) for o in ops]
-    ready, fin, avail, order = {}, [0.0] * n, {}, []
-    rt = [0.0] * n
     for i in range(n):
-        if not need[i]: ready[i] = 0.0
-    while ready:
-        st = {}
-        for i, r in ready.items():
-            q = ops[i]["q"]; q = "A" if q == "AD" else q
-            st[i] = max(r, avail.get(q, 0.0)) if q != "R" else r
-        best = {}
-        for i in st:
-            q = ops[i]["q"]
-            if q not in best or st[i] < best[q]: best[q] = st[i]
-        q0 = min(best, key=lambda q: best[q])
-        cand = [i for i in st if ops[i]["q"] == q0 and st[i] <= best[q0] + LOOK[q0]]
-        i = max(cand, key=lambda k: (pr[k] + PRI.get(ops[k]["tag"], 0.0), -k))
-        o = ops[i]; q = "A" if o["q"] == "AD" else o["q"]
-        s = st[i]
-        fin[i] = s + o["c"]
-        if q != "R": avail[q] = s + (0.1 if o["q"] in ("AD", "S") else o["c"])
-        o["s"] = s
-        order.append(i)
-        del ready[i]
-        for k in succ[i]:
-            need[k] -= 1
-            wk = WAKE if ops[k]["q"] != o["q"] else .05
-            rt[k] = max(rt[k], fin[i] + wk)
-            if not need[k]: ready[k] = rt[k]
-    return order, max(fin)
+        for d in pred[i]: succ[d].append(i)
+    que = [{"AD": "A"}.get(o["q"], o["q"]) for o in ops]
+    cost = [o["c"] for o in ops]
+    hold = [0.0 if o["q"] == "R" else ISSUE if o["q"] in ("AD", "S") else o["c"] for o in ops]
+
+    def lag(a, b):
+        return WAKE if ops[a]["q"] != ops[b]["q"] else SELF if (a in ops[b]["wait"] or b in ops[a]["wait"]) else 0.0
+
+    def place(key, before, after, back):
+        need = [len(x) for x in before]
+        ready = [i for i in range(n) if not need[i]]
+        start, busy = [0.0] * n, {}
+        while ready:
+            i = min(ready, key=key)
+            ready.remove(i)
+            s = max([start[d] + cost[d] + lag(d, i) for d in before[i]], default=0.0)
+            shift = cost[i] - hold[i] if back else 0.0
+            line = busy.setdefault(que[i], [])
+            s += shift; k = len(line)
+            while k and line[k - 1][1] > s: k -= 1
+            while k < len(line) and line[k][0] < s + hold[i]:
+                s = max(s, line[k][1]); k += 1
+            if hold[i]: line.insert(k, (s, s + hold[i]))
+            start[i] = s - shift
+            for k in after[i]:
+                need[k] -= 1
+                if not need[k]: ready.append(k)
+        return start, max(start[i] + cost[i] for i in range(n))
+
+    tail = [0.0] * n
+    for i in range(n - 1, -1, -1):
+        tail[i] = cost[i] + max([tail[s] + lag(i, s) for s in succ[i]], default=0.0)
+    best = place(lambda i: (-tail[i], i), pred, succ, False)
+    last = best
+    for _ in range(PASSES):
+        fw = last[0]
+        bw = place(lambda i: (-fw[i] - cost[i], -i), succ, pred, True)[0]
+        last = place(lambda i: (-bw[i] - cost[i], i), pred, succ, False)
+        if last[1] < best[1]: best = last
+    for o in ops: o["s"] = best[0][o["i"]]
+    return sorted(range(n), key=lambda i: (-1.0 if "first" in ops[i] else best[0][i], i)), best[1]
 
 
 def rank_program(g, core, T, topo):
     if T.rank_of(core) is None:
         return
     ops, lanes, peer = make_ops(core, T, topo)
-    order, est = schedule(ops)
+    if not PLAN:
+        PLAN.extend([schedule(ops), [o["s"] for o in ops]])
+    order = PLAN[0][0]
+    for o in ops: o["s"] = PLAN[1][o["i"]]
     eng = {"V": g.vector, "A": g.scalar, "T": g.tensor, "G": g, "S": g.sync, "AD": g.scalar}
     qsem = {"V": "qV", "A": "qA", "T": "qT", "G": "qG"}
+    total, seen = {}, {}
+    for o in ops:
+        if o["q"] in ("S", "AD"): total[o["sem"]] = total.get(o["sem"], 0) + 16
     cnt, known, snap, done = {}, {}, {}, {}
     sent = 0
     for i in order:
@@ -421,7 +465,7 @@ def rank_program(g, core, T, topo):
             _, src, dst, sem, to = o["fn"]
             ln = lanes(core, to)
             rid, pid, _ = topo.addr(to)
-            g.remote_dma(out_ap=T[dst][:, 0:128], in_ap=src, remote_sem=T.sem[sem], local_sem=T.sem.snd, pid=pid, routing_id=rid,
+            g.remote_dma(out_ap=dst, in_ap=src, remote_sem=T.sem[sem], local_sem=T.sem.snd, pid=pid, routing_id=rid,
                          dma_engine_mask=sum(1 << x for x in ln))
             sent += len(ln)
             done[i] = ("snd", sent); snap[i] = dict(kn)
@@ -429,7 +473,7 @@ def rank_program(g, core, T, topo):
             r = o["fn"](e)
             if o["q"] in ("S", "AD"):
                 r.then_inc(T.sem[o["sem"]], 16)
-                done[i] = (o["sem"], o["n"]); cnt[o["sem"]] = o["n"]
+                done[i] = (o["sem"], total[o["sem"]]); cnt[o["sem"]] = total[o["sem"]]
             else:
                 s = qsem[o["q"]]
                 cnt[s] = cnt.get(s, 0) + 1

@@ -1,3 +1,4 @@
+import numpy as np
 from concourse.mybir import AluOpType, AxisListType, ActivationFunctionType
 
 A = AluOpType
@@ -13,58 +14,66 @@ for _b in "AB":
     for _n in ("G", "M", "H", "Gc", "P"):
         SCRATCH[_n + _b] = ("sbuf", [128, 2048], BF)
     for _n, _d in (("us", F32), ("Lp", F32), ("t32", I32), ("c32", I32), ("Wm", BF), ("Ws", F32), ("cm", F32), ("OHc", F32),
-                   ("Km", F32), ("pm", F32), ("mn", F32), ("Y", I32), ("pass", BF), ("q", BF), ("OH", BF), ("Z", BF), ("Zt", BF),
-                   ("Zh", F32), ("cu", U16), ("ej", BF)):
+                   ("Km", F32), ("pm", F32), ("mn", F32), ("pass", BF), ("q", BF), ("OH", BF), ("Z", BF), ("Zt", BF),
+                   ("Zh", F32), ("cu", U16), ("Gm", BF)):
         SCRATCH[_n + _b] = ("sbuf", [128, 128], _d)
+    SCRATCH["nw" + _b] = ("sbuf", [128, 512], F32)
     SCRATCH["ys" + _b] = ("sbuf", [128, 256], F32)
-    SCRATCH["ki" + _b] = ("sbuf", [128, 16], I32)
-    SCRATCH["ku" + _b] = ("sbuf", [128, 8], U16)
     SCRATCH["zo" + _b] = ("sbuf", [128, 16], U16)
     SCRATCH["su" + _b] = ("sbuf", [128, 384], U16)
-    SCRATCH["nw" + _b] = ("sbuf", [128, 512], F32)
-    SCRATCH["lu" + _b] = ("sbuf", [128, 512], U16)
-    SCRATCH["lf" + _b] = ("sbuf", [128, 512], F32)
-    SCRATCH["win" + _b] = ("sbuf", [128, 2048], F32)
     SCRATCH["rows" + _b] = ("dram", [8, 16, 128], F32)
-for _n, _s, _d in (("X", 8192, BF), ("R", 512, BF), ("Rk", 128, F32), ("ones", 256, BF), ("Exp", 2048, BF),
+for _n, _s, _d in (("X", 8192, BF), ("R", 2048, BF), ("Rk", 128, F32), ("ones", 256, BF), ("Exp", 2048, BF),
+                   ("win", 4096, F32), ("lu", 1024, U16), ("lf", 256, F32), ("Y", 256, I32), ("ki", 32, I32), ("ku", 16, U16),
                    ("E", 144, BF), ("E2", 144, BF), ("wE", 144, BF), ("wD", 144, BF), ("nE", 144, BF), ("E32", 144, F32),
-                   ("Bd", 128, BF), ("Id", 128, BF), ("Ih", 128, BF), ("In", 128, BF), ("Im", 128, BF), ("Bn", 128, BF), ("Qe", 128, BF),
-                   ("R16", 128, BF), ("mask", 128, BF), ("K8", 16, BF), ("sel", 16, BF), ("CV", 16, BF), ("cr", 256, BF),
-                   ("row16", 128, BF), ("rowi", 128, BF), ("Bd32", 128, F32), ("Bq32", 128, F32), ("I32", 128, F32),
-                   ("z8", 16, F32), ("cols", 16, F32), ("wi", 1, I32), ("kni", 1, I32), ("limi", 4, I32), ("limf", 4, F32),
-                   ("tub", 256, I32), ("pi", 48, I32), ("cvb", 48, I32), ("cv", 32, I32), ("cidx", 8, U16), ("Wi", 16, I32),
-                   ("nu", 16, I32), ("nv", 16, I32), ("rp", 16, U16), ("ei", 2, I32), ("ec", 2, F32)):
+                   ("Bd", 128, BF), ("Id", 128, BF), ("Ih", 128, BF), ("Im", 128, BF), ("Bn", 128, BF), ("Qe", 128, BF),
+                   ("R16", 128, BF), ("mask", 128, BF), ("K8", 16, BF), ("sel", 16, BF), ("CV", 64, BF), ("cr", 384, BF),
+                   ("kl", 128, BF), ("kr", 128, BF), ("Bd32", 128, F32), ("Bq32", 128, F32), ("I32", 128, F32),
+                   ("wQ", 144, BF), ("Dm", 128, BF), ("wq", 128, BF), ("wB", 128, BF),
+                   ("z8", 16, F32), ("cols", 16, F32), ("wi", 1, I32), ("kni", 1, I32), ("limi", 4, I32), ("limf", 8, F32),
+                   ("tub", 256, I32), ("pi", 48, I32), ("cvb", 56, I32), ("cv", 48, I32), ("cidx", 8, U16),
+                   ("sel32", 16, F32), ("I32n", 128, F32), ("rq", 16, F32), ("rp", 16, U16), ("ec", 4, F32), ("ej", 128, BF)):
     SCRATCH[_n] = ("sbuf", [128, _s], _d)
 
 SEMAPHORES = ["qV", "qA", "qT", "qG", "lX", "ltub", "lwt", "lkn", "llim", "snd", "out"]
-for _b in "AB":
-    SEMAPHORES += [_n + "%d%s" % (_t, _b) for _n in "wr" for _t in range(RO)]
-    SEMAPHORES += ["au%d%s" % (_t, _b) for _t in range(1, RO)] + ["af%d%s" % (_t, _b) for _t in range(1, RO)]
+SEMAPHORES += [_n + str(_t) + _b for _n in "wr" for _t in range(RO) for _b in "AB"]
+SEMAPHORES += ["au%d%s" % (_t, _b) for _t in range(1, RO) for _b in "AB"]
 
-CY = 0.83e-3 * 1.15
-PEC = 0.42e-3 * 1.15
+CY = 0.86e-3
+PEC = 0.56e-3
+VFIX, AFIX = 0.03, 0.06
 GA = 1.5
-WAKE = 0.1
-FLY = 3.0
-SELF = 0.05
-ISSUE = 0.1
-PASSES = 6
-G1Q = {"A": "AVAV", "B": "AAAA"}
-G2Q = {"A": "AAAA", "B": "AAAA"}
-CPQ = {"A": "VVVV", "B": "AAAA"}
-MXQ = {"A": "VVVV", "B": "VVVV"}
-OPQ = {"pass": "V", "Z": "A", "mn": "A", "late": "V"}
+WAKE = 0.2
+FLY = 2.5
+SELF = 0.12
+WIN = 5.5
+ISSUE = 0.2
+PASSES, SHAKE, SHARE, SLACK = 1500, 0.7, 0.04, 0.4
+G1Q = {"A": "AVAA", "B": "AAAV"}
+G2Q = {"A": "AAAV", "B": "AVAA"}
+SCQ = {"A": "V-VV", "B": "VVVV"}
+CPQ = {"A": "V-AV", "B": "AVVA"}
+MXQ = {"A": "VAAA", "B": "VVVA"}
+OPQ = {"A": "VAAAV", "B": "VAAAV"}
+SUMS = {"A": "V", "B": "A"}
+TAIL = {"A": "A", "B": "A"}
+CHUNK = 4
 PLAN = []
+DMAS = {"S": "S", "AD": "A", "GD": "G"}
 
 
-def vcost(n, f=1.0): return 0.05 + max(64, n * f) * CY
+def pieces(s):
+    cut = [j for j in range(4) if j == 0 or s[j] != "-"] + [4]
+    return [(s[a].replace("-", "V"), a, z) for a, z in zip(cut, cut[1:])]
+
+
+def names(s, j0, j1): return [s + str(j) for j in range(j0, j1)]
+def vcost(n, f=1.0): return VFIX + max(64, n * f) * CY
 def gcost(n): return 0.06 + n * GA * CY
 
 
 def make_ops(core, T, topo):
     ops = []
     lastw, readers, bank = {}, {}, {}
-    dcount = {}
     cur = [""]
 
     def op(q, cost, reads, writes, fn, banks=(), sem=None, cnt=0, sched=(), tag=""):
@@ -74,7 +83,7 @@ def make_ops(core, T, topo):
         for k in writes:
             if k in lastw: o["wait"].add(lastw[k])
             for r in readers.get(k, ()):
-                if ops[r]["q"] == q and q != "S": o["order"].add(r)
+                if ops[r]["q"] == q and q not in DMAS: o["order"].add(r)
                 else: o["wait"].add(r)
         for k in banks:
             if k in bank:
@@ -85,9 +94,6 @@ def make_ops(core, T, topo):
         for k in writes:
             lastw[k] = o["i"]; readers[k] = []
         o["wait"].discard(o["i"]); o["order"].discard(o["i"])
-        if q in ("S", "AD"):
-            dcount[sem] = dcount.get(sem, 0) + 16
-            o["n"] = dcount[sem]
         ops.append(o)
         return o["i"]
 
@@ -95,10 +101,10 @@ def make_ops(core, T, topo):
         return op("V", vcost(n, f), reads, writes, fn, banks, tag=tag)
 
     def C(n, reads, writes, fn, banks=(), tag=""):
-        return op("A", 0.07 + max(64, n) * CY, reads, writes, fn, banks, tag=tag)
+        return op("A", AFIX + max(64, n) * CY, reads, writes, fn, banks, tag=tag)
 
     def P(cyc, reads, fn, banks, tag=""):
-        return op("T", 0.03 + cyc * PEC, reads, (), fn, banks, tag=tag)
+        return op("T", 0.01 + cyc * PEC, reads, (), fn, banks, tag=tag)
 
     def Gc(n, reads, writes, fn, tag=""):
         return op("G", 0.17 + 2 * n * CY, reads, writes, fn, tag=tag)
@@ -122,6 +128,11 @@ def make_ops(core, T, topo):
         return topo.engines(s, d)[:8]
 
     half = {"A": slice(0, 128), "B": slice(128, 256)}
+    wins = {b: names("win" + b, 0, 16) for b in "AB"}
+
+    def lists(t, b, j0=0, j1=4):
+        c = t * 256 + half[b].start
+        return T.lu[:, c + 32 * j0:c + 32 * j1]
 
     small = [DMA("S", 2.0, (), ("tub",), T.tub[:], T.tube[:], "ltub"), DMA("AD", 2.0, (), ("wi",), T.wi[:], T.wt[:], "lwt"),
              DMA("AD", 2.0, (), ("kni",), T.kni[:], T.kn[:], "lkn"), DMA("S", 2.0, (), ("limi",), T.limi[:], T.lim[:], "llim")]
@@ -138,20 +149,19 @@ def make_ops(core, T, topo):
     Gc(144, ("E0",), ("E1",), lambda e: e.affine_select(T.E[:], T.E[:], [[-16, 9], [0, 16]], A.is_ge, 0.0, 0, 1))
     Gc(144, ("E1",), ("E",), lambda e: e.affine_select(T.E[:], T.E[:], [[16, 9], [0, 16]], A.is_ge, 0.0, 15, -1))
     Gc(128, ("ones",), ("R16",), lambda e: e.affine_select(T.R16[:], ON[:, 0:128], [[0, 8], [1, 16]], A.is_equal, 0.0, 0, -1))
-    Gc(128, (), ("row16",), lambda e: e.iota(T.row16[:], [[16, 128]], 0, 0, allow_small_or_imprecise_dtypes=True))
-    Gc(128, (), ("rowi",), lambda e: e.iota(T.rowi[:], [[0, 8], [1, 16]], 0, 0, allow_small_or_imprecise_dtypes=True))
-    Gc(32, (), ("pi",), lambda e: e.iota(T.pi[:, 0:32], [[0, 32]], 0, 1))
-    Gc(8, (), ("cvb0",), lambda e: e.iota(T.cvb[:, 0:8], [[256, 8]], 0, 0))
-    Gc(8, (), ("cvb1",), lambda e: e.iota(T.cvb[:, 8:16], [[16, 8]], 0, 0))
-    Gc(16, (), ("cvb2",), lambda e: e.iota(T.cvb[:, 16:32], [[512, 16]], 0, 0))
-    Gc(8, (), ("cvb3",), lambda e: e.iota(T.cvb[:, 32:40], [[16, 8]], 15, 0))
+    V(128, .5, (), ("kl0",), lambda e: e.memset(T.kl[0:2, :], 1.0))
+    Gc(128, ("kl0",), ("kl",), lambda e: e.iota(T.kl[0:1, :], [[16, 128]], 0, 0, allow_small_or_imprecise_dtypes=True))
+    Gc(128, (), ("kr0",), lambda e: e.iota(T.kr[0:2, :], [[0, 8], [1, 16]], 0, 0, allow_small_or_imprecise_dtypes=True))
+    V(128, .5, ("kr0",), ("kr",), lambda e: e.memset(T.kr[0:1, :], 1.0))
+    Gc(48, (), ("pi",), lambda e: e.iota(T.pi[:], [[0, 48]], 0, 1))
+    for c, n, step, base in ((0, 8, 256, 0), (8, 8, 16, 0), (16, 8, 256, 0), (24, 8, 16, 128), (32, 16, 512, 0), (48, 8, 16, 15)):
+        Gc(n, (), ("cvb%d" % c,), lambda e, c=c, n=n, step=step, base=base: e.iota(T.cvb[:, c:c + n], [[step, n]], base, 0))
     V(2048, .5, (), ("Exp0",), lambda e: e.memset(T.Exp[:], 1.0))
     Gc(2048, ("Exp0",), ("Exp",), lambda e: e.affine_select(T.Exp[:], T.Exp[:], [[-1, 128], [0, 16]], A.is_equal, 0.0, 0, 1))
-    V(2048, .5, (), ["HA%d" % j for j in range(4)], lambda e: e.memset(T.HA[:], 0.0))
-    for b in "AB":
-        V(128, 1, ("tub",), ("lf0" + b,), lambda e, b=b: e.tensor_copy(T["lf" + b][:, 0:128], T.tub[:, half[b]]))
-        V(128, 1, ("tub",), ("lu0" + b,), lambda e, b=b: e.tensor_copy(T["lu" + b][:, 0:128], T.tub[:, half[b]]))
-        C(2048, ["HA%d" % j for j in range(4)], ["win%s%d" % (b, j) for j in range(16)], lambda e, b=b: e.activation(T["win" + b][:], T.HA[:], F.Copy))
+    V(256, 1, ("tub",), ("lu0A", "lu0B"), lambda e: e.tensor_copy(T.lu[:, 0:256], T.tub[:]))
+    V(2048, .5, (), names("HA", 0, 4), lambda e: e.memset(T.HA[:], 0.0))
+    for c, b in ((0, "A"), (2048, "B")):
+        C(2048, names("HA", 0, 4), wins[b], lambda e, c=c: e.activation(T.win[:, c:c + 2048], T.HA[:], F.Copy))
     V(8, 1, ("z8",), ("c0",), lambda e: e.tensor_reduce(col[:, 0:1], T.z8[:, 0:8], AxisListType.X, A.add))
     V(8, 1, ("z15",), ("c2",), lambda e: e.tensor_reduce(col[:, 2:3], T.z8[:, 8:16], AxisListType.X, A.add, negate=True))
     V(1, 1, ("c0",), ("c1",), lambda e: e.tensor_scalar(col[:, 1:2], col[:, 0:1], -1.0, 1.0, A.mult, A.add))
@@ -159,30 +169,42 @@ def make_ops(core, T, topo):
     V(1, 1, ("kni",), ("c5",), lambda e: e.tensor_scalar(col[:, 5:6], T.kni[:], 8.0, None, A.mult))
     V(1, 1, ("c5",), ("c6",), lambda e: e.tensor_scalar(col[:, 6:7], col[:, 5:6], col[:, 5:6], -1.0, A.mult, A.mult))
     V(1, 1, ("c5",), ("c8",), lambda e: e.tensor_scalar(col[:, 8:9], col[:, 5:6], 2047.5, None, A.add))
-    V(4, 1, ("limi",), ("limf",), lambda e: e.tensor_copy(T.limf[:], T.limi[:]))
+    V(4, 1, ("limi",), ("limf",), lambda e: e.tensor_copy(T.limf[:, 0:4], T.limi[:]))
+    V(4, 1, ("limi",), ("limg",), lambda e: e.tensor_scalar(T.limf[:, 4:8], T.limi[:], 3.5, None, A.add))
     V(1, 1, ("limf",), ("thr",), lambda e: e.tensor_copy(col[:, 7:8], T.limf[:, 0:1]))
     sigmoid = "A" in CPQ["A"] + CPQ["B"]
 
     def nthr():
-        if sigmoid: V(1, 1, ("thr",), ("nthr",), lambda e: e.tensor_scalar(col[:, 9:10], col[:, 7:8], -256.0, 128.0, A.mult, A.add), tag="e4")
+        if sigmoid: C(1, ("thr",), ("nthr",), lambda e: e.activation(col[:, 9:10], col[:, 7:8], F.Copy, bias=128.0, scale=-256.0), tag="e5")
     nthr()
-    if sigmoid or OPQ["pass"] == "A":
-        C(1400, ("ones",), ("ejA",), lambda e: e.activation(T.ejA[:], ON[:, 0:128], F.Sigmoid))
+    if sigmoid or "A" in OPQ["A"][0] + OPQ["B"][0]:
+        C(1400, ("ones",), ("ej",), lambda e: e.activation(T.ej[:], ON[:, 0:128], F.Sigmoid))
     V(128, .5, ("Id",), ("Im",), lambda e: e.tensor_scalar(T.Im[:], T.Id[:], -1.0, None, A.mult))
-    V(1, 1, (), ("E20",), lambda e: e.memset(T.E2[:, 0:1], 0.0))
-    V(143, 2, ("E",), ("E21",), lambda e: e.tensor_tensor(T.E2[:, 1:144], T.E[:, 1:144], T.E[:, 0:143], A.subtract))
-    V(144, .5, ("E", "c4"), ("wE",), lambda e: e.tensor_scalar(T.wE[:], T.E[:], col[:, 4:5], None, A.mult))
-    V(144, .5, ("E20", "E21", "c4"), ("wD",), lambda e: e.tensor_scalar(T.wD[:], T.E2[:], col[:, 4:5], None, A.mult))
+    every = SUMS["A"] + SUMS["B"] != "AA"
+    if "W" in SUMS["A"] + SUMS["B"]:
+        V(144, .5, ("E", "c4"), ("wQ",), lambda e: e.tensor_scalar(T.wQ[:], T.E[:], col[:, 4:5], 1.0 / 4096, A.mult, A.mult))
+        Gc(128, ("Bd",), ("Dm0",), lambda e: e.affine_select(T.Dm[:], T.Bd[:], [[-1, 128]], A.is_equal, 0.0, 1, 1))
+        V(128, 2, ("Dm0", "Id"), ("Dm1",), lambda e: e.tensor_tensor(T.Dm[:], T.Dm[:], T.Id[:], A.subtract))
+        V(128, .5, ("Dm1",), ("Dm",), lambda e: e.tensor_scalar(T.Dm[:], T.Dm[:], 4096.0, None, A.mult))
+    if every:
+        V(1, 1, (), ("E20",), lambda e: e.memset(T.E2[:, 0:1], 0.0))
+        V(143, 2, ("E",), ("E21",), lambda e: e.tensor_tensor(T.E2[:, 1:144], T.E[:, 1:144], T.E[:, 0:143], A.subtract))
+        V(144, .5, ("E", "c4"), ("wE",), lambda e: e.tensor_scalar(T.wE[:], T.E[:], col[:, 4:5], None, A.mult))
+        V(144, .5, ("E20", "E21", "c4"), ("wD",), lambda e: e.tensor_scalar(T.wD[:], T.E2[:], col[:, 4:5], None, A.mult))
+        V(128, 1, ("Bd",), ("Bq32",), lambda e: e.tensor_scalar(T.Bq32[:], T.Bd[:], 1.0 / 4096, None, A.mult))
+    V(128, .5, ("Bd", "c4"), ("wq",), lambda e: e.tensor_scalar(T.wq[:], T.Bd[:], col[:, 4:5], 1.0 / 4096, A.mult, A.mult))
+    V(128, .5, ("Bd", "c4"), ("wB",), lambda e: e.tensor_scalar(T.wB[:], T.Bd[:], col[:, 4:5], None, A.mult))
     V(144, .5, ("E",), ("nE",), lambda e: e.tensor_scalar(T.nE[:], T.E[:], -16384.0, None, A.mult))
     V(144, 1, ("E",), ("E32",), lambda e: e.tensor_copy(T.E32[:], T.E[:]))
-    V(512, .5, (), ("R0",), lambda e: e.memset(T.R[:], 0.0))
-    V(32, .5, ("R0",), ("R",), lambda e: e.memset(T.R[:, 0:512:16], 255.0))
+    V(2048, .5, (), ("R0",), lambda e: e.memset(T.R[:], 0.0))
+    V(128, .5, ("R0",), ("R",), lambda e: e.memset(T.R[:, 0:2048:16], 255.0))
     V(128, .5, ("Bd", "c1"), ("Bn",), lambda e: e.tensor_scalar(T.Bn[:], T.Bd[:], col[:, 1:2], None, A.mult))
     V(128, 1, ("Bd",), ("Bd32",), lambda e: e.tensor_copy(T.Bd32[:], T.Bd[:]))
-    V(128, 1, ("Bd",), ("Bq32",), lambda e: e.tensor_scalar(T.Bq32[:], T.Bd[:], 1.0 / 4096, None, A.mult))
     V(128, .5, ("ones", "c2"), ("Qe",), lambda e: e.tensor_scalar(T.Qe[:], ON[:, 0:128], col[:, 2:3], None, A.mult))
     V(128, .5, ("Id",), ("Ih",), lambda e: e.tensor_scalar(T.Ih[:], T.Id[:], 0.5, None, A.mult))
-    V(128, .5, ("Id",), ("In",), lambda e: e.tensor_scalar(T.In[:], T.Id[:], -4096.0, None, A.mult))
+    V(128, 1, ("Id",), ("I32n",), lambda e: e.tensor_scalar(T.I32n[:], T.Id[:], -32.0, None, A.mult))
+    V(8, 1, ("Bd",), ("sel32a",), lambda e: e.tensor_scalar(T.sel32[:, 0:8], T.Bd[:, 0:128:16], 1.0 / 32, None, A.mult))
+    V(8, 1, ("Bd",), ("sel32b",), lambda e: e.tensor_copy(T.sel32[:, 8:16], T.Bd[:, 0:128:16]))
     V(128, 1, ("Id",), ("I32",), lambda e: e.tensor_copy(T.I32[:], T.Id[:]))
     P(128, ("R16",), lambda e: e.matmul(T.z0[:, 0:128], T.R16[:], T.R16[:], True, True), ("z0",))
     V(128, 1, (), ("mask",), lambda e: e.tensor_copy(T.mask[:], T.z0[:, 0:128]), ("z0",))
@@ -197,121 +219,171 @@ def make_ops(core, T, topo):
     V(8, .5, ("cr1",), ("crS",), lambda e: e.memset(cr[0:1, 0:128:16], -2048.0))
     V(128, .5, (), ("cr2",), lambda e: e.memset(cr[0:1, 128:256], 90112.0))
     V(8, .5, ("cr2",), ("crX",), lambda e: e.memset(cr[0:1, 128:256:16], -1048576.0))
-    V(32, 1, ("pi",), ("pi2",), lambda e: e.tensor_scalar(T.pi[:, 0:32], T.pi[:, 0:32], 15, None, A.bitwise_and))
-    V(8, 1, ("pi2",), ("pi3",), lambda e: e.tensor_scalar(T.pi[:, 0:8], T.pi[:, 0:8], 16, None, A.mult))
-    V(16, 1, ("pi2",), ("pi4",), lambda e: e.tensor_scalar(T.pi[:, 16:32], T.pi[:, 16:32], 32, None, A.mult))
-    V(32, 2, ("pi3", "pi4", "cvb0", "cvb1", "cvb2"), ("cv",), lambda e: e.tensor_tensor(T.cv[:], T.pi[:, 0:32], T.cvb[:, 0:32], A.add))
-    V(16, 1, ("cv",), ("CV",), lambda e: e.tensor_copy(T.CV[:], T.cv[:, 0:16]))
-    V(8, 1, ("cvb3",), ("cidx",), lambda e: e.tensor_copy(T.cidx[:], T.cvb[:, 32:40]))
+    V(128, .5, (), ("cr3",), lambda e: e.memset(cr[0:2, 256:384], 1.0 / 8192))
+    V(128, .5, ("cr3",), ("crQ",), lambda e: e.memset(cr[0:1, 256:384], -0.5))
+    V(48, 1, ("pi",), ("pi2",), lambda e: e.tensor_scalar(T.pi[:], T.pi[:], 15, None, A.bitwise_and))
+    for c, n, k in ((0, 8, 16), (16, 8, 16), (32, 16, 32)):
+        V(n, 1, ("pi2",), ("pj%d" % c,), lambda e, c=c, n=n, k=k: e.tensor_scalar(T.pi[:, c:c + n], T.pi[:, c:c + n], k, None, A.mult))
+    V(48, 2, ("pj0", "pj16", "pj32", "cvb0", "cvb8", "cvb16", "cvb24", "cvb32"), ("cv",),
+      lambda e: e.tensor_tensor(T.cv[:], T.pi[:], T.cvb[:, 0:48], A.add))
+    V(48, 1, ("cv",), ("CV",), lambda e: e.tensor_copy(T.CV[:, 0:48], T.cv[:]))
+    for b in "AB":
+        c = 48 if b == "A" else 56
+        V(8, 1, (), ("CW" + b,), lambda e, b=b, c=c: e.memset(T.CV[:, c:c + 8], 63.5 if SUMS[b] != "A" else -15.5 / 32))
+    V(8, 1, ("cvb48",), ("cidx",), lambda e: e.tensor_copy(T.cidx[:], T.cvb[:, 48:56]))
 
     pend = {}
 
-    def window(t, b):
-        ts = slice(t * 128, t * 128 + 128)
-        if t:
-            op("R", FLY, (), ("lf%d%s" % (t, b),), None, sem="af%d%s" % (t, b), cnt=len(lanes(peer[b][1], core)), sched=(pend["f" + b],))
-        DMA("S", 2.0, ("lf%d%s" % (t, b),), ("rows" + b,), T["rows" + b][:], T["lf" + b][:, ts], "r%d%s" % (t, b), tag="D1")
-        for j in range(1, 16):
-            DMA("S", 2.5, ("rows" + b,), ("win%s%d" % (b, j),), T["win" + b][j:128:16, 128 * j:2048], T["rows" + b][:, 1:17 - j, :],
-                "w%d%s" % (t, b), tag="Dj")
+    def window(t):
+        for b in "AB":
+            if t: op("R", FLY, (), ("lu%d%s" % (t, b),), None, sem="au%d%s" % (t, b), cnt=len(lanes(peer[b][1], core)), sched=(pend[b],))
+            V(128, 1, ("lu%d%s" % (t, b),), ("lf" + b,), lambda e, b=b: e.tensor_copy(T.lf[:, half[b]], lists(t, b)), tag="lf" + b)
+            DMA("S", 2.0, ("lf" + b,), ("rows" + b,), T["rows" + b][:], T.lf[:, half[b]], "r%d%s" % (t, b), tag="D1" + b)
+            c = 16 * half[b].start
+            for j in range(1, 16):
+                DMA("S", WIN, ("rows" + b,), (wins[b][j],), T.win[j:128:16, c + 128 * j:c + 2048], T["rows" + b][:, 1:17 - j, :],
+                    "w%d%s" % (t, b), tag="Dj" + b)
 
     def front(t, b):
         last = t == RO - 1
-        ts = slice(t * 128, t * 128 + 128)
         b0, b1, b2 = "0" + b, "1" + b, "2" + b
         p0, p1, p2 = T["p0" + b], T["p1" + b], T["p2" + b]
-        lu = T["lu" + b]; luk = "lu%d%s" % (t, b)
-        q = {n: T[n + b] for n in ("G", "M", "H", "us", "Lp", "t32", "c32", "Wm", "Ws", "pass", "zo", "cu", "ej", "q", "Z", "Zt", "Zh", "cm")}
+        luk = "lu%d%s" % (t, b)
+        q = {n: T[n + b] for n in ("G", "M", "H", "us", "Lp", "t32", "c32", "Wm", "Ws", "pass", "zo", "cu", "q", "Z", "Zt", "Zh", "cm", "Gm")}
         G, M, H = q["G"], q["M"], q["H"]
-        if t:
-            op("R", FLY, (), (luk,), None, sem="au%d%s" % (t, b), cnt=len(lanes(peer[b][1], core)), sched=(pend["u" + b],))
-        V(128, 1, (luk, "c6"), ("Lp" + b,), lambda e: e.tensor_scalar(q["Lp"][:], lu[:, ts], 16.0, col[:, 6:7], A.mult, A.add), tag="Lp")
-        for j in range(4):
-            f = slice(j * 512, j * 512 + 512); o = slice(t * 128 + j * 32, t * 128 + j * 32 + 32)
-            gather(G1Q[b][j], 512, ("X", luk), ("G%s%d" % (b, j),), G[:, f], T.X[:, 0:8192].indirect(lu[:, o]), tag="G1")
-            V(512, .5, ("G%s%d" % (b, j), "R"), ("M%s%d" % (b, j),),
-              lambda e, f=f: e.tensor_tensor_scan(M[:, f], T.R[:, 0:512], G[:, f], 0.0, A.max, A.min), tag="SC")
-            if CPQ[b][j] == "V":
-                V(512, .5, ("M%s%d" % (b, j), "thr"), ("H%s%d" % (b, j),),
+        Lp = q["Lp"][:]
+        allp, early = SUMS[b] != "A", SUMS[b] == "W"
+        if OPQ[b][3] == "A":
+            C(128, ("lf" + b, "c6"), ("Lp" + b,), lambda e: e.activation(Lp, T.lf[:, half[b]], F.Identity, bias=col[:, 6:7], scale=16.0), tag="Lp")
+        else:
+            V(128, 1, (luk, "c6"), ("Lp" + b,), lambda e: e.tensor_scalar(Lp, lists(t, b), 16.0, col[:, 6:7], A.mult, A.add), tag="Lp")
+        for who, j0, j1 in pieces(G1Q[b]):
+            gather(who, 512 * (j1 - j0), ("X", luk), names("G" + b, j0, j1), G[:, 512 * j0:512 * j1],
+                   T.X[:, 0:8192].indirect(lists(t, b, j0, j1)), tag="G1")
+        for who, j0, j1 in pieces(SCQ[b]):
+            f = slice(512 * j0, 512 * j1); n = 512 * (j1 - j0)
+            V(n, .5, names("G" + b, j0, j1) + ["R"], names("M" + b, j0, j1),
+              lambda e, f=f, n=n: e.tensor_tensor_scan(M[:, f], T.R[:, 0:n], G[:, f], 0.0, A.max, A.min), tag="SC")
+        for who, j0, j1 in pieces(CPQ[b]):
+            f = slice(512 * j0, 512 * j1); n = 512 * (j1 - j0)
+            if who == "V":
+                V(n, .5, names("M" + b, j0, j1) + ["thr"], names("H" + b, j0, j1),
                   lambda e, f=f: e.tensor_scalar(H[:, f], M[:, f], col[:, 7:8], None, A.is_ge), tag="CP")
             else:
-                C(512, ("M%s%d" % (b, j), "nthr"), ("H%s%d" % (b, j),),
+                C(n, names("M" + b, j0, j1) + ["nthr"], names("H" + b, j0, j1),
                   lambda e, f=f: e.activation(H[:, f], M[:, f], F.Sigmoid, bias=col[:, 9:10], scale=256.0), tag="CP")
-            if j & 1:
-                h = j // 2; o = slice(h * 64, h * 64 + 64)
-
-                def sums(e, dst, row, ws, src, h=h, o=o):
-                    e.matmul(dst[:, o], row, ON[0:row.shape[0], 0:64], True, False)
-                    for i in range(16):
-                        r = e.matmul(dst[:, o], ws[i][:, 15 - i:143 - i], src[:, h * 1024 + i:h * 1024 + 1024:16], False, i == 15)
-                    return r
-                P(1088, ("G%s%d" % (b, j - 1), "G%s%d" % (b, j), "wE", "wD", "crS", "ones"),
-                  lambda e, f=sums: f(e, p1, cr[0:2, 0:128], [T.wD] * 15 + [T.wE], G), (b1,), tag="dS")
-                P(1088, ("H%s%d" % (b, j - 1), "H%s%d" % (b, j), "nE", "crX", "ones"),
-                  lambda e, f=sums: f(e, p0, cr[0:1, 128:256], [T.nE] * 16, H), (b0,), tag="cnt")
-        mk = ["M%s%d" % (b, j) for j in range(4)]
-        if OPQ["pass"] == "V":
+        for h in (0, 1):
+            def sums(e, dst, row, ws, src, i0, c=0, whole=False, h=h):
+                o = slice(c + h * 64, c + h * 64 + 64)
+                if whole:
+                    if i0 == 0 and h == 0: e.matmul(dst[:, c:c + 128], row, ON[0:row.shape[0], 0:128], True, False)
+                elif i0 == 0: e.matmul(dst[:, o], row, ON[0:row.shape[0], 0:64], True, False)
+                for i in range(i0, i0 + CHUNK):
+                    r = e.matmul(dst[:, o], ws[i][:, 15 - i:143 - i], src[:, h * 1024 + i:h * 1024 + 1024:16], False, i == 15 and not whole)
+                return r
+            for i0 in range(0, 16 if early else 0, CHUNK):
+                P(68 * CHUNK, names("G" + b, 2 * h, 2 * h + 2) + ["wQ", "crQ", "ones"],
+                  lambda e, f=sums, i0=i0: f(e, p2, cr[0:2, 256:384], [T.wQ] * 16, G, i0, 384), (b2,), tag="xS")
+            for i0 in range(0, 16 if allp else 0, CHUNK):
+                P(68 * CHUNK, names("G" + b, 2 * h, 2 * h + 2) + ["wE", "wD", "crS", "ones"],
+                  lambda e, f=sums, i0=i0: f(e, p1, cr[0:2, 0:128], [T.wD] * 15 + [T.wE], G, i0, 0, early), (b1,), tag="dS")
+            if early and h:
+                V(128, 1, (), ("q" + b,), lambda e: e.tensor_scalar(q["q"][:], p2[:, 384:512], MAGIC, MAGIC, A.add, A.subtract), (b2,), tag="q")
+                P(128, ("q" + b, "Dm"), lambda e: e.matmul(p1[:, 0:128], T.Dm[:], q["q"][:], False, True), (b1,), tag="dq")
+            for i0 in range(0, 16, CHUNK):
+                P(68 * CHUNK, names("H" + b, 2 * h, 2 * h + 2) + ["nE", "crX", "ones"],
+                  lambda e, f=sums, i0=i0: f(e, p0, cr[0:1, 128:256], [T.nE] * 16, H, i0), (b0,), tag="cnt")
+        if OPQ[b][0] == "V":
             V(128, 1, (), ("pass" + b,), lambda e: e.tensor_scalar(q["pass"][:], p0[:, 0:128], 0.0, None, A.is_lt), (b0,), tag="pass")
         else:
             C(128, (), ("pass" + b,), lambda e: e.activation(q["pass"][:], p0[:, 0:128], F.Sigmoid, scale=-1.0), (b0,), tag="pass")
-        V(128, 1, ("pass" + b,), ("us" + b,), lambda e: e.tensor_tensor(q["us"][:], q["pass"][:], p1[:, 0:128], A.mult), (b1,), tag="us")
         P(128, ("pass" + b, "Bn"), lambda e: e.matmul(p0[:, 128:256], q["pass"][:], T.Bn[:], True, True), (b0,), tag="mT")
-        P(512, ("us" + b, "Bq32"), lambda e: e.matmul(p1[:, 384:512], T.Bq32[:], q["us"][:], True, True), (b1,), tag="x")
-        P(512, ("us" + b, "Bd32"), lambda e: e.matmul(p2[:, 128:256], T.Bd32[:], q["us"][:], True, False), (b2,), tag="u1")
         V(128, 1, ("mask",), ("Wm" + b,), lambda e: e.tensor_tensor(q["Wm"][:], p0[:, 128:256], T.mask[:], A.mult), (b0,), tag="Wm")
-        V(128, 1, (), ("q" + b,), lambda e: e.tensor_scalar(q["q"][:], p1[:, 384:512], MAGIC, MAGIC, A.add, A.subtract), (b1,), tag="q")
 
-        def mP(e):
-            e.matmul(p0[:, 384:400], T.Id[:], T.CV[:], True, False)
+        def mP(e, c=0):
+            e.matmul(p0[:, 384:400], T.Id[:], T.CV[:, c:c + 16], True, False)
             return e.matmul(p0[:, 384:400], q["Wm"][:], T.sel[:], False, True)
         P(128, ("Wm" + b, "Id", "CV", "sela", "selb"), mP, (b0,), tag="mP")
-        P(128, ("q" + b, "In"), lambda e: e.matmul(p2[:, 128:256], T.In[:], q["q"][:], False, True), (b2,), tag="u2")
         V(16, 1, (), ("zo" + b,), lambda e: e.tensor_copy(q["zo"][:], p0[:, 384:400]), (b0,), tag="zo")
-        C(128, ("c8",), (), lambda e: e.activation(p2[:, 256:384], p2[:, 128:256], F.Square, bias=col[:, 8:9]), (b2,), tag="Sq")
-        gather(OPQ["Z"], 128, ["zo" + b] + mk, ("Z" + b,), q["Z"][:], M[:, 0:2048].indirect(q["zo"][:, 0:8]), tag="Z")
-        V(128, 1, ("Lp" + b,), ("t32" + b,), lambda e: e.tensor_tensor(q["t32"][:], p2[:, 256:384], q["Lp"][:], A.add), (b2,), tag="t32")
+        if allp:
+            V(128, 1, ("pass" + b,), ("us" + b,), lambda e: e.tensor_tensor(q["us"][:], q["pass"][:], p1[:, 0:128], A.mult), (b1,), tag="us")
+            if not early: P(512, ("us" + b, "Bq32"), lambda e: e.matmul(p1[:, 384:512], T.Bq32[:], q["us"][:], True, True), (b1,), tag="x")
+            P(512, ("us" + b, "Bq32"), lambda e: e.matmul(p2[:, 128:256], T.Bq32[:], q["us"][:], True, early), (b2,), tag="u1")
+        else:
+            gather(OPQ[b][4], 128, ["zo" + b] + names("G" + b, 0, 4), ("Gm" + b,), q["Gm"][:], G[:, 0:2048].indirect(q["zo"][:, 0:8]), tag="Gm")
+            for dst, bk, stop in ((p1[:, 384:512], b1, True), (p2[:, 128:256], b2, False)):
+                P(128, ("crQ", "ones"), lambda e, dst=dst: e.matmul(dst, cr[0:2, 256:384], ON[0:2, 0:128], True, False), (bk,), tag="x0")
+                P(128, ("Gm" + b, "wq"), lambda e, dst=dst, stop=stop: e.matmul(dst, T.wq[:], q["Gm"][:], False, stop), (bk,), tag="x")
+        if not early:
+            V(128, 1, (), ("q" + b,), lambda e: e.tensor_scalar(q["q"][:], p1[:, 384:512], MAGIC, MAGIC, A.add, A.subtract), (b1,), tag="q")
+            P(128, ("q" + b, "Im"), lambda e: e.matmul(p2[:, 128:256], T.Im[:], q["q"][:], False, True), (b2,), tag="u2")
+        C(128, ("c8",), (), lambda e: e.activation(p2[:, 256:384], p2[:, 128:256], F.Square, bias=col[:, 8:9], scale=4096.0), (b2,), tag="Sq")
+        gather(OPQ[b][1], 128, ["zo" + b] + names("M" + b, 0, 4), ("Z" + b,), q["Z"][:], M[:, 0:2048].indirect(q["zo"][:, 0:8]), tag="Z")
+        V(128, 1, ("Lp" + b,), ("t32" + b,), lambda e: e.tensor_tensor(q["t32"][:], p2[:, 256:384], Lp, A.add), (b2,), tag="t32")
         V(128, 1, ("t32" + b,), ("c32" + b,), lambda e: e.tensor_scalar(q["c32"][:], q["t32"][:], 4, 8191, A.arith_shift_right, A.bitwise_and), tag="c32")
         V(128, 1, ("c32" + b,), ("cu" + b,), lambda e: e.tensor_copy(q["cu"][:], q["c32"][:]), tag="cu")
         P(128, ("Z" + b, "Ih"), lambda e: e.matmul(p1[:, 256:384], q["Z"][:], T.Ih[:], True, True), (b1,), tag="Ztr")
         C(128, (), ("Zt" + b,), lambda e: e.activation(q["Zt"][:], p1[:, 256:384], F.Copy), (b1,), tag="Zt")
         V(128, 1, ("c32" + b,), ("cm" + b,), lambda e: e.tensor_tensor(q["cm"][:], q["c32"][:], p0[:, 0:128], A.min), (b0,), tag="cm")
-        nw = T["nw" + b][:, ts]
-        op("V", gcost(128), ["win%s%d" % (b, j) for j in range(16)] + ["zo" + b, "cm" + b], ("nw%d%s" % (t, b),),
-           lambda e: e.tensor_tensor(nw, T["win" + b][:, 0:2048].indirect(q["zo"][:, 8:16]), q["cm"][:], A.max), tag="nw")
+        nw = T["nw" + b][:, t * 128:t * 128 + 128]
+        c = 16 * half[b].start
+        op("V", gcost(128), wins[b] + ["zo" + b, "cm" + b], ("nw%d%s" % (t, b),),
+           lambda e: e.tensor_tensor(nw, T.win[:, c:c + 2048].indirect(q["zo"][:, 8:16]), q["cm"][:], A.max), tag="nw")
         P(512, ("I32", "nw%d%s" % (t, b)), lambda e: e.matmul(p2[:, 0:128], T.I32[:], nw, True, False), (b2,), tag="nat1")
         if last:
             C(128, ("Z" + b,), ("yzs" + b,), lambda e: e.activation(T["ys" + b][:, 128:256], q["Z"][:], F.Copy), tag="yz")
             DMA("S", 2.0, ("yzs" + b,), (), T.yz[:, half[b]], T["ys" + b][:, 128:256], "out", tag="out")
             return
-        nxt = slice(t * 128 + 128, t * 128 + 256)
-        pend["f" + b] = op("G", 0.8, ("nw%d%s" % (t, b),), (), ("send", nw, T["lf" + b][:, nxt], "af%d%s" % (t + 1, b), peer[b][0]), sem="snd", tag="sendf")
         C(128, ("Z" + b,), ("Zh" + b,), lambda e: e.activation(q["Zh"][:], q["Z"][:], F.Copy, bias=-0.25, scale=0.5), tag="Zh")
-        P(512, ("us" + b, "Bd32"), lambda e: e.matmul(p1[:, 128:256], q["us"][:], T.Bd32[:], True, True), (b1,), tag="sT")
+        if allp:
+            P(512, ("us" + b, "Bd32"), lambda e: e.matmul(p1[:, 128:256], q["us"][:], T.Bd32[:], True, True), (b1,), tag="sT")
+        else:
+            P(128, ("Gm" + b, "wB"), lambda e: e.matmul(p1[:, 128:256], q["Gm"][:], T.wB[:], True, True), (b1,), tag="sT")
         V(128, 1, ("mask",), ("Ws" + b,), lambda e: e.tensor_tensor(q["Ws"][:], p1[:, 128:256], T.mask[:], A.mult), (b1,), tag="Ws")
-        P(256, ("Ws" + b, "Bd32"), lambda e: e.matmul(p1[:, 0:8], q["Ws"][:], T.Bd32[:, 0:128:16], True, True), (b1,), tag="sP")
-        c0 = 0 if b == "A" else 8
-        V(8, 1, (), ("Wi" + b,), lambda e: e.tensor_scalar(T.Wi[:, c0:c0 + 8], p1[:, 0:8], 2047.5, None, A.add), (b1,), tag="w1")
-        P(128, ("Qe", "pass" + b), lambda e: e.matmul(p0[:, 128:256], T.Qe[:], q["pass"][:], True, True), (b0,), tag="E")
-        ec = T.ec[:, 0:1] if b == "A" else T.ec[:, 1:2]
-        C(128, (), ("ec" + b, "ej" + b), lambda e: e.activation(q["ej"][:], p0[:, 128:256], F.Copy, accum_out=ec), (b0,), tag="Eacc")
 
     def joint(t):
-        V(16, 1, ("WiA", "WiB"), ("nu",), lambda e: e.tensor_scalar(T.nu[:], T.Wi[:], 31, None, A.bitwise_and), tag="w2")
-        V(16, 2, ("nu", "cv"), ("nv",), lambda e: e.tensor_tensor(T.nv[:], T.nu[:], T.cv[:, 16:32], A.add), tag="w3")
-        V(16, 1, ("nv",), ("rp",), lambda e: e.tensor_copy(T.rp[:], T.nv[:]), tag="w4")
-        V(1, 1, ("ecA", "ecB"), ("ei",), lambda e: e.tensor_tensor(T.ei[:, 0:1], T.ec[:, 0:1], T.ec[:, 1:2], A.add), tag="e1")
-        V(1, 1, ("ei",), ("ej2",), lambda e: e.tensor_scalar(T.ei[:, 1:2], T.ei[:, 0:1], 7, None, A.bitwise_and), tag="e2")
-        V(1, 2, ("ej2", "limf"), ("thr",), lambda e: e.tensor_tensor(col[:, 7:8], T.ei[:, 1:2], T.limf[:, t + 1:t + 2], A.add), tag="e3")
+        p1 = T.p1B
+
+        def sP(e, c, last):
+            e.matmul(p1[:, c:c + 16], T.Id[:], T.CV[:, 48 - c:64 - c], True, False)
+            e.matmul(p1[:, c:c + 8], T.WsA[:], T.sel32[:, c // 2:c // 2 + 8], False, False)
+            r = e.matmul(p1[:, c + 8:c + 16], T.WsB[:], T.sel32[:, c // 2:c // 2 + 8], False, last is None)
+            return r if last is None else e.matmul(p1[:, c:c + 16], T.I32n[:], last, False, True)
+        rd = ("WsA", "WsB", "Id", "CV", "CWA", "CWB", "sel32a", "sel32b", "I32n")
+        P(576, rd, lambda e: sP(e, 0, None), ("1B",), tag="sP")
+        V(16, 1, (), ("rq",), lambda e: e.tensor_scalar(T.rq[:], p1[:, 0:16], MAGIC, MAGIC, A.add, A.subtract), ("1B",), tag="w1")
+        P(832, rd + ("rq",), lambda e: sP(e, 16, T.rq[:]), ("1B",), tag="rP")
+        if (SUMS["A"] == "A") == (SUMS["B"] == "A"):
+            V(16, 1, (), ("rp",), lambda e: e.tensor_scalar(T.rp[:], p1[:, 16:32], 2047.5 if every else 0.0, None, A.add), ("1B",), tag="w2")
+        else:
+            for c, b in ((0, "A"), (8, "B")):
+                V(8, 1, (), ("rp",), lambda e, c=c, b=b: e.tensor_scalar(T.rp[:, c:c + 8], p1[:, 16 + c:24 + c], 2047.5 if SUMS[b] != "A" else 0.0, None, A.add), ("1B",), tag="w2")
+
+    def cuts(t):
+        p0 = T.p0A
+
+        def full(e):
+            e.matmul(p0[:, 128:256], T.Qe[:], T.passA[:], True, False)
+            return e.matmul(p0[:, 128:256], T.Qe[:], T.passB[:], False, True)
+        P(256, ("Qe", "passA", "passB"), full, ("0A",), tag="E")
+        ec = T.ec
+        C(200, (), ("ec", "ej"), lambda e: e.activation(T.ej[:], p0[:, 128:256], F.Copy, bias=-3.5 / 128, accum_out=ec[:, 0:1]), ("0A",), tag="Eacc")
+        C(1, ("ec",), ("e1",), lambda e: e.activation(ec[:, 1:2], ec[:, 0:1], F.Copy, bias=MAGIC, scale=0.125), tag="e1")
+        C(1, ("ec", "limg"), ("e2",), lambda e: e.activation(ec[:, 2:3], ec[:, 0:1], F.Identity, bias=T.limf[:, t + 5:t + 6]), tag="e2")
+        C(1, ("e1",), ("e3",), lambda e: e.activation(ec[:, 3:4], ec[:, 1:2], F.Copy, bias=-MAGIC), tag="e3")
+        C(1, ("e2", "e3"), ("thr",), lambda e: e.activation(col[:, 7:8], ec[:, 3:4], F.Identity, bias=ec[:, 2:3], scale=-8.0), tag="e4")
         nthr()
 
     zn = [0]
 
     def middle(t, b):
         Gh, Pm, cu, Zt = T["Gc" + b], T["P" + b], T["cu" + b], T["Zt" + b]
+        for who, j0, j1 in pieces(G2Q[b]):
+            gather(who, 512 * (j1 - j0), ("X", "cu" + b), names("Gc" + b, j0, j1), Gh[:, 512 * j0:512 * j1],
+                   T.X[:, 0:8192].indirect(cu[:, 32 * j0:32 * j1]), 0.5, tag="G2")
         for j in range(4):
-            f = slice(j * 512, j * 512 + 512); o = slice(j * 32, j * 32 + 32)
+            f = slice(j * 512, j * 512 + 512)
             z = "z%d" % (zn[0] & 1); zn[0] += 1
-            gather(G2Q[b][j], 512, ("X", "cu" + b), ("Gc%s%d" % (b, j),), Gh[:, f], T.X[:, 0:8192].indirect(cu[:, o]), 0.5, tag="G2")
             onv = MXQ[b][j] == "V"
             P(512, ("Zt" + b, "Exp"), lambda e, z=z, f=f, onv=onv: e.matmul(T[z][:], Zt[:], T.Exp[:, f], True, onv), (z,), tag="Zx")
             if onv:
@@ -324,32 +396,44 @@ def make_ops(core, T, topo):
         last = t == RO - 1
         b0, b1, b2 = "0" + b, "1" + b, "2" + b
         p0, p1, p2 = T["p0" + b], T["p1" + b], T["p2" + b]
-        q = {n: T[n + b] for n in ("Gc", "P", "OHc", "Km", "pm", "mn", "OH", "Y", "c32", "ki", "ku", "Zh")}
-        gk = ["Gc%s%d" % (b, j) for j in range(4)]
-        c0 = 0 if b == "A" else 8
+        q = {n: T[n + b] for n in ("Gc", "P", "OHc", "Km", "pm", "mn", "OH", "c32")}
 
-        def kc(e):
-            e.matmul(p0[:, 256:384], T.row16[0:1, :], ON[0:1, 0:128], True, False)
-            return e.matmul(p0[:, 256:384], ON[0:1, 0:128], T.rowi[0:1, :], False, False)
-
-        def kd(e, src, w, stop):
-            for i in range(16):
-                r = e.matmul(p0[:, 256 + i:384:16], src[:, i:2048:16], w, False, stop and i == 15)
-            return r
-        P(256, ("row16", "ones", "rowi"), kc, (b0,), tag="kc")
-        P(1024, gk + ["K8b"], lambda e: kd(e, q["Gc"], T.K8[:, 8:16], False), (b0,), tag="keyG")
-        P(1024, ["P%s%d" % (b, j) for j in range(4)] + ["K8a"], lambda e: kd(e, q["P"], T.K8[:, 0:8], True), (b0,), tag="keyP")
+        def keys(name, w, stop):
+            def kd(e, i0):
+                for i in range(i0, i0 + CHUNK):
+                    r = e.matmul(p0[:, 256 + i:384:16], q[name][:, i:2048:16], w, False, stop and i == 15)
+                return r
+            for i0 in range(0, 16, CHUNK):
+                P(64 * CHUNK, names(name + b, 0, 4) + ["K8a", "K8b"], lambda e, i0=i0: kd(e, i0), (b0,), tag="key" + name[0])
+        P(128, ("kl", "kr"), lambda e: e.matmul(p0[:, 256:384], T.kl[0:2, :], T.kr[0:2, :], True, False), (b0,), tag="kc")
+        keys("Gc", T.K8[:, 8:16], False)
+        keys("P", T.K8[:, 0:8], True)
         V(128, 1, ("Rk",), ("pm" + b,), lambda e: e.tensor_tensor_scan(q["pm"][:], T.Rk[:], p0[:, 256:384], 0.0, A.max, A.min), (b0,), tag="scan")
         least = q["pm"][:, 0:128].indirect(T.cidx[:])
         if not last:
             op("V", gcost(128), ("pm" + b, "cidx", "mask"), ("Km" + b,), lambda e: e.tensor_tensor(q["Km"][:], least, T.mask[:], A.mult), tag="Km")
-        gather(OPQ["mn"], 128, ("pm" + b, "cidx"), ("mn" + b,), q["mn"][:], least, tag="mn")
+        if OPQ[b][2] == "A":
+            gather("A", 128, ("pm" + b, "cidx"), ("mn" + b,), q["mn"][:], least, tag="mn")
+        else:
+            V(128, 1, ("Rk", "pm" + b), ("mn" + b,), lambda e: e.tensor_tensor_scan(q["mn"][:, 127::-1], T.Rk[:], q["pm"][:, 127::-1], 0.0, A.max, A.min), tag="mn")
         V(128, 1, ("mn" + b,), ("OH" + b,), lambda e: e.tensor_tensor(q["OH"][:], p0[:, 256:384], q["mn"][:], A.is_equal), (b0,), tag="OH")
-        if not last:
-            P(256, ("Km" + b, "Bd32"), lambda e: e.matmul(p1[:, 384:392], q["Km"][:], T.Bd32[:, 0:128:16], True, True), (b1,), tag="Kp")
-            V(8, 1, (), ("ki" + b,), lambda e: e.tensor_copy(q["ki"][:, 0:8], p1[:, 384:392]), (b1,), tag="k1")
+
+        def index(blocks):
+            n = 8 * len(blocks); c = 8 if blocks == "B" else 0
+            pk, bk = (T.z0, "z0") if b == "B" else (p1, b1)
+            for j, a in enumerate(blocks):
+                P(256, ("Km" + a, "Bd32"), lambda e, j=j, a=a: e.matmul(pk[:, 384 + 8 * j:392 + 8 * j], T["Km" + a][:], T.Bd32[:, 0:128:16], True, True), (bk,), tag="Kp" + a)
+            V(n, 1, (), ("ki" + b,), lambda e: e.tensor_copy(T.ki[:, c:c + n], pk[:, 384:384 + n]), (bk,), tag="k1")
+            V(n, 1, ("ki" + b,), ("kj" + b,), lambda e: e.tensor_scalar(T.ki[:, 16 + c:16 + c + n], T.ki[:, c:c + n], 2047, None, A.bitwise_and), tag="k2")
+            V(n, 1, ("kj" + b,), ["ku" + a for a in blocks], lambda e: e.tensor_copy(T.ku[:, c:c + n], T.ki[:, 16 + c:16 + c + n]), tag="k3")
+            for a in blocks:
+                k = half[a].start // 16
+                op("V", gcost(128), ["ku" + a, "Zh" + a] + names("Gc" + a, 0, 4), ("Y" + a,),
+                   lambda e, a=a, k=k: e.tensor_tensor(T.Y[:, half[a]], T["Gc" + a][:, 0:2048].indirect(T.ku[:, k:k + 8]), T["Zh" + a][:], A.add), tag="Y" + a)
+        if not last and b == "B": index("AB" if TAIL["A"][0] == "A" else "B")
         P(128, ("OH" + b, "Id"), lambda e: e.matmul(p1[:, 0:128], q["OH"][:], T.Id[:], True, True), (b1,), tag="OHT")
         V(128, 1, ("c32" + b,), ("OHc" + b,), lambda e: e.tensor_tensor(q["OHc"][:], q["c32"][:], p1[:, 0:128], A.mult), (b1,), tag="OHc")
+        if not last and b == "A" and TAIL["A"][0] != "A": index("A")
         P(512, ("E32", "OHc" + b), lambda e: e.matmul(p2[:, 0:128], T.E32[:, 15:143], q["OHc"][:], False, True), (b2,), tag="nat2")
         if last:
             ys = T["ys" + b]
@@ -358,29 +442,32 @@ def make_ops(core, T, topo):
             return
         su = T["su" + b][:, t * 128:t * 128 + 128]
         V(128, 1, (), ("su%d%s" % (t, b),), lambda e: e.tensor_copy(su, p2[:, 0:128]), (b2,), tag="su")
-        pend["u" + b] = op("G", 0.8, ("su%d%s" % (t, b),), (),
-                           ("send", su, T["lu" + b][:, t * 128 + 128:t * 128 + 256], "au%d%s" % (t + 1, b), peer[b][0]), sem="snd", tag="sendu")
-        V(8, 1, ("ki" + b,), ("kj" + b,), lambda e: e.tensor_scalar(q["ki"][:, 8:16], q["ki"][:, 0:8], 2047, None, A.bitwise_and), tag="k2")
-        V(8, 1, ("kj" + b,), ("ku" + b,), lambda e: e.tensor_copy(q["ku"][:], q["ki"][:, 8:16]), tag="k3")
-        op("V", gcost(128), ["ku" + b, "Zh" + b] + gk, ("Y" + b,),
-           lambda e: e.tensor_tensor(q["Y"][:], q["Gc"][:, 0:2048].indirect(q["ku"][:]), q["Zh"][:], A.add), tag="Y")
+        pend[b] = op("G", 0.8, ("su%d%s" % (t, b),), (), ("send", su, lists(t + 1, b), "au%d%s" % (t + 1, b), peer[b][0]), sem="snd", tag="send")
 
-    def scatter(b):
+    def scatter(t, b):
+        if TAIL["B"][0] == "A":
+            if b == "B":
+                op("V", 0.06 + 256 * 3.5 * CY, ("YA", "YB", "rp"), ("X",), lambda e: e.tensor_copy(T.X[:, 0:8192].indirect(T.rp[:]), T.Y[:]), tag="scat")
+            return
         c0 = 0 if b == "A" else 8
         op("V", 0.06 + 128 * 3.5 * CY, ("Y" + b, "rp"), ("X",),
-           lambda e: e.tensor_copy(T.X[:, 0:8192].indirect(T.rp[:, c0:c0 + 8]), T["Y" + b][:]), tag="scat")
+           lambda e: e.tensor_copy(T.X[:, 0:8192].indirect(T.rp[:, c0:c0 + 8]), T.Y[:, half[b]]), tag="scat")
+
+    def both(step, t):
+        for b in "AB":
+            cur[0] = b
+            step(t, b)
+        cur[0] = ""
 
     for t in range(RO):
-        for step in (window, front, None, middle, back):
-            for b in "AB":
-                cur[0] = b
-                if step: step(t, b)
-            cur[0] = ""
-            if step is None and t < RO - 1: joint(t)
+        window(t)
+        both(front, t)
+        if t < RO - 1: joint(t)
+        both(middle, t)
+        both(back, t)
         if t < RO - 1:
-            for b in "AB":
-                cur[0] = b
-                scatter(b)
+            cuts(t)
+            both(scatter, t)
     return ops, lanes, peer
 
 
@@ -390,21 +477,23 @@ def schedule(ops):
     succ = [[] for _ in range(n)]
     for i in range(n):
         for d in pred[i]: succ[d].append(i)
-    que = [{"AD": "A"}.get(o["q"], o["q"]) for o in ops]
+    que = [DMAS.get(o["q"], o["q"]) for o in ops]
     cost = [o["c"] for o in ops]
-    hold = [0.0 if o["q"] == "R" else ISSUE if o["q"] in ("AD", "S") else o["c"] for o in ops]
+    hold = [0.0 if o["q"] == "R" else ISSUE if o["q"] in DMAS else o["c"] for o in ops]
 
     def lag(a, b):
         return WAKE if ops[a]["q"] != ops[b]["q"] else SELF if (a in ops[b]["wait"] or b in ops[a]["wait"]) else 0.0
+    before = [[(d, cost[d] + lag(d, i)) for d in pred[i]] for i in range(n)]
+    behind = [[(d, cost[d] + lag(d, i)) for d in succ[i]] for i in range(n)]
 
-    def place(key, before, after, back):
-        need = [len(x) for x in before]
+    def place(key, first, after, back):
+        need = [len(x) for x in first]
         ready = [i for i in range(n) if not need[i]]
         start, busy = [0.0] * n, {}
         while ready:
-            i = min(ready, key=key)
+            i = min(ready, key=lambda k: key[k])
             ready.remove(i)
-            s = max([start[d] + cost[d] + lag(d, i) for d in before[i]], default=0.0)
+            s = max([start[d] + w for d, w in first[i]], default=0.0)
             shift = cost[i] - hold[i] if back else 0.0
             line = busy.setdefault(que[i], [])
             s += shift; k = len(line)
@@ -421,13 +510,20 @@ def schedule(ops):
     tail = [0.0] * n
     for i in range(n - 1, -1, -1):
         tail[i] = cost[i] + max([tail[s] + lag(i, s) for s in succ[i]], default=0.0)
-    best = place(lambda i: (-tail[i], i), pred, succ, False)
-    last = best
-    for _ in range(PASSES):
-        fw = last[0]
-        bw = place(lambda i: (-fw[i] - cost[i], -i), succ, pred, True)[0]
-        last = place(lambda i: (-bw[i] - cost[i], i), pred, succ, False)
-        if last[1] < best[1]: best = last
+    best = place([-x for x in tail], before, succ, False)
+    rng = np.random.default_rng(0)
+    kinds = sorted(set(o["tag"] for o in ops))
+    kind = [kinds.index(o["tag"]) for o in ops]
+    now = best
+    for k in range(PASSES):
+        push = rng.normal(0.0, SHAKE, len(kinds)) * (rng.random(len(kinds)) < SHARE) if k else np.zeros(len(kinds))
+        if k & 1:
+            last = place([s + float(push[j]) for s, j in zip(now[0], kind)], before, succ, False)
+        else:
+            bw = place([-(s + c + float(push[j])) for s, c, j in zip(now[0], cost, kind)], behind, pred, True)[0]
+            last = place([-(s + c) for s, c in zip(bw, cost)], before, succ, False)
+        if last[1] <= now[1] + SLACK * (1 - k / PASSES) * rng.random(): now = last
+        if last[1] <= best[1]: best = last
     for o in ops: o["s"] = best[0][o["i"]]
     return sorted(range(n), key=lambda i: (-1.0 if "first" in ops[i] else best[0][i], i)), best[1]
 
@@ -440,11 +536,11 @@ def rank_program(g, core, T, topo):
         PLAN.extend([schedule(ops), [o["s"] for o in ops]])
     order = PLAN[0][0]
     for o in ops: o["s"] = PLAN[1][o["i"]]
-    eng = {"V": g.vector, "A": g.scalar, "T": g.tensor, "G": g, "S": g.sync, "AD": g.scalar}
+    eng = {"V": g.vector, "A": g.scalar, "T": g.tensor, "G": g, "S": g.sync, "AD": g.scalar, "GD": g}
     qsem = {"V": "qV", "A": "qA", "T": "qT", "G": "qG"}
-    total, seen = {}, {}
+    total = {}
     for o in ops:
-        if o["q"] in ("S", "AD"): total[o["sem"]] = total.get(o["sem"], 0) + 16
+        if o["q"] in DMAS: total[o["sem"]] = total.get(o["sem"], 0) + 16
     cnt, known, snap, done = {}, {}, {}, {}
     sent = 0
     for i in order:
@@ -452,10 +548,10 @@ def rank_program(g, core, T, topo):
         if o["q"] == "R":
             done[i] = (o["sem"], o["n"]); snap[i] = {o["sem"]: o["n"]}
             continue
-        qn = "A" if o["q"] == "AD" else o["q"]
+        qn = DMAS.get(o["q"], o["q"])
         e = eng[o["q"]]
         kn = known.setdefault(qn, {})
-        for d in sorted(o["wait"], key=lambda d: -ops[d].get("s", 0.0)):
+        for d in sorted(o["wait"], key=lambda d: -ops[d]["s"]):
             s, v = done[d]
             if kn.get(s, 0) >= v: continue
             e.wait_ge(T.sem[s], v)
@@ -471,7 +567,7 @@ def rank_program(g, core, T, topo):
             done[i] = ("snd", sent); snap[i] = dict(kn)
         else:
             r = o["fn"](e)
-            if o["q"] in ("S", "AD"):
+            if o["q"] in DMAS:
                 r.then_inc(T.sem[o["sem"]], 16)
                 done[i] = (o["sem"], total[o["sem"]]); cnt[o["sem"]] = total[o["sem"]]
             else:

@@ -1,4 +1,6 @@
+import math
 import numpy as np
+from concourse.bass import DstId, RemoteDMATransfer
 from concourse.mybir import AluOpType, AxisListType, ActivationFunctionType
 
 A = AluOpType
@@ -6,56 +8,62 @@ F = ActivationFunctionType
 RO = 4
 BF, F32, I32, U16 = "bfloat16", "float32", "int32", "uint16"
 MAGIC = 12582912.0
+SETS = "AB"
 
 SCRATCH = {}
-for _n in ("p0A", "p1A", "p2A", "p0B", "p1B", "p2B", "z0", "z1"):
-    SCRATCH[_n] = ("psum", [128, 512], F32)
-for _b in "AB":
-    for _n in ("G", "M", "H", "Gc", "P"):
-        SCRATCH[_n + _b] = ("sbuf", [128, 2048], BF)
-    for _n, _d in (("us", F32), ("Lp", F32), ("t32", I32), ("c32", I32), ("Wm", BF), ("Ws", F32), ("cm", F32), ("OHc", F32),
-                   ("Km", F32), ("pm", F32), ("mn", F32), ("pass", BF), ("q", BF), ("OH", BF), ("Z", BF), ("Zt", BF),
-                   ("Zh", F32), ("cu", U16), ("Gm", BF)):
-        SCRATCH[_n + _b] = ("sbuf", [128, 128], _d)
-    SCRATCH["nw" + _b] = ("sbuf", [128, 512], F32)
-    SCRATCH["ys" + _b] = ("sbuf", [128, 256], F32)
-    SCRATCH["zo" + _b] = ("sbuf", [128, 16], U16)
-    SCRATCH["su" + _b] = ("sbuf", [128, 384], U16)
-    SCRATCH["rows" + _b] = ("dram", [8, 16, 128], F32)
-for _n, _s, _d in (("X", 8192, BF), ("R", 2048, BF), ("Rk", 128, F32), ("ones", 256, BF), ("Exp", 2048, BF),
-                   ("win", 4096, F32), ("lu", 1024, U16), ("lf", 256, F32), ("Y", 256, I32), ("ki", 32, I32), ("ku", 16, U16),
-                   ("E", 144, BF), ("E2", 144, BF), ("wE", 144, BF), ("wD", 144, BF), ("nE", 144, BF), ("E32", 144, F32),
-                   ("Bd", 128, BF), ("Id", 128, BF), ("Ih", 128, BF), ("Im", 128, BF), ("Bn", 128, BF), ("Qe", 128, BF),
-                   ("R16", 128, BF), ("mask", 128, BF), ("K8", 16, BF), ("sel", 16, BF), ("CV", 64, BF), ("cr", 384, BF),
-                   ("kl", 128, BF), ("kr", 128, BF), ("Bd32", 128, F32), ("Bq32", 128, F32), ("I32", 128, F32),
-                   ("wQ", 144, BF), ("Dm", 128, BF), ("wq", 128, BF), ("wB", 128, BF),
-                   ("z8", 16, F32), ("cols", 16, F32), ("wi", 1, I32), ("kni", 1, I32), ("limi", 4, I32), ("limf", 8, F32),
-                   ("tub", 256, I32), ("pi", 48, I32), ("cvb", 56, I32), ("cv", 48, I32), ("cidx", 8, U16),
-                   ("sel32", 16, F32), ("I32n", 128, F32), ("rq", 16, F32), ("rp", 16, U16), ("ec", 4, F32), ("ej", 128, BF)):
+for _b in SETS:
+    for _n in ("p0", "p1", "p2", "z"):
+        SCRATCH[_n + _b] = ("psum", [128, 512], F32)
+    for _n, _s, _d in (("X", 8192, BF), ("G", 2048, BF), ("M", 2048, BF), ("H", 2048, BF), ("Gc", 2048, BF), ("P", 2048, BF),
+                       ("Lp", 128, F32), ("t32", 128, I32), ("c32", 128, I32), ("Wm", 128, BF), ("cm", 128, F32), ("Km", 128, BF),
+                       ("pm", 128, F32), ("pass", 128, BF), ("q", 128, BF), ("Z", 128, BF), ("Zt", 128, BF), ("cu", 128, U16),
+                       ("uf", 128, F32), ("us", 128, F32), ("Ws", 128, F32), ("Gy", 256, BF), ("lf", 512, F32), ("nw", 128, F32),
+                       ("nl", 640, F32), ("zo", 16, U16), ("ku", 16, U16), ("ki", 16, I32), ("rq", 8, I32), ("rd", 8, F32),
+                       ("rp", 16, U16), ("Y", 256, I32), ("su", 768, U16), ("lu", 512, U16), ("win", 2048, F32),
+                       ("cw", 2048, I32), ("wE", 512, BF), ("col", 8, F32)):
+        SCRATCH[_n + _b] = ("sbuf", [128, _s], _d)
+    SCRATCH["rows" + _b] = ("dram", [8, 32, 128], F32)
+for _n, _s, _d in (("R", 512, BF), ("Bd32", 128, F32), ("Bd128", 128, F32), ("Dm", 128, F32), ("Rk", 128, F32), ("ones", 256, BF),
+                   ("Exp", 2048, BF), ("E", 144, BF), ("pE", 144, BF), ("Bd", 128, BF), ("Id", 128, BF), ("Sw", 128, BF),
+                   ("Im", 128, BF), ("Bn", 128, BF), ("mask", 128, BF), ("K8", 16, BF), ("sel", 24, BF), ("CV", 32, BF),
+                   ("cr", 896, BF), ("kr", 128, BF), ("I32", 128, F32), ("S32", 128, F32), ("neg", 128, BF), ("cols", 8, F32),
+                   ("l15", 2, BF), ("prm", 8, I32), ("prf", 8, F32), ("tub", 256, I32), ("pi", 32, I32), ("cv", 32, I32),
+                   ("cidx", 8, U16), ("vt", 16, F32), ("cst", 8, F32), ("nb", 8, F32), ("ec", 2, BF), ("eR", 1, F32),
+                   ("ej", 128, BF)):
     SCRATCH[_n] = ("sbuf", [128, _s], _d)
 
-SEMAPHORES = ["qV", "qA", "qT", "qG", "lX", "ltub", "lwt", "lkn", "llim", "snd", "out"]
-SEMAPHORES += [_n + str(_t) + _b for _n in "wr" for _t in range(RO) for _b in "AB"]
-SEMAPHORES += ["au%d%s" % (_t, _b) for _t in range(1, RO) for _b in "AB"]
+PARTS = 4
+SEMAPHORES = ["qV", "qA", "qT", "qG", "ltub", "lwt", "lkn", "llim", "snd", "out"]
+SEMAPHORES += ["x%d%s" % (_t, _b) for _t in range(2 * PARTS) for _b in SETS]
+SEMAPHORES += [_n + str(_t) + _b for _n in "wrc" for _t in range(RO) for _b in SETS]
+SEMAPHORES += [_n + str(_t) + _b for _n in ("au", "af") for _t in range(1, RO) for _b in SETS]
 
-CY = 0.86e-3
-PEC = 0.56e-3
+CY = np.array([0.85e-3, 1.1e-3])
+PEC = np.array([0.55e-3, 0.72e-3])
 VFIX, AFIX = 0.03, 0.06
-GA = 1.5
-WAKE = 0.2
-FLY = 2.5
-SELF = 0.12
-WIN = 5.5
-ISSUE = 0.2
-PASSES, SHAKE, SHARE, SLACK = 1500, 0.7, 0.04, 0.4
-G1Q = {"A": "AVAA", "B": "AAAV"}
-G2Q = {"A": "AAAV", "B": "AVAA"}
-SCQ = {"A": "V-VV", "B": "VVVV"}
-CPQ = {"A": "V-AV", "B": "AVVA"}
-MXQ = {"A": "VAAA", "B": "VVVA"}
-OPQ = {"A": "VAAAV", "B": "VAAAV"}
-SUMS = {"A": "V", "B": "A"}
-TAIL = {"A": "A", "B": "A"}
+GA = np.array([1.56, 1.6])
+SCA = np.array([3.8, 3.8])
+WAKE = np.array([0.2, 0.18])
+FLY = np.array([2.2, 2.0])
+SELF = np.array([0.14, 0.12])
+DMA0 = np.array([2.2, 2.0])
+LOAD = np.array([5.5, 4.5])
+ISSUE = np.array([0.22, 0.15])
+DCQ = "S"
+WEIGHT = (0.5, 0.5)
+EARLY, FLIP = 0.5, 0.1
+STEPS, HEAT, EVERY, FAR, SEED = 40000, 0.25, 0.7, 4, 2
+G1Q = {"A": "AVAA", "B": "AVAA"}
+G2Q = {"A": "AVAA", "B": "AVAA"}
+SCQ = "VVVV"
+CPQ = {"A": "AVAV", "B": "AVAV"}
+MXQ = {"A": "VAAV", "B": "VAAV"}
+OPQ = {"A": "VAAAAV", "B": "VAAAAV"}
+SUMS = {"A": "W", "B": "G"}
+DUP = {"A": "VAVV", "B": "VVVV"}
+STRETCH, BEHIND = (1.2,), (0.2,)
+FOLD = True
+ZERO = {"A": "A", "B": "G"}
 CHUNK = 4
 PLAN = []
 DMAS = {"S": "S", "AD": "A", "GD": "G"}
@@ -68,32 +76,58 @@ def pieces(s):
 
 def names(s, j0, j1): return [s + str(j) for j in range(j0, j1)]
 def vcost(n, f=1.0): return VFIX + max(64, n * f) * CY
+def acost(n): return AFIX + max(64, n) * CY
 def gcost(n): return 0.06 + n * GA * CY
+
+
+def choose(ops, i, q):
+    o = ops[i]
+    o["q"] = q
+    o["c"], o["fn"] = o["alt"][q]
+    if "twin" in o: ops[o["twin"]]["q"] = "T" if q == "A" else "N"
+
+
+def waits(ops, o):
+    return o["hard"] | set(d for d in o["soft"] if ops[d]["q"] != o["q"] or o["q"] in DMAS)
+
+
+def lanes(T, topo, core):
+    r, n = T.rank_of(core), len(T.cores)
+    to = [T.cores[(r + 1) % n], T.cores[(r - 1) % n]]
+    may = [topo.engines(core, d) for d in to]
+    few = 0 if len(may[0]) <= len(may[1]) else 1
+    rest = [x for x in may[1 - few] if x not in may[few]]
+    if rest:
+        k = min(len(rest), len(may[few]))
+        use = {few: may[few][:k], 1 - few: rest[:k]}
+    else:
+        k = len(may[few]) // 2
+        use = {few: may[few][:k], 1 - few: may[few][k:2 * k]}
+    return to, [use[0], use[1]]
 
 
 def make_ops(core, T, topo):
     ops = []
-    lastw, readers, bank = {}, {}, {}
-    cur = [""]
+    lastw, readers, bank, seen = {}, {}, {}, {}
+    cur = ["", -1]
 
     def op(q, cost, reads, writes, fn, banks=(), sem=None, cnt=0, sched=(), tag=""):
-        o = {"i": len(ops), "q": q, "c": cost, "fn": fn, "wait": set(), "order": set(sched), "sem": sem, "tag": tag + cur[0], "n": cnt}
+        o = {"i": len(ops), "q": q, "c": cost, "fn": fn, "hard": set(), "soft": set(), "order": set(sched), "sem": sem,
+             "tag": tag + cur[0], "n": cnt, "b": cur[0], "t": cur[1]}
+        seen[o["tag"], cur[1]] = seen.get((o["tag"], cur[1]), 0) + 1
+        o["kind"] = (o["tag"], seen[o["tag"], cur[1]])
         for k in reads:
-            if k in lastw: o["wait"].add(lastw[k])
+            if k in lastw: o["hard"].add(lastw[k])
         for k in writes:
-            if k in lastw: o["wait"].add(lastw[k])
-            for r in readers.get(k, ()):
-                if ops[r]["q"] == q and q not in DMAS: o["order"].add(r)
-                else: o["wait"].add(r)
+            if k in lastw: o["hard"].add(lastw[k])
+            o["soft"].update(readers.get(k, ()))
         for k in banks:
-            if k in bank:
-                r = bank[k]
-                (o["order"] if ops[r]["q"] == q else o["wait"]).add(r)
+            if k in bank: o["soft"].add(bank[k])
             bank[k] = o["i"]
         for k in reads: readers.setdefault(k, []).append(o["i"])
         for k in writes:
             lastw[k] = o["i"]; readers[k] = []
-        o["wait"].discard(o["i"]); o["order"].discard(o["i"])
+        o["hard"].discard(o["i"]); o["soft"].discard(o["i"])
         ops.append(o)
         return o["i"]
 
@@ -101,302 +135,332 @@ def make_ops(core, T, topo):
         return op("V", vcost(n, f), reads, writes, fn, banks, tag=tag)
 
     def C(n, reads, writes, fn, banks=(), tag=""):
-        return op("A", AFIX + max(64, n) * CY, reads, writes, fn, banks, tag=tag)
+        return op("A", acost(n), reads, writes, fn, banks, tag=tag)
 
-    def P(cyc, reads, fn, banks, tag=""):
-        return op("T", 0.01 + cyc * PEC, reads, (), fn, banks, tag=tag)
+    def either(q, reads, writes, onv, ona, banks=(), tag=""):
+        i = op(q, None, reads, writes, None, banks, tag=tag)
+        ops[i]["alt"] = {"V": onv, "A": ona}
+        choose(ops, i, q)
+        return i
+
+    def P(cyc, reads, fn, banks, tag="", writes=()):
+        return op("T", 0.01 + cyc * PEC, reads, writes, fn, banks, tag=tag)
 
     def Gc(n, reads, writes, fn, tag=""):
         return op("G", 0.17 + 2 * n * CY, reads, writes, fn, tag=tag)
 
-    def DMA(q, cost, reads, writes, out, in_, sem, tag=""):
-        return op(q, cost, reads, writes, lambda e: e.dma_start(out, in_), sem=sem, tag=tag)
+    def moves(i, kb):
+        ops[i]["kb"] = kb
+        return i
+
+    def DMA(q, kb, reads, writes, out, in_, sem, tag=""):
+        return moves(op(q, DMA0, reads, writes, lambda e: [e.dma_start(out, in_)], sem=sem, cnt=1, tag=tag), kb)
+
+    def times(n, reads, write, out, src, scale=1.0, bias=0.0):
+        return either("A", reads, (write,), (vcost(n, .75), lambda e: e.tensor_scalar(out, src, scale, bias, A.mult, A.add)),
+                      (acost(n), lambda e: e.activation(out, src, F.Copy if isinstance(scale, float) else F.Identity, bias=bias, scale=scale)))
 
     def gather(q, n, reads, writes, out, src, scale=None, tag=""):
-        if q == "A":
-            fn = (lambda e: e.activation(out, src, F.Copy)) if scale is None else (lambda e: e.activation(out, src, F.Copy, scale=scale))
-        else:
-            fn = (lambda e: e.tensor_copy(out, src)) if scale is None else (lambda e: e.tensor_scalar(out, src, scale, None, A.mult))
-        return op(q, gcost(n), reads, writes, fn, tag=tag)
+        ona = (lambda e: e.activation(out, src, F.Copy)) if scale is None else (lambda e: e.activation(out, src, F.Copy, scale=scale))
+        onv = (lambda e: e.tensor_copy(out, src)) if scale is None else (lambda e: e.tensor_scalar(out, src, scale, None, A.mult))
+        return either(q, reads, writes, (gcost(n), onv), (gcost(n) + 0.02, ona), tag=tag)
 
-    rank = T.rank_of(core)
-    ncore = len(T.cores)
-    peer = {"A": (T.cores[(rank + 1) % ncore], T.cores[(rank - 1) % ncore]),
-            "B": (T.cores[(rank - 1) % ncore], T.cores[(rank + 1) % ncore])}
+    rank, ncore = T.rank_of(core), len(T.cores)
+    arrive = len(lanes(T, topo, T.cores[(rank - 1) % ncore])[1][0]) + len(lanes(T, topo, T.cores[(rank + 1) % ncore])[1][1])
+    half = (slice(0, 64), slice(64, 128))
+    own = {"A": half[0], "B": half[1]}
+    wins = {b: names("win" + b, 0, 16) for b in SETS}
+    xs = {b: names("X" + b, 0, 2 * PARTS) for b in SETS}
 
-    def lanes(s, d):
-        return topo.engines(s, d)[:8]
+    def lists(t, b, j0=0, j1=4, n="lu"):
+        return T[n + b][:, t * 128 + 32 * j0:t * 128 + 32 * j1]
 
-    half = {"A": slice(0, 128), "B": slice(128, 256)}
-    wins = {b: names("win" + b, 0, 16) for b in "AB"}
+    def tubes(h, k):
+        return slice(128 * k + 64 * h, 128 * k + 64 * h + 64)
 
-    def lists(t, b, j0=0, j1=4):
-        c = t * 256 + half[b].start
-        return T.lu[:, c + 32 * j0:c + 32 * j1]
-
-    small = [DMA("S", 2.0, (), ("tub",), T.tub[:], T.tube[:], "ltub"), DMA("AD", 2.0, (), ("wi",), T.wi[:], T.wt[:], "lwt"),
-             DMA("AD", 2.0, (), ("kni",), T.kni[:], T.kn[:], "lkn"), DMA("S", 2.0, (), ("limi",), T.limi[:], T.lim[:], "llim")]
-    DMA("S", 11.0, (), ("X",), T.X[:], T.field[:], "lX")
+    small = [DMA("S", 128, (), ("tub",), T.tub[:], T.tube[:], "ltub"), DMA("AD", 32, (), ("wi",), T.prm[:, 0:1], T.wt[:], "lwt"),
+             DMA("AD", 32, (), ("kni",), T.prm[:, 1:2], T.kn[:], "lkn"), DMA("AD", 32, (), ("limi",), T.prm[:, 4:8], T.lim[:], "llim")]
+    w = 8192 // PARTS
+    for b in SETS:
+        for k in range(PARTS):
+            for h in (0, 1) if DUP[b][k] == "D" else (0,):
+                small.append(DMA("S", 1024 // PARTS, (), (xs[b][2 * k + h],), T["X" + b][half[(k + h) & 1], k * w:k * w + w],
+                                 T.field[own[b], k * w:k * w + w], "x%d%s" % (2 * k + h, b), tag="ld" + b))
     for i in small: ops[i]["first"] = True
+    for b in SETS:
+        for k in range(PARTS):
+            dst, src = T["X" + b][half[1 - (k & 1)], k * w:k * w + w], T["X" + b][half[k & 1], k * w:k * w + w]
+            if DUP[b][k] != "D":
+                either(DUP[b][k], (xs[b][2 * k],), (xs[b][2 * k + 1],), (vcost(w, .5), lambda e, dst=dst, src=src: e.tensor_copy(dst, src)),
+                       (acost(w), lambda e, dst=dst, src=src: e.activation(dst, src, F.Copy)), tag="dup" + b)
     ON, col, cr = T.ones, T.cols, T.cr
     V(256, .5, (), ("ones",), lambda e: e.memset(ON[:], 1.0))
     Gc(128, ("ones",), ("Bd0",), lambda e: e.affine_select(T.Bd[:], ON[:, 0:128], [[-16, 8], [0, 16]], A.is_ge, 0.0, 0, 1))
     Gc(128, ("Bd0",), ("Bd",), lambda e: e.affine_select(T.Bd[:], T.Bd[:], [[16, 8], [0, 16]], A.is_ge, 0.0, 15, -1))
     Gc(128, ("ones",), ("Id",), lambda e: e.affine_select(T.Id[:], ON[:, 0:128], [[-1, 128]], A.is_equal, 0.0, 0, 1))
-    Gc(8, ("ones",), ("z8",), lambda e: e.affine_select(T.z8[:, 0:8], ON[:, 0:8], [[-16, 8]], A.is_equal, 0.0, 0, 1))
-    Gc(8, ("ones",), ("z15",), lambda e: e.affine_select(T.z8[:, 8:16], ON[:, 0:8], [[-16, 8]], A.is_equal, 0.0, -15, 1))
+    Gc(128, ("ones",), ("Sw",), lambda e: e.affine_select(T.Sw[:], ON[:, 0:128], [[64, 2], [-1, 64]], A.is_equal, 0.0, -64, 1))
     Gc(144, ("ones",), ("E0",), lambda e: e.affine_select(T.E[:], ON[:, 0:144], [[0, 9], [1, 16]], A.is_equal, 0.0, -15, 0))
     Gc(144, ("E0",), ("E1",), lambda e: e.affine_select(T.E[:], T.E[:], [[-16, 9], [0, 16]], A.is_ge, 0.0, 0, 1))
     Gc(144, ("E1",), ("E",), lambda e: e.affine_select(T.E[:], T.E[:], [[16, 9], [0, 16]], A.is_ge, 0.0, 15, -1))
-    Gc(128, ("ones",), ("R16",), lambda e: e.affine_select(T.R16[:], ON[:, 0:128], [[0, 8], [1, 16]], A.is_equal, 0.0, 0, -1))
-    V(128, .5, (), ("kl0",), lambda e: e.memset(T.kl[0:2, :], 1.0))
-    Gc(128, ("kl0",), ("kl",), lambda e: e.iota(T.kl[0:1, :], [[16, 128]], 0, 0, allow_small_or_imprecise_dtypes=True))
-    Gc(128, (), ("kr0",), lambda e: e.iota(T.kr[0:2, :], [[0, 8], [1, 16]], 0, 0, allow_small_or_imprecise_dtypes=True))
-    V(128, .5, ("kr0",), ("kr",), lambda e: e.memset(T.kr[0:1, :], 1.0))
-    Gc(48, (), ("pi",), lambda e: e.iota(T.pi[:], [[0, 48]], 0, 1))
-    for c, n, step, base in ((0, 8, 256, 0), (8, 8, 16, 0), (16, 8, 256, 0), (24, 8, 16, 128), (32, 16, 512, 0), (48, 8, 16, 15)):
-        Gc(n, (), ("cvb%d" % c,), lambda e, c=c, n=n, step=step, base=base: e.iota(T.cvb[:, c:c + n], [[step, n]], base, 0))
-    V(2048, .5, (), ("Exp0",), lambda e: e.memset(T.Exp[:], 1.0))
-    Gc(2048, ("Exp0",), ("Exp",), lambda e: e.affine_select(T.Exp[:], T.Exp[:], [[-1, 128], [0, 16]], A.is_equal, 0.0, 0, 1))
-    V(256, 1, ("tub",), ("lu0A", "lu0B"), lambda e: e.tensor_copy(T.lu[:, 0:256], T.tub[:]))
-    V(2048, .5, (), names("HA", 0, 4), lambda e: e.memset(T.HA[:], 0.0))
-    for c, b in ((0, "A"), (2048, "B")):
-        C(2048, names("HA", 0, 4), wins[b], lambda e, c=c: e.activation(T.win[:, c:c + 2048], T.HA[:], F.Copy))
-    V(8, 1, ("z8",), ("c0",), lambda e: e.tensor_reduce(col[:, 0:1], T.z8[:, 0:8], AxisListType.X, A.add))
-    V(8, 1, ("z15",), ("c2",), lambda e: e.tensor_reduce(col[:, 2:3], T.z8[:, 8:16], AxisListType.X, A.add, negate=True))
-    V(1, 1, ("c0",), ("c1",), lambda e: e.tensor_scalar(col[:, 1:2], col[:, 0:1], -1.0, 1.0, A.mult, A.add))
-    V(1, 1, ("wi",), ("c4",), lambda e: e.tensor_copy(col[:, 4:5], T.wi[:]))
-    V(1, 1, ("kni",), ("c5",), lambda e: e.tensor_scalar(col[:, 5:6], T.kni[:], 8.0, None, A.mult))
-    V(1, 1, ("c5",), ("c6",), lambda e: e.tensor_scalar(col[:, 6:7], col[:, 5:6], col[:, 5:6], -1.0, A.mult, A.mult))
-    V(1, 1, ("c5",), ("c8",), lambda e: e.tensor_scalar(col[:, 8:9], col[:, 5:6], 2047.5, None, A.add))
-    V(4, 1, ("limi",), ("limf",), lambda e: e.tensor_copy(T.limf[:, 0:4], T.limi[:]))
-    V(4, 1, ("limi",), ("limg",), lambda e: e.tensor_scalar(T.limf[:, 4:8], T.limi[:], 3.5, None, A.add))
-    V(1, 1, ("limf",), ("thr",), lambda e: e.tensor_copy(col[:, 7:8], T.limf[:, 0:1]))
-    sigmoid = "A" in CPQ["A"] + CPQ["B"]
-
-    def nthr():
-        if sigmoid: C(1, ("thr",), ("nthr",), lambda e: e.activation(col[:, 9:10], col[:, 7:8], F.Copy, bias=128.0, scale=-256.0), tag="e5")
-    nthr()
-    if sigmoid or "A" in OPQ["A"][0] + OPQ["B"][0]:
-        C(1400, ("ones",), ("ej",), lambda e: e.activation(T.ej[:], ON[:, 0:128], F.Sigmoid))
-    V(128, .5, ("Id",), ("Im",), lambda e: e.tensor_scalar(T.Im[:], T.Id[:], -1.0, None, A.mult))
-    every = SUMS["A"] + SUMS["B"] != "AA"
+    Gc(128, (), ("kr",), lambda e: e.iota(T.kr[:], [[0, 8], [1, 16]], 0, 0, allow_small_or_imprecise_dtypes=True))
+    Gc(32, (), ("pi",), lambda e: e.iota(T.pi[:], [[0, 32]], 0, 1))
+    for c, pat in ((0, [[256, 8]]), (8, [[16, 8]]), (16, [[128, 2], [16, 4]]), (24, [[1, 8]])):
+        Gc(8, (), ("cv%d" % c,), lambda e, c=c, pat=pat: e.iota(T.cv[:, c:c + 8], pat, 0, 0))
+    ops[V(2048, .5, (), names("HB", 0, 4), lambda e: e.memset(T.HB[:], 0.0))]["soon"] = True
+    Gc(2048, names("HB", 0, 4), ("Exp",), lambda e: e.affine_select(T.Exp[:], T.HB[:], [[-1, 128], [0, 16]], A.not_equal, 1.0, 0, 1))
+    for b in SETS:
+        for h in (0, 1):
+            for k in (0, 1):
+                V(64, 1, ("tub",), ("lu0%s%d" % (b, 2 * h + k),),
+                  lambda e, b=b, h=h, k=k: e.tensor_copy(T["lu" + b][half[h], 64 * k:64 * k + 64], T.tub[own[b], tubes(h, k)]))
+    if "D" in ZERO["A"] + ZERO["B"]: V(128, 1, (), ("usB",), lambda e: e.memset(T.usB[:], 0.0))
+    for b in SETS:
+        if ZERO[b] == "A":
+            ops[C(2048, names("HB", 0, 4), wins[b], lambda e, b=b: e.activation(T["win" + b][:], T.HB[:], F.Copy), tag="wz" + b)]["soon"] = True
+        if ZERO[b] == "G":
+            Gc(2048, (), wins[b], lambda e, b=b: e.iota(T["win" + b][:], [[0, 2048]], 0, 0, allow_small_or_imprecise_dtypes=True), tag="wz" + b)
+        Gc(2048, (), ("cw" + b,), lambda e, b=b: e.iota(T["cw" + b][:], [[0, 2048]], 0, 0))
+    V(16, 1, ("pi",), ("pi0",), lambda e: e.tensor_scalar(T.pi[:, 0:16], T.pi[:, 0:16], 15, None, A.bitwise_and))
+    V(8, 1, ("pi",), ("pi16",), lambda e: e.tensor_scalar(T.pi[:, 16:24], T.pi[:, 16:24], 79, None, A.bitwise_and))
+    V(1, 1, ("pi0",), ("c0",), lambda e: e.tensor_copy(col[:, 0:1], T.pi[:, 0:1]))
+    V(1, 1, ("c0",), ("c1",), lambda e: e.tensor_scalar(col[:, 1:2], col[:, 0:1], 0.0, None, A.is_gt))
+    V(1, 1, ("c0",), ("l15",), lambda e: e.tensor_scalar(T.l15[:, 0:1], col[:, 0:1], 15.0, None, A.is_equal))
+    V(128, .5, ("c0", "kr"), ("mask",), lambda e: e.tensor_scalar(T.mask[:], T.kr[:], col[:, 0:1], None, A.is_equal))
+    V(8, 1, ("pi0", "c0"), ("pj",), lambda e: e.tensor_scalar(T.pi[:, 0:8], T.pi[:, 0:8], 16.0, None, A.mult))
+    V(24, 2, ("pj", "pi0", "pi16", "cv0", "cv8", "cv16"), ("cv",), lambda e: e.tensor_tensor(T.cv[:, 0:24], T.cv[:, 0:24], T.pi[:, 0:24], A.add))
+    V(16, 1, ("cv",), ("CV",), lambda e: e.tensor_copy(T.CV[:, 0:16], T.cv[:, 0:16]))
+    V(8, 1, ("cv",), ("vtW",), lambda e: e.tensor_scalar(T.vt[:, 0:8], T.cv[:, 16:24], -63.5, None, A.add))
+    times(8, ("vtW",), "V0", T.CV[:, 16:24], T.vt[:, 0:8], 32.0, 2032.0)
+    for h in (0, 1): times(8, ("V0",), "V%d" % (h + 1), T.CV[half[h], 24:32], T.CV[half[1 - h], 16:24])
+    V(8, 1, ("cv24",), ("cidx",), lambda e: e.tensor_copy(T.cidx[:], T.cv[:, 24:32]))
+    pf = T.prf
+    V(1, 1, ("wi",), ("prf0",), lambda e: e.tensor_scalar(pf[:, 0:1], T.prm[:, 0:1], 1.0 / 4096, None, A.mult))
+    times(1, ("prf0",), "prf1", pf[:, 1:2], pf[:, 0:1], 128.0)
+    V(1, 1, ("kni",), ("prf2",), lambda e: e.tensor_scalar(pf[:, 2:3], T.prm[:, 1:2], 8.0, 2047.5, A.mult, A.add))
+    V(1, 2, ("kni",), ("kk",), lambda e: e.tensor_tensor(col[:, 2:3], T.prm[:, 1:2], T.prm[:, 1:2], A.mult))
+    times(1, ("kk",), "prf3", pf[:, 3:4], col[:, 2:3], -64.0)
+    V(4, 1, ("limi",), ("prf4",), lambda e: e.tensor_scalar(pf[:, 4:8], T.prm[:, 4:8], 256.0, 768.0, A.mult, A.add))
+    for n, b in enumerate(SETS):
+        cb = T["col" + b]
+        for h in (0, 1):
+            times(4, names("prf", 0, 4), "col%s%d" % (b, h), cb[half[h], 0:4], pf[own[b], 0:4])
+            times(4, ("prf4",), "cst%s%d" % (b, h), T.cst[half[h], n:8:2], pf[own[b], 4:8])
+        both = names("col" + b, 0, 2)
+        wE = T["wE" + b]
+        if SUMS[b] == "W":
+            times(144, both + ["E"], "wE" + b, wE[:, 0:144], T.E[:], cb[:, 0:1])
+        else:
+            times(1, both, "col2" + b, cb[:, 4:5], cb[:, 2:3], 1.0, -2047.5)
+            times(128, both + ["Bd"], "wq" + b, wE[:, 128:256], T.Bd[:], cb[:, 0:1])
+            times(128, ["wq" + b], "wn" + b, wE[:, 0:128], wE[:, 128:256], -1.0)
+            times(128, ["wq" + b], "wr" + b, wE[:, 256:384], wE[:, 128:256], -128.0)
+            times(128, ["wq" + b], "ws" + b, wE[:, 384:512], wE[:, 128:256], 128.0)
+    csts = ("cstA0", "cstA1", "cstB0", "cstB1")
+    times(2, csts, "nb0", T.nb[:, 0:2], T.cst[:, 0:2], 1.0, -896.0)
+    ops[C(1600, ("ones",), ("ej",), lambda e: e.activation(T.ej[:], ON[:, 0:128], F.Sigmoid))]["soon"] = True
+    for name, n, out, src, need, k in (("Im", 128, T.Im[:], T.Id[:], "Id", -1.0), ("pE", 144, T.pE[:], T.E[:], "E", 16384.0),
+                                       ("neg", 128, T.neg[:], ON[:, 0:128], "ones", -256.0), ("Bd32", 128, T.Bd32[:], T.Bd[:], "Bd", 1.0),
+                                       ("Bd128", 128, T.Bd128[:], T.Bd[:], "Bd", 128.0), ("I32", 128, T.I32[:], T.Id[:], "Id", 32.0),
+                                       ("S32", 128, T.S32[:], T.Sw[:], "Sw", 32.0), ("K8a", 8, T.K8[:, 0:8], T.Bd[:, 0:128:16], "Bd", 64.0),
+                                       ("K8b", 8, T.K8[:, 8:16], T.Bd[:, 0:128:16], "Bd", -32.0), ("sela", 8, T.sel[:, 0:8], T.Bd[:, 0:128:16], "Bd", 1.0),
+                                       ("selb", 8, T.sel[:, 8:16], T.Bd[:, 0:128:16], "Bd", 128.0),
+                                       ("selc", 8, T.sel[:, 16:24], T.Bd[:, 0:128:16], "Bd", 32.0)):
+        times(n, (need,), name, out, src, k)
+    times(128, ("Bd", "c1"), "Bn", T.Bn[:], T.Bd[:], col[:, 1:2])
+    V(512, .5, (), ("R0",), lambda e: e.memset(T.R[:], 0.0))
+    V(64, .5, ("R0",), ("R",), lambda e: e.memset(T.R[:, 0:512:16], 255.0))
     if "W" in SUMS["A"] + SUMS["B"]:
-        V(144, .5, ("E", "c4"), ("wQ",), lambda e: e.tensor_scalar(T.wQ[:], T.E[:], col[:, 4:5], 1.0 / 4096, A.mult, A.mult))
         Gc(128, ("Bd",), ("Dm0",), lambda e: e.affine_select(T.Dm[:], T.Bd[:], [[-1, 128]], A.is_equal, 0.0, 1, 1))
-        V(128, 2, ("Dm0", "Id"), ("Dm1",), lambda e: e.tensor_tensor(T.Dm[:], T.Dm[:], T.Id[:], A.subtract))
-        V(128, .5, ("Dm1",), ("Dm",), lambda e: e.tensor_scalar(T.Dm[:], T.Dm[:], 4096.0, None, A.mult))
-    if every:
-        V(1, 1, (), ("E20",), lambda e: e.memset(T.E2[:, 0:1], 0.0))
-        V(143, 2, ("E",), ("E21",), lambda e: e.tensor_tensor(T.E2[:, 1:144], T.E[:, 1:144], T.E[:, 0:143], A.subtract))
-        V(144, .5, ("E", "c4"), ("wE",), lambda e: e.tensor_scalar(T.wE[:], T.E[:], col[:, 4:5], None, A.mult))
-        V(144, .5, ("E20", "E21", "c4"), ("wD",), lambda e: e.tensor_scalar(T.wD[:], T.E2[:], col[:, 4:5], None, A.mult))
-        V(128, 1, ("Bd",), ("Bq32",), lambda e: e.tensor_scalar(T.Bq32[:], T.Bd[:], 1.0 / 4096, None, A.mult))
-    V(128, .5, ("Bd", "c4"), ("wq",), lambda e: e.tensor_scalar(T.wq[:], T.Bd[:], col[:, 4:5], 1.0 / 4096, A.mult, A.mult))
-    V(128, .5, ("Bd", "c4"), ("wB",), lambda e: e.tensor_scalar(T.wB[:], T.Bd[:], col[:, 4:5], None, A.mult))
-    V(144, .5, ("E",), ("nE",), lambda e: e.tensor_scalar(T.nE[:], T.E[:], -16384.0, None, A.mult))
-    V(144, 1, ("E",), ("E32",), lambda e: e.tensor_copy(T.E32[:], T.E[:]))
-    V(2048, .5, (), ("R0",), lambda e: e.memset(T.R[:], 0.0))
-    V(128, .5, ("R0",), ("R",), lambda e: e.memset(T.R[:, 0:2048:16], 255.0))
-    V(128, .5, ("Bd", "c1"), ("Bn",), lambda e: e.tensor_scalar(T.Bn[:], T.Bd[:], col[:, 1:2], None, A.mult))
-    V(128, 1, ("Bd",), ("Bd32",), lambda e: e.tensor_copy(T.Bd32[:], T.Bd[:]))
-    V(128, .5, ("ones", "c2"), ("Qe",), lambda e: e.tensor_scalar(T.Qe[:], ON[:, 0:128], col[:, 2:3], None, A.mult))
-    V(128, .5, ("Id",), ("Ih",), lambda e: e.tensor_scalar(T.Ih[:], T.Id[:], 0.5, None, A.mult))
-    V(128, 1, ("Id",), ("I32n",), lambda e: e.tensor_scalar(T.I32n[:], T.Id[:], -32.0, None, A.mult))
-    V(8, 1, ("Bd",), ("sel32a",), lambda e: e.tensor_scalar(T.sel32[:, 0:8], T.Bd[:, 0:128:16], 1.0 / 32, None, A.mult))
-    V(8, 1, ("Bd",), ("sel32b",), lambda e: e.tensor_copy(T.sel32[:, 8:16], T.Bd[:, 0:128:16]))
-    V(128, 1, ("Id",), ("I32",), lambda e: e.tensor_copy(T.I32[:], T.Id[:]))
-    P(128, ("R16",), lambda e: e.matmul(T.z0[:, 0:128], T.R16[:], T.R16[:], True, True), ("z0",))
-    V(128, 1, (), ("mask",), lambda e: e.tensor_copy(T.mask[:], T.z0[:, 0:128]), ("z0",))
-    V(8, 1, ("Bd",), ("K8a",), lambda e: e.tensor_scalar(T.K8[:, 0:8], T.Bd[:, 0:128:16], 8192.0, None, A.mult))
-    V(8, 1, ("Bd",), ("K8b",), lambda e: e.tensor_scalar(T.K8[:, 8:16], T.Bd[:, 0:128:16], -4096.0, None, A.mult))
-    V(8, 1, ("Bd",), ("sela",), lambda e: e.tensor_copy(T.sel[:, 0:8], T.Bd[:, 0:128:16]))
-    V(8, 1, ("Bd",), ("selb",), lambda e: e.tensor_scalar(T.sel[:, 8:16], T.Bd[:, 0:128:16], 128.0, None, A.mult))
+        V(128, 2, ("Dm0", "Id"), ("Dm",), lambda e: e.tensor_tensor(T.Dm[:], T.Id[:], T.Dm[:], A.subtract))
     V(128, 1, (), ("Rk0",), lambda e: e.memset(T.Rk[:], -33554432.0))
     V(8, 1, ("Rk0",), ("Rk",), lambda e: e.memset(T.Rk[:, 0:128:16], 33554432.0))
-    V(128, .5, (), ("cr0",), lambda e: e.memset(cr[0:2, 0:128], 0.0))
-    V(8, .5, ("cr0",), ("cr1",), lambda e: e.memset(cr[0:2, 0:128:16], 0.5))
-    V(8, .5, ("cr1",), ("crS",), lambda e: e.memset(cr[0:1, 0:128:16], -2048.0))
-    V(128, .5, (), ("cr2",), lambda e: e.memset(cr[0:1, 128:256], 90112.0))
+    V(128, .5, (), ("crE",), lambda e: e.memset(cr[0:1, 0:128], -896.0))
+    V(128, .5, (), ("cr2",), lambda e: e.memset(cr[0:1, 128:256], -172032.0))
     V(8, .5, ("cr2",), ("crX",), lambda e: e.memset(cr[0:1, 128:256:16], -1048576.0))
     V(128, .5, (), ("cr3",), lambda e: e.memset(cr[0:2, 256:384], 1.0 / 8192))
     V(128, .5, ("cr3",), ("crQ",), lambda e: e.memset(cr[0:1, 256:384], -0.5))
-    V(48, 1, ("pi",), ("pi2",), lambda e: e.tensor_scalar(T.pi[:], T.pi[:], 15, None, A.bitwise_and))
-    for c, n, k in ((0, 8, 16), (16, 8, 16), (32, 16, 32)):
-        V(n, 1, ("pi2",), ("pj%d" % c,), lambda e, c=c, n=n, k=k: e.tensor_scalar(T.pi[:, c:c + n], T.pi[:, c:c + n], k, None, A.mult))
-    V(48, 2, ("pj0", "pj16", "pj32", "cvb0", "cvb8", "cvb16", "cvb24", "cvb32"), ("cv",),
-      lambda e: e.tensor_tensor(T.cv[:], T.pi[:], T.cvb[:, 0:48], A.add))
-    V(48, 1, ("cv",), ("CV",), lambda e: e.tensor_copy(T.CV[:, 0:48], T.cv[:]))
-    for b in "AB":
-        c = 48 if b == "A" else 56
-        V(8, 1, (), ("CW" + b,), lambda e, b=b, c=c: e.memset(T.CV[:, c:c + 8], 63.5 if SUMS[b] != "A" else -15.5 / 32))
-    V(8, 1, ("cvb48",), ("cidx",), lambda e: e.tensor_copy(T.cidx[:], T.cvb[:, 48:56]))
+    times(128, ("crQ",), "crP", cr[0:2, 640:768], cr[0:2, 256:384], -1.0)
+    V(128, .5, (), ("crM",), lambda e: e.memset(cr[0:1, 384:512], MAGIC))
+    V(128, .5, (), ("crN",), lambda e: e.memset(cr[0:1, 512:640], -MAGIC))
+    V(128, .5, (), ("cr4",), lambda e: e.memset(cr[0:2, 768:896], -1.0 / 64))
+    V(128, .5, ("cr4",), ("crR",), lambda e: e.memset(cr[0:1, 768:896], 0.5))
 
     pend = {}
 
-    def window(t):
-        for b in "AB":
-            if t: op("R", FLY, (), ("lu%d%s" % (t, b),), None, sem="au%d%s" % (t, b), cnt=len(lanes(peer[b][1], core)), sched=(pend[b],))
-            V(128, 1, ("lu%d%s" % (t, b),), ("lf" + b,), lambda e, b=b: e.tensor_copy(T.lf[:, half[b]], lists(t, b)), tag="lf" + b)
-            DMA("S", 2.0, ("lf" + b,), ("rows" + b,), T["rows" + b][:], T.lf[:, half[b]], "r%d%s" % (t, b), tag="D1" + b)
-            c = 16 * half[b].start
-            for j in range(1, 16):
-                DMA("S", WIN, ("rows" + b,), (wins[b][j],), T.win[j:128:16, c + 128 * j:c + 2048], T["rows" + b][:, 1:17 - j, :],
-                    "w%d%s" % (t, b), tag="Dj" + b)
+    def luk(t, b): return names("lu0" + b, 0, 4) if t == 0 else ["lu%d%s" % (t, b)]
+
+    def window(t, b):
+        lf = "lf%d%s" % (t, b)
+        if t: moves(op("R", FLY, (), luk(t, b), None, sem="au%d%s" % (t, b), cnt=arrive, sched=(pend[b],), tag="fly"), 64)
+        if t and not FOLD: moves(op("R", FLY, (), (lf,), None, sem="af%d%s" % (t, b), cnt=arrive, sched=(pend["f" + b],), tag="flyf"), 96)
+        else: V(128, 1, luk(t, b), (lf,), lambda e: e.tensor_copy(lists(t, b, n="lf"), lists(t, b)), tag="lf")
+        rows, win = T["rows" + b], T["win" + b]
+        if t == 0 and ZERO[b] == "D":
+            V(128, 1, luk(t, b) + ["c1"], ("nw" + b,), lambda e: e.tensor_scalar(T["nw" + b][:], lists(t, b), col[:, 1:2], None, A.mult), tag="lz")
+            moves(op("S", DMA0, ("nw" + b, "usB"), ("rows" + b,),
+                     lambda e: [e.dma_start(rows[:, 0:16, :], T.usB[:]), e.dma_start(rows[:, 16:32, :], T["nw" + b][:])], sem="r0" + b, cnt=2, tag="D1"), 160)
+            for j0 in range(0, 16, 4):
+                moves(op("S", DMA0, ("rows" + b,), wins[b][j0:j0 + 4],
+                         lambda e, j0=j0: [e.dma_start(win[j:128:16, :], rows[:, 17 - j:33 - j, :] if j else rows[:, 0:16, :]) for j in range(j0, j0 + 4)],
+                         sem="w0" + b, cnt=4, tag="Dz"), 280)
+            return
+        DMA("S", 80, [lf], ("rows" + b,), rows[:, 16:32, :], lists(t, b, n="lf"), "r%d%s" % (t, b), tag="D1")
+        for j0 in range(1, 16, 3):
+            moves(op("S", DMA0, ("rows" + b,), wins[b][j0:j0 + 3],
+                     lambda e, j0=j0: [e.dma_start(win[j:128:16, 128 * j:2048], rows[:, 17:33 - j, :]) for j in range(j0, j0 + 3)],
+                     sem="w%d%s" % (t, b), cnt=3, tag="Dj"), 24 + 12 * (15 - j0))
 
     def front(t, b):
         last = t == RO - 1
         b0, b1, b2 = "0" + b, "1" + b, "2" + b
         p0, p1, p2 = T["p0" + b], T["p1" + b], T["p2" + b]
-        luk = "lu%d%s" % (t, b)
-        q = {n: T[n + b] for n in ("G", "M", "H", "us", "Lp", "t32", "c32", "Wm", "Ws", "pass", "zo", "cu", "q", "Z", "Zt", "Zh", "cm", "Gm")}
-        G, M, H = q["G"], q["M"], q["H"]
-        Lp = q["Lp"][:]
-        allp, early = SUMS[b] != "A", SUMS[b] == "W"
-        if OPQ[b][3] == "A":
-            C(128, ("lf" + b, "c6"), ("Lp" + b,), lambda e: e.activation(Lp, T.lf[:, half[b]], F.Identity, bias=col[:, 6:7], scale=16.0), tag="Lp")
-        else:
-            V(128, 1, (luk, "c6"), ("Lp" + b,), lambda e: e.tensor_scalar(Lp, lists(t, b), 16.0, col[:, 6:7], A.mult, A.add), tag="Lp")
-        for who, j0, j1 in pieces(G1Q[b]):
-            gather(who, 512 * (j1 - j0), ("X", luk), names("G" + b, j0, j1), G[:, 512 * j0:512 * j1],
-                   T.X[:, 0:8192].indirect(lists(t, b, j0, j1)), tag="G1")
-        for who, j0, j1 in pieces(SCQ[b]):
-            f = slice(512 * j0, 512 * j1); n = 512 * (j1 - j0)
-            V(n, .5, names("G" + b, j0, j1) + ["R"], names("M" + b, j0, j1),
-              lambda e, f=f, n=n: e.tensor_tensor_scan(M[:, f], T.R[:, 0:n], G[:, f], 0.0, A.max, A.min), tag="SC")
-        for who, j0, j1 in pieces(CPQ[b]):
-            f = slice(512 * j0, 512 * j1); n = 512 * (j1 - j0)
-            if who == "V":
-                V(n, .5, names("M" + b, j0, j1) + ["thr"], names("H" + b, j0, j1),
-                  lambda e, f=f: e.tensor_scalar(H[:, f], M[:, f], col[:, 7:8], None, A.is_ge), tag="CP")
-            else:
-                C(n, names("M" + b, j0, j1) + ["nthr"], names("H" + b, j0, j1),
-                  lambda e, f=f: e.activation(H[:, f], M[:, f], F.Sigmoid, bias=col[:, 9:10], scale=256.0), tag="CP")
+        q = {n: T[n + b] for n in ("X", "G", "M", "H", "Lp", "t32", "c32", "Wm", "pass", "zo", "cu", "q", "Z", "Zt", "cm", "col",
+                                   "uf", "us", "Ws", "wE", "nw", "rq", "rd", "rp", "win", "cw", "nl", "Gy")}
+        G, M, H, cb = q["G"], q["M"], q["H"], q["col"]
+        Lp, Gm, cols = q["Lp"][:], q["Gy"][:, 128:256], names("col" + b, 0, 2) + ["col2" + b]
+        n, every, who = SETS.index(b), SUMS[b] == "W", OPQ[b]
+        nb = T.nb[:, 2 * t + n:2 * t + n + 1]
+        C(128, ["lf%d%s" % (t, b)] + cols, ("Lp" + b,), lambda e: e.activation(Lp, lists(t, b, n="lf"), F.Identity, bias=cb[:, 3:4], scale=16.0), tag="Lp")
+        for x, j0, j1 in pieces(G1Q[b]):
+            gather(x, 512 * (j1 - j0), xs[b] + luk(t, b), names("G" + b, j0, j1), G[:, 512 * j0:512 * j1],
+                   q["X"][:, 0:8192].indirect(lists(t, b, j0, j1)), tag="G1")
+        for x, j0, j1 in pieces(SCQ):
+            f = slice(512 * j0, 512 * j1); k = 512 * (j1 - j0)
+            V(k, .5, names("G" + b, j0, j1) + ["R"], names("M" + b, j0, j1),
+              lambda e, f=f, k=k: e.tensor_tensor_scan(M[:, f], T.R[:, 0:k], G[:, f], 0.0, A.max, A.min), tag="SC")
+        for x, j0, j1 in pieces(CPQ[b]):
+            f = slice(512 * j0, 512 * j1); k = 512 * (j1 - j0)
+            either(x, names("M" + b, j0, j1) + ["nb%d" % t, "ej"], names("H" + b, j0, j1),
+                   (vcost(k, .5), lambda e, f=f: e.tensor_scalar(H[:, f], M[:, f], 256.0, nb, A.mult, A.is_lt)),
+                   (acost(k), lambda e, f=f: e.activation(H[:, f], M[:, f], F.Sigmoid, bias=nb, scale=-256.0)), tag="CP")
+
+        def nearest():
+            V(128, 1, (), ("q" + b,), lambda e: e.tensor_scalar(q["q"][:], p1[:, 384:512], MAGIC, MAGIC, A.add, A.subtract), (b1,), tag="q")
         for h in (0, 1):
-            def sums(e, dst, row, ws, src, i0, c=0, whole=False, h=h):
-                o = slice(c + h * 64, c + h * 64 + 64)
-                if whole:
-                    if i0 == 0 and h == 0: e.matmul(dst[:, c:c + 128], row, ON[0:row.shape[0], 0:128], True, False)
-                elif i0 == 0: e.matmul(dst[:, o], row, ON[0:row.shape[0], 0:64], True, False)
+            def sums(e, dst, row, k, w, src, i0, h=h):
+                if i0 == 0: e.matmul(dst, row, ON[0:k, 0:64], True, False)
                 for i in range(i0, i0 + CHUNK):
-                    r = e.matmul(dst[:, o], ws[i][:, 15 - i:143 - i], src[:, h * 1024 + i:h * 1024 + 1024:16], False, i == 15 and not whole)
+                    r = e.matmul(dst, w[:, 15 - i:143 - i], src[:, h * 1024 + i:h * 1024 + 1024:16], False, i == 15)
                 return r
-            for i0 in range(0, 16 if early else 0, CHUNK):
-                P(68 * CHUNK, names("G" + b, 2 * h, 2 * h + 2) + ["wQ", "crQ", "ones"],
-                  lambda e, f=sums, i0=i0: f(e, p2, cr[0:2, 256:384], [T.wQ] * 16, G, i0, 384), (b2,), tag="xS")
-            for i0 in range(0, 16 if allp else 0, CHUNK):
-                P(68 * CHUNK, names("G" + b, 2 * h, 2 * h + 2) + ["wE", "wD", "crS", "ones"],
-                  lambda e, f=sums, i0=i0: f(e, p1, cr[0:2, 0:128], [T.wD] * 15 + [T.wE], G, i0, 0, early), (b1,), tag="dS")
-            if early and h:
-                V(128, 1, (), ("q" + b,), lambda e: e.tensor_scalar(q["q"][:], p2[:, 384:512], MAGIC, MAGIC, A.add, A.subtract), (b2,), tag="q")
-                P(128, ("q" + b, "Dm"), lambda e: e.matmul(p1[:, 0:128], T.Dm[:], q["q"][:], False, True), (b1,), tag="dq")
+            for i0 in range(0, 16 if every else 0, CHUNK):
+                P(68 * CHUNK, names("G" + b, 2 * h, 2 * h + 2) + ["wE" + b, "crQ", "ones"],
+                  lambda e, f=sums, i0=i0, h=h: f(e, p1[:, 384 + 64 * h:448 + 64 * h], cr[0:2, 256:384], 2, q["wE"], G, i0), (b1,), tag="xS")
+            if h and every:
+                nearest()
+                V(128, 1, ("q" + b,), ("uf" + b,), lambda e: e.tensor_tensor(q["uf"][:], p1[:, 384:512], q["q"][:], A.subtract), (b1,), tag="uf")
+                P(512, ("uf" + b, "Dm"), lambda e: e.matmul(p1[:, 0:128], T.Dm[:], q["uf"][:], True, True), (b1,), tag="dq")
             for i0 in range(0, 16, CHUNK):
-                P(68 * CHUNK, names("H" + b, 2 * h, 2 * h + 2) + ["nE", "crX", "ones"],
-                  lambda e, f=sums, i0=i0: f(e, p0, cr[0:1, 128:256], [T.nE] * 16, H, i0), (b0,), tag="cnt")
-        if OPQ[b][0] == "V":
-            V(128, 1, (), ("pass" + b,), lambda e: e.tensor_scalar(q["pass"][:], p0[:, 0:128], 0.0, None, A.is_lt), (b0,), tag="pass")
-        else:
-            C(128, (), ("pass" + b,), lambda e: e.activation(q["pass"][:], p0[:, 0:128], F.Sigmoid, scale=-1.0), (b0,), tag="pass")
+                P(68 * CHUNK, names("H" + b, 2 * h, 2 * h + 2) + ["pE", "crX", "ones"],
+                  lambda e, f=sums, i0=i0, h=h: f(e, p0[:, 64 * h:64 * h + 64], cr[0:1, 128:256], 1, T.pE, H, i0), (b0,), tag="cnt")
+        either(who[0], ("ej",), ("pass" + b,), (vcost(128), lambda e: e.tensor_scalar(q["pass"][:], p0[:, 0:128], 0.0, None, A.is_lt)),
+               (acost(128), lambda e: e.activation(q["pass"][:], p0[:, 0:128], F.Sigmoid, scale=-1.0)), (b0,), tag="pass")
         P(128, ("pass" + b, "Bn"), lambda e: e.matmul(p0[:, 128:256], q["pass"][:], T.Bn[:], True, True), (b0,), tag="mT")
         V(128, 1, ("mask",), ("Wm" + b,), lambda e: e.tensor_tensor(q["Wm"][:], p0[:, 128:256], T.mask[:], A.mult), (b0,), tag="Wm")
 
-        def mP(e, c=0):
-            e.matmul(p0[:, 384:400], T.Id[:], T.CV[:, c:c + 16], True, False)
-            return e.matmul(p0[:, 384:400], q["Wm"][:], T.sel[:], False, True)
+        def mP(e):
+            e.matmul(p0[:, 384:400], T.Id[:], T.CV[:, 0:16], True, False)
+            return e.matmul(p0[:, 384:400], q["Wm"][:], T.sel[:, 0:16], False, True)
         P(128, ("Wm" + b, "Id", "CV", "sela", "selb"), mP, (b0,), tag="mP")
         V(16, 1, (), ("zo" + b,), lambda e: e.tensor_copy(q["zo"][:], p0[:, 384:400]), (b0,), tag="zo")
-        if allp:
+        if every:
             V(128, 1, ("pass" + b,), ("us" + b,), lambda e: e.tensor_tensor(q["us"][:], q["pass"][:], p1[:, 0:128], A.mult), (b1,), tag="us")
-            if not early: P(512, ("us" + b, "Bq32"), lambda e: e.matmul(p1[:, 384:512], T.Bq32[:], q["us"][:], True, True), (b1,), tag="x")
-            P(512, ("us" + b, "Bq32"), lambda e: e.matmul(p2[:, 128:256], T.Bq32[:], q["us"][:], True, early), (b2,), tag="u1")
+            P(512, ("us" + b, "Bd32"), lambda e: e.matmul(p2[:, 128:256], T.Bd32[:], q["us"][:], True, True), (b2,), tag="u1")
         else:
-            gather(OPQ[b][4], 128, ["zo" + b] + names("G" + b, 0, 4), ("Gm" + b,), q["Gm"][:], G[:, 0:2048].indirect(q["zo"][:, 0:8]), tag="Gm")
-            for dst, bk, stop in ((p1[:, 384:512], b1, True), (p2[:, 128:256], b2, False)):
-                P(128, ("crQ", "ones"), lambda e, dst=dst: e.matmul(dst, cr[0:2, 256:384], ON[0:2, 0:128], True, False), (bk,), tag="x0")
-                P(128, ("Gm" + b, "wq"), lambda e, dst=dst, stop=stop: e.matmul(dst, T.wq[:], q["Gm"][:], False, stop), (bk,), tag="x")
-        if not early:
-            V(128, 1, (), ("q" + b,), lambda e: e.tensor_scalar(q["q"][:], p1[:, 384:512], MAGIC, MAGIC, A.add, A.subtract), (b1,), tag="q")
-            P(128, ("q" + b, "Im"), lambda e: e.matmul(p2[:, 128:256], T.Im[:], q["q"][:], False, True), (b2,), tag="u2")
-        C(128, ("c8",), (), lambda e: e.activation(p2[:, 256:384], p2[:, 128:256], F.Square, bias=col[:, 8:9], scale=4096.0), (b2,), tag="Sq")
-        gather(OPQ[b][1], 128, ["zo" + b] + names("M" + b, 0, 4), ("Z" + b,), q["Z"][:], M[:, 0:2048].indirect(q["zo"][:, 0:8]), tag="Z")
+            gather(who[5], 128, ["zo" + b] + names("G" + b, 0, 4), ("Gm" + b,), Gm, G[:, 0:2048].indirect(q["zo"][:, 0:8]), tag="Gm")
+            dst = p2[:, 128:256]
+            P(128, ("crP", "ones"), lambda e: e.matmul(dst, cr[0:2, 640:768], ON[0:2, 0:128], True, False), (b2,), tag="x0")
+
+            def mod(e):
+                e.matmul(dst, q["wE"][:, 0:128], Gm, False, False)
+                e.matmul(dst, cr[0:1, 384:512], ON[0:1, 0:128], False, False)
+                e.matmul(dst, cr[0:1, 512:640], ON[0:1, 0:128], False, False)
+                return e.matmul(dst, q["wE"][:, 128:256], Gm, False, True)
+            P(512, ("Gm" + b, "wq" + b, "wn" + b, "crM", "crN"), mod, (b2,), tag="x")
+        C(128, cols, (), lambda e: e.activation(p2[:, 256:384], p2[:, 128:256], F.Square, bias=cb[:, 2:3] if every else cb[:, 4:5], scale=4096.0), (b2,), tag="Sq")
+        gather(who[1], 128, ["zo" + b] + names("M" + b, 0, 4), ("Z" + b,), q["Z"][:], M[:, 0:2048].indirect(q["zo"][:, 0:8]), 0.5, tag="Z")
         V(128, 1, ("Lp" + b,), ("t32" + b,), lambda e: e.tensor_tensor(q["t32"][:], p2[:, 256:384], Lp, A.add), (b2,), tag="t32")
         V(128, 1, ("t32" + b,), ("c32" + b,), lambda e: e.tensor_scalar(q["c32"][:], q["t32"][:], 4, 8191, A.arith_shift_right, A.bitwise_and), tag="c32")
         V(128, 1, ("c32" + b,), ("cu" + b,), lambda e: e.tensor_copy(q["cu"][:], q["c32"][:]), tag="cu")
-        P(128, ("Z" + b, "Ih"), lambda e: e.matmul(p1[:, 256:384], q["Z"][:], T.Ih[:], True, True), (b1,), tag="Ztr")
-        C(128, (), ("Zt" + b,), lambda e: e.activation(q["Zt"][:], p1[:, 256:384], F.Copy), (b1,), tag="Zt")
+        DMA(DCQ, 80, ("c32" + b,), ("cw" + b,), q["cw"][0:128:16, :], q["c32"][:], "c%d%s" % (t, b), tag="Dc")
+        P(128, ("Z" + b, "Id"), lambda e: e.matmul(p1[:, 256:384], q["Z"][:], T.Id[:], True, True), (b1,), tag="Ztr")
+        either("A", (), ("Zt" + b,), (vcost(128), lambda e: e.tensor_copy(q["Zt"][:], p1[:, 256:384])),
+               (acost(128), lambda e: e.activation(q["Zt"][:], p1[:, 256:384], F.Copy)), (b1,), tag="Zt")
+        if not last:
+            P(64, ("pass" + b, "l15"), lambda e: e.matmul(p0[:, 416:417], q["pass"][:], T.l15[:, 0:1], True, True), (b0,), tag="e0")
+            either(who[2], (), ("ec" + b,), (vcost(1), lambda e: e.tensor_copy(T.ec[:, n:n + 1], p0[:, 416:417])),
+                   (acost(1), lambda e: e.activation(T.ec[:, n:n + 1], p0[:, 416:417], F.Copy)), (b0,), tag="e1")
+        if not last and n:
+            def full(e):
+                e.matmul(p0[:, 420:421], cr[0:1, 0:128], ON[0:1, 0:1], True, False)
+                e.matmul(p0[:, 420:421], T.neg[:], T.ec[:, 0:1], False, False)
+                return e.matmul(p0[:, 420:421], T.neg[:], T.ec[:, 1:2], False, True)
+            P(192, ("crE", "ones", "neg", "ecA", "ecB"), full, (b0,), tag="e2")
+            V(1, 1, (), ("eR",), lambda e: e.tensor_scalar(T.eR[:], p0[:, 420:421], 2048 * MAGIC, 2048 * MAGIC, A.add, A.subtract), (b0,), tag="e3")
+            V(2, 1, ("eR",) + csts, ("nb%d" % (t + 1),),
+              lambda e: e.tensor_scalar(T.nb[:, 2 * t + 2:2 * t + 4], T.cst[:, 2 * t + 2:2 * t + 4], p0[:, 420:421], T.eR[:], A.add, A.subtract), (b0,), tag="e4")
         V(128, 1, ("c32" + b,), ("cm" + b,), lambda e: e.tensor_tensor(q["cm"][:], q["c32"][:], p0[:, 0:128], A.min), (b0,), tag="cm")
-        nw = T["nw" + b][:, t * 128:t * 128 + 128]
-        c = 16 * half[b].start
-        op("V", gcost(128), wins[b] + ["zo" + b, "cm" + b], ("nw%d%s" % (t, b),),
-           lambda e: e.tensor_tensor(nw, T.win[:, c:c + 2048].indirect(q["zo"][:, 8:16]), q["cm"][:], A.max), tag="nw")
-        P(512, ("I32", "nw%d%s" % (t, b)), lambda e: e.matmul(p2[:, 0:128], T.I32[:], nw, True, False), (b2,), tag="nat1")
+        op("V", gcost(128), wins[b] + ["zo" + b, "cm" + b], ("nw" + b,),
+           lambda e: e.tensor_tensor(q["nw"][:], q["win"][:, 0:2048].indirect(q["zo"][:, 8:16]), q["cm"][:], A.max), tag="nw")
         if last:
-            C(128, ("Z" + b,), ("yzs" + b,), lambda e: e.activation(T["ys" + b][:, 128:256], q["Z"][:], F.Copy), tag="yz")
-            DMA("S", 2.0, ("yzs" + b,), (), T.yz[:, half[b]], T["ys" + b][:, 128:256], "out", tag="out")
+            C(128, ("Z" + b,), ("yzs" + b,), lambda e: e.activation(q["nl"][:, 512:640], q["Z"][:], F.Copy, scale=2.0), tag="yz")
+            for h in (0, 1):
+                for k in (0, 1):
+                    DMA("S", 24, ("yzs" + b,), (), T.yz[own[b], tubes(h, k)], q["nl"][half[h], 512 + 64 * k:576 + 64 * k], "out", tag="out")
             return
-        C(128, ("Z" + b,), ("Zh" + b,), lambda e: e.activation(q["Zh"][:], q["Z"][:], F.Copy, bias=-0.25, scale=0.5), tag="Zh")
-        if allp:
-            P(512, ("us" + b, "Bd32"), lambda e: e.matmul(p1[:, 128:256], q["us"][:], T.Bd32[:], True, True), (b1,), tag="sT")
+
+        if every:
+            P(512, ("us" + b, "Bd128"), lambda e: e.matmul(p1[:, 128:256], q["us"][:], T.Bd128[:], True, True), (b1,), tag="sT")
+            V(128, 1, ("mask",), ("Ws" + b,), lambda e: e.tensor_tensor(q["Ws"][:], p1[:, 128:256], T.mask[:], A.mult), (b1,), tag="Ws")
+            P(256, ("Ws" + b, "Bd32"), lambda e: e.matmul(p1[:, 0:8], q["Ws"][:], T.Bd32[:, 0:128:16], True, True), (b1,), tag="sP")
         else:
-            P(128, ("Gm" + b, "wB"), lambda e: e.matmul(p1[:, 128:256], q["Gm"][:], T.wB[:], True, True), (b1,), tag="sT")
-        V(128, 1, ("mask",), ("Ws" + b,), lambda e: e.tensor_tensor(q["Ws"][:], p1[:, 128:256], T.mask[:], A.mult), (b1,), tag="Ws")
+            def sT(e):
+                e.matmul(p1[:, 128:256], ON[0:2, 0:128], cr[0:2, 768:896], True, False)
+                e.matmul(p1[:, 128:256], Gm, q["wE"][:, 256:384], False, False)
+                e.matmul(p1[:, 128:256], ON[0:1, 0:128], cr[0:1, 384:512], False, False)
+                e.matmul(p1[:, 128:256], ON[0:1, 0:128], cr[0:1, 512:640], False, False)
+                return e.matmul(p1[:, 128:256], Gm, q["wE"][:, 384:512], False, True)
+            P(640, ("Gm" + b, "wr" + b, "ws" + b, "crM", "crN", "crR", "ones"), sT, (b1,), tag="sT")
+            V(128, 1, ("mask",), ("q" + b,), lambda e: e.tensor_tensor(q["q"][:], p1[:, 128:256], T.mask[:], A.mult), (b1,), tag="Ws")
 
-    def joint(t):
-        p1 = T.p1B
+            def sP(e):
+                e.matmul(p1[:, 16:32], T.Id[:], T.CV[:, 16:32], True, False)
+                e.matmul(p1[0:64, 24:32], q["q"][:, 64:128], T.sel[:, 16:24], False, False)
+                e.matmul(p1[64:128, 24:32], q["q"][:, 0:64], T.sel[:, 16:24], False, False)
+                return e.matmul(p1[:, 16:24], q["q"][:], T.sel[:, 16:24], False, True)
+            P(256, ("q" + b, "Id", "V0", "V1", "V2", "selc"), sP, (b1,), tag="sP")
+            V(16, 1, (), ("rp" + b,), lambda e: e.tensor_copy(q["rp"][:], p1[:, 16:32]), (b1,), tag="w3")
+            return
+        vt = T.vt[:, 0:8]
+        V(8, 1, ("vtW",), ("rq" + b,), lambda e: e.tensor_tensor(q["rq"][:], p1[:, 0:8], vt, A.subtract), (b1,), tag="w1")
+        V(8, 1, ("rq" + b,), ("rd" + b,), lambda e: e.tensor_tensor(q["rd"][:], p1[:, 0:8], q["rq"][:], A.subtract), (b1,), tag="w2")
 
-        def sP(e, c, last):
-            e.matmul(p1[:, c:c + 16], T.Id[:], T.CV[:, 48 - c:64 - c], True, False)
-            e.matmul(p1[:, c:c + 8], T.WsA[:], T.sel32[:, c // 2:c // 2 + 8], False, False)
-            r = e.matmul(p1[:, c + 8:c + 16], T.WsB[:], T.sel32[:, c // 2:c // 2 + 8], False, last is None)
-            return r if last is None else e.matmul(p1[:, c:c + 16], T.I32n[:], last, False, True)
-        rd = ("WsA", "WsB", "Id", "CV", "CWA", "CWB", "sel32a", "sel32b", "I32n")
-        P(576, rd, lambda e: sP(e, 0, None), ("1B",), tag="sP")
-        V(16, 1, (), ("rq",), lambda e: e.tensor_scalar(T.rq[:], p1[:, 0:16], MAGIC, MAGIC, A.add, A.subtract), ("1B",), tag="w1")
-        P(832, rd + ("rq",), lambda e: sP(e, 16, T.rq[:]), ("1B",), tag="rP")
-        if (SUMS["A"] == "A") == (SUMS["B"] == "A"):
-            V(16, 1, (), ("rp",), lambda e: e.tensor_scalar(T.rp[:], p1[:, 16:32], 2047.5 if every else 0.0, None, A.add), ("1B",), tag="w2")
-        else:
-            for c, b in ((0, "A"), (8, "B")):
-                V(8, 1, (), ("rp",), lambda e, c=c, b=b: e.tensor_scalar(T.rp[:, c:c + 8], p1[:, 16 + c:24 + c], 2047.5 if SUMS[b] != "A" else 0.0, None, A.add), ("1B",), tag="w2")
-
-    def cuts(t):
-        p0 = T.p0A
-
-        def full(e):
-            e.matmul(p0[:, 128:256], T.Qe[:], T.passA[:], True, False)
-            return e.matmul(p0[:, 128:256], T.Qe[:], T.passB[:], False, True)
-        P(256, ("Qe", "passA", "passB"), full, ("0A",), tag="E")
-        ec = T.ec
-        C(200, (), ("ec", "ej"), lambda e: e.activation(T.ej[:], p0[:, 128:256], F.Copy, bias=-3.5 / 128, accum_out=ec[:, 0:1]), ("0A",), tag="Eacc")
-        C(1, ("ec",), ("e1",), lambda e: e.activation(ec[:, 1:2], ec[:, 0:1], F.Copy, bias=MAGIC, scale=0.125), tag="e1")
-        C(1, ("ec", "limg"), ("e2",), lambda e: e.activation(ec[:, 2:3], ec[:, 0:1], F.Identity, bias=T.limf[:, t + 5:t + 6]), tag="e2")
-        C(1, ("e1",), ("e3",), lambda e: e.activation(ec[:, 3:4], ec[:, 1:2], F.Copy, bias=-MAGIC), tag="e3")
-        C(1, ("e2", "e3"), ("thr",), lambda e: e.activation(col[:, 7:8], ec[:, 3:4], F.Identity, bias=ec[:, 2:3], scale=-8.0), tag="e4")
-        nthr()
-
-    zn = [0]
+        def rP(e):
+            e.matmul(p1[:, 16:24], T.I32[:], q["rd"][:], True, True)
+            return e.matmul(p1[:, 24:32], T.S32[:], q["rd"][:], True, True)
+        P(512, ("rd" + b, "I32", "S32"), rP, (b1,), tag="rP")
+        V(16, 1, (), ("rp" + b,), lambda e: e.tensor_scalar(q["rp"][:], p1[:, 16:32], 2047.5 if every else 0.0, None, A.add), (b1,), tag="w3")
 
     def middle(t, b):
         Gh, Pm, cu, Zt = T["Gc" + b], T["P" + b], T["cu" + b], T["Zt" + b]
         for who, j0, j1 in pieces(G2Q[b]):
-            gather(who, 512 * (j1 - j0), ("X", "cu" + b), names("Gc" + b, j0, j1), Gh[:, 512 * j0:512 * j1],
-                   T.X[:, 0:8192].indirect(cu[:, 32 * j0:32 * j1]), 0.5, tag="G2")
+            gather(who, 512 * (j1 - j0), xs[b] + ["cu" + b], names("Gc" + b, j0, j1), Gh[:, 512 * j0:512 * j1],
+                   T["X" + b][:, 0:8192].indirect(cu[:, 32 * j0:32 * j1]), 0.5, tag="G2")
         for j in range(4):
             f = slice(j * 512, j * 512 + 512)
-            z = "z%d" % (zn[0] & 1); zn[0] += 1
-            onv = MXQ[b][j] == "V"
-            P(512, ("Zt" + b, "Exp"), lambda e, z=z, f=f, onv=onv: e.matmul(T[z][:], Zt[:], T.Exp[:, f], True, onv), (z,), tag="Zx")
-            if onv:
-                V(512, 1, ("Gc%s%d" % (b, j),), ("P%s%d" % (b, j),), lambda e, z=z, f=f: e.tensor_tensor(Pm[:, f], Gh[:, f], T[z][:], A.max), (z,), tag="max")
-            else:
-                P(512, ("Gc%s%d" % (b, j), "Im"), lambda e, z=z, f=f: e.matmul(T[z][:], T.Im[:], Gh[:, f], False, True), (z,), tag="Zd")
-                C(512, (), ("P%s%d" % (b, j),), lambda e, z=z, f=f: e.activation(Pm[:, f], T[z][:], F.Relu, scale=-1.0), (z,), tag="max")
+            z, bk = (T["p2" + b], "2" + b) if j & 1 else (T["z" + b], "z" + b)
+            gk, zk, k = "Gc%s%d" % (b, j), "zx" + bk, len(ops) + 2
+            P(512, ("Zt" + b, "Exp"), lambda e, z=z, f=f, k=k: e.matmul(z[:], Zt[:], T.Exp[:, f], True, ops[k]["q"] == "V"), (bk,), tag="Zx", writes=(zk,))
+            P(512, (gk, "Im"), lambda e, z=z, f=f: e.matmul(z[:], T.Im[:], Gh[:, f], False, True), (bk,), tag="Zd")
+            either("A", (gk, zk), ("P%s%d" % (b, j),), (vcost(512), lambda e, z=z, f=f: e.tensor_tensor(Pm[:, f], Gh[:, f], z[:], A.max)),
+                   (acost(512), lambda e, z=z, f=f: e.activation(Pm[:, f], z[:], F.Relu, scale=-1.0)), (bk,), tag="max")
+            ops[k]["twin"] = k - 1
+            choose(ops, k, MXQ[b][j])
 
     def back(t, b):
         last = t == RO - 1
-        b0, b1, b2 = "0" + b, "1" + b, "2" + b
-        p0, p1, p2 = T["p0" + b], T["p1" + b], T["p2" + b]
-        q = {n: T[n + b] for n in ("Gc", "P", "OHc", "Km", "pm", "mn", "OH", "c32")}
+        b0, b1 = "0" + b, "1" + b
+        p0, p1 = T["p0" + b], T["p1" + b]
+        q = {n: T[n + b] for n in ("X", "Gc", "P", "Km", "pm", "ki", "ku", "Gy", "Z", "Y", "rp", "cw", "nw", "nl")}
 
         def keys(name, w, stop):
             def kd(e, i0):
@@ -405,170 +469,279 @@ def make_ops(core, T, topo):
                 return r
             for i0 in range(0, 16, CHUNK):
                 P(64 * CHUNK, names(name + b, 0, 4) + ["K8a", "K8b"], lambda e, i0=i0: kd(e, i0), (b0,), tag="key" + name[0])
-        P(128, ("kl", "kr"), lambda e: e.matmul(p0[:, 256:384], T.kl[0:2, :], T.kr[0:2, :], True, False), (b0,), tag="kc")
+        P(128, ("ones", "kr"), lambda e: e.matmul(p0[:, 256:384], ON[0:1, 0:128], T.kr[0:1, :], True, False), (b0,), tag="kc")
         keys("Gc", T.K8[:, 8:16], False)
         keys("P", T.K8[:, 0:8], True)
         V(128, 1, ("Rk",), ("pm" + b,), lambda e: e.tensor_tensor_scan(q["pm"][:], T.Rk[:], p0[:, 256:384], 0.0, A.max, A.min), (b0,), tag="scan")
-        least = q["pm"][:, 0:128].indirect(T.cidx[:])
-        if not last:
-            op("V", gcost(128), ("pm" + b, "cidx", "mask"), ("Km" + b,), lambda e: e.tensor_tensor(q["Km"][:], least, T.mask[:], A.mult), tag="Km")
-        if OPQ[b][2] == "A":
-            gather("A", 128, ("pm" + b, "cidx"), ("mn" + b,), q["mn"][:], least, tag="mn")
-        else:
-            V(128, 1, ("Rk", "pm" + b), ("mn" + b,), lambda e: e.tensor_tensor_scan(q["mn"][:, 127::-1], T.Rk[:], q["pm"][:, 127::-1], 0.0, A.max, A.min), tag="mn")
-        V(128, 1, ("mn" + b,), ("OH" + b,), lambda e: e.tensor_tensor(q["OH"][:], p0[:, 256:384], q["mn"][:], A.is_equal), (b0,), tag="OH")
+        V(8, 1, ("pm" + b,), ("ki" + b,), lambda e: e.tensor_copy(q["ki"][:, 0:8], q["pm"][:, 15:128:16]), tag="k1")
+        V(8, 1, ("ki" + b,), ("kj" + b,), lambda e: e.tensor_scalar(q["ki"][:, 8:16], q["ki"][:, 0:8], 15, None, A.bitwise_and), tag="k2")
+        op("V", gcost(128), ("kj" + b, "cidx", "mask"), ("Km" + b,),
+           lambda e: e.tensor_tensor(q["Km"][:], q["ki"][:, 8:16].indirect(T.cidx[:]), T.mask[:], A.mult), tag="Km")
 
-        def index(blocks):
-            n = 8 * len(blocks); c = 8 if blocks == "B" else 0
-            pk, bk = (T.z0, "z0") if b == "B" else (p1, b1)
-            for j, a in enumerate(blocks):
-                P(256, ("Km" + a, "Bd32"), lambda e, j=j, a=a: e.matmul(pk[:, 384 + 8 * j:392 + 8 * j], T["Km" + a][:], T.Bd32[:, 0:128:16], True, True), (bk,), tag="Kp" + a)
-            V(n, 1, (), ("ki" + b,), lambda e: e.tensor_copy(T.ki[:, c:c + n], pk[:, 384:384 + n]), (bk,), tag="k1")
-            V(n, 1, ("ki" + b,), ("kj" + b,), lambda e: e.tensor_scalar(T.ki[:, 16 + c:16 + c + n], T.ki[:, c:c + n], 2047, None, A.bitwise_and), tag="k2")
-            V(n, 1, ("kj" + b,), ["ku" + a for a in blocks], lambda e: e.tensor_copy(T.ku[:, c:c + n], T.ki[:, 16 + c:16 + c + n]), tag="k3")
-            for a in blocks:
-                k = half[a].start // 16
-                op("V", gcost(128), ["ku" + a, "Zh" + a] + names("Gc" + a, 0, 4), ("Y" + a,),
-                   lambda e, a=a, k=k: e.tensor_tensor(T.Y[:, half[a]], T["Gc" + a][:, 0:2048].indirect(T.ku[:, k:k + 8]), T["Zh" + a][:], A.add), tag="Y" + a)
-        if not last and b == "B": index("AB" if TAIL["A"][0] == "A" else "B")
-        P(128, ("OH" + b, "Id"), lambda e: e.matmul(p1[:, 0:128], q["OH"][:], T.Id[:], True, True), (b1,), tag="OHT")
-        V(128, 1, ("c32" + b,), ("OHc" + b,), lambda e: e.tensor_tensor(q["OHc"][:], q["c32"][:], p1[:, 0:128], A.mult), (b1,), tag="OHc")
-        if not last and b == "A" and TAIL["A"][0] != "A": index("A")
-        P(512, ("E32", "OHc" + b), lambda e: e.matmul(p2[:, 0:128], T.E32[:, 15:143], q["OHc"][:], False, True), (b2,), tag="nat2")
+        def kP(e):
+            e.matmul(p0[:, 400:416], T.Id[:], T.CV[:, 0:16], True, False)
+            return e.matmul(p0[:, 400:416], q["Km"][:], T.sel[:, 0:16], False, True)
+        P(128, ("Km" + b, "Id", "CV", "sela", "selb"), kP, (b0,), tag="Kp")
+        V(16, 1, (), ("ku" + b,), lambda e: e.tensor_copy(q["ku"][:], p0[:, 400:416]), (b0,), tag="k3")
+        nl, su, best = lists(t, b, n="nl"), T["su" + b], q["cw"][:, 0:2048].indirect(q["ku"][:, 8:16])
+        c, nlk, suk = [256 * t, 256 * t + 128][:1 + FOLD], "nl%d%s" % (t, b), "su%d%s" % (t, b)
+        if last or not FOLD:
+            op("V", gcost(128), ("cw" + b, "ku" + b, "nw" + b), (nlk,), lambda e: e.tensor_tensor(nl, best, q["nw"][:], A.max), tag="n0")
         if last:
-            ys = T["ys" + b]
-            V(128, 1, (), ("yls" + b,), lambda e: e.tensor_copy(ys[:, 0:128], p2[:, 0:128]), (b2,), tag="yl")
-            DMA("S", 2.0, ("yls" + b,), (), T.yl[:, half[b]], ys[:, 0:128], "out", tag="out")
+            for h in (0, 1):
+                for k in (0, 1):
+                    DMA("AD" if k else "S", 24, (nlk,), (), T.yl[own[b], tubes(h, k)], q["nl"][half[h], 128 * t + 64 * k:128 * t + 64 * k + 64], "out", tag="out")
             return
-        su = T["su" + b][:, t * 128:t * 128 + 128]
-        V(128, 1, (), ("su%d%s" % (t, b),), lambda e: e.tensor_copy(su, p2[:, 0:128]), (b2,), tag="su")
-        pend[b] = op("G", 0.8, ("su%d%s" % (t, b),), (), ("send", su, lists(t + 1, b), "au%d%s" % (t + 1, b), peer[b][0]), sem="snd", tag="send")
+        if FOLD:
+            V(128, 1, ("nw" + b,), (suk,), lambda e: e.tensor_copy(su[:, c[0]:c[0] + 128], q["nw"][:]), tag="su")
+            op("V", gcost(128), ("cw" + b, "ku" + b), (nlk,), lambda e: e.tensor_copy(su[:, c[1]:c[1] + 128], best), tag="n0")
+        else:
+            V(128, 1, (nlk,), (suk,), lambda e: e.tensor_copy(su[:, c[0]:c[0] + 128], nl), tag="su")
+        pend[b] = op("G", 0.8, (suk, nlk), (),
+                     [([su[:, x + 64 * k:x + 64 * k + 64] for x in c], lists(t + 1, b, 2 * k, 2 * k + 2)) for k in (0, 1)] + ["au%d%s" % (t + 1, b)],
+                     sem="snd", tag="send")
+        if not FOLD:
+            pend["f" + b] = op("G", 0.8, (nlk,), (), [([lists(t, b, 2 * k, 2 * k + 2, "nl")], lists(t + 1, b, 2 * k, 2 * k + 2, "lf")) for k in (0, 1)]
+                               + ["af%d%s" % (t + 1, b)], sem="snd", sched=(pend[b],), tag="sendf")
+        gather(OPQ[b][4], 128, ["ku" + b] + names("Gc" + b, 0, 4), ("Gy" + b,), q["Gy"][:, 0:128], q["Gc"][:, 0:2048].indirect(q["ku"][:, 0:8]), tag="Gy")
 
-    def scatter(t, b):
-        if TAIL["B"][0] == "A":
-            if b == "B":
-                op("V", 0.06 + 256 * 3.5 * CY, ("YA", "YB", "rp"), ("X",), lambda e: e.tensor_copy(T.X[:, 0:8192].indirect(T.rp[:]), T.Y[:]), tag="scat")
-            return
-        c0 = 0 if b == "A" else 8
-        op("V", 0.06 + 128 * 3.5 * CY, ("Y" + b, "rp"), ("X",),
-           lambda e: e.tensor_copy(T.X[:, 0:8192].indirect(T.rp[:, c0:c0 + 8]), T.Y[:, half[b]]), tag="scat")
-
-    def both(step, t):
-        for b in "AB":
-            cur[0] = b
-            step(t, b)
-        cur[0] = ""
+        def yP(e):
+            for c, m in ((0, T.Id), (128, T.Sw)):
+                e.matmul(p1[:, c:c + 128], m[:], q["Z"][:], True, False)
+                r = e.matmul(p1[:, c:c + 128], m[:], q["Gy"][:, 0:128], False, True)
+            return r
+        P(512, ("Gy" + b, "Z" + b, "Id", "Sw"), yP, (b1,), tag="yP")
+        V(256, 1, (), ("Y" + b,), lambda e: e.tensor_scalar(q["Y"][:], p1[:, 0:256], -0.25, None, A.add), (b1,), tag="Y")
+        op("V", 0.06 + 256 * SCA * CY, ("Y" + b, "rp" + b), xs[b], lambda e: e.tensor_copy(q["X"][:, 0:8192].indirect(q["rp"][:]), q["Y"][:]), tag="scat")
 
     for t in range(RO):
-        window(t)
-        both(front, t)
-        if t < RO - 1: joint(t)
-        both(middle, t)
-        both(back, t)
-        if t < RO - 1:
-            cuts(t)
-            both(scatter, t)
-    return ops, lanes, peer
+        for b in SETS:
+            cur[0:2] = [b, t]
+            for step in (window, front, middle, back): step(t, b)
+    return ops
 
 
-def schedule(ops):
-    n = len(ops)
-    pred = [sorted(o["wait"] | o["order"]) for o in ops]
+def schedule(ops, given=None):
+    n, nm = len(ops), len(CY)
+    pred = [sorted(o["hard"] | o["soft"] | o["order"]) for o in ops]
     succ = [[] for _ in range(n)]
     for i in range(n):
         for d in pred[i]: succ[d].append(i)
-    que = [DMAS.get(o["q"], o["q"]) for o in ops]
-    cost = [o["c"] for o in ops]
-    hold = [0.0 if o["q"] == "R" else ISSUE if o["q"] in DMAS else o["c"] for o in ops]
+    que, wake, own = [0] * n, [float(x) for x in WAKE], [float(x) for x in SELF]
+    cost, hold, after = ([[0.0] * n for m in range(nm)] for _ in range(3))
 
-    def lag(a, b):
-        return WAKE if ops[a]["q"] != ops[b]["q"] else SELF if (a in ops[b]["wait"] or b in ops[a]["wait"]) else 0.0
-    before = [[(d, cost[d] + lag(d, i)) for d in pred[i]] for i in range(n)]
-    behind = [[(d, cost[d] + lag(d, i)) for d in succ[i]] for i in range(n)]
+    def lag(a, b, m):
+        qa, qb = ops[a]["q"], ops[b]["q"]
+        return 0.0 if "N" in (qa, qb) else wake[m] if qa != qb else own[m] if a in ops[b]["hard"] and qa != "T" else 0.0
 
-    def place(key, first, after, back):
-        need = [len(x) for x in first]
+    def enter(i):
+        o = ops[i]
+        que[i] = "VATGSRN".index(DMAS.get(o["q"], o["q"])) if o["q"] != "N" else 5
+        for m in range(nm):
+            cost[m][i] = 0.0 if o["q"] == "N" else float((o["c"] + 0 * CY)[m])
+            hold[m][i] = 0.0 if o["q"] == "R" else float(ISSUE[m]) * o["n"] if o["q"] in DMAS else cost[m][i]
+            for k in [i] + succ[i]: after[m][k] = [(d, lag(d, k, m)) for d in pred[k]]
+
+    def flip(i):
+        choose(ops, i, "A" if ops[i]["q"] == "V" else "V")
+        enter(i)
+        if "twin" in ops[i]: enter(ops[i]["twin"])
+    for i in range(n): enter(i)
+    work = [[o.get("kb", 0) * float(LOAD[m]) / 1024 for o in ops] for m in range(nm)]
+    late, at = [0.0] * n, 0.0
+    for i in range(n):
+        at += work[0][i] if "first" in ops[i] else 0.0
+        late[i] = at if "first" in ops[i] else 4 * work[0][i]
+    before = [[[(d, cost[0][d] + late[d] + lag(d, i, 0)) for d in pred[i]] for i in range(n)]]
+
+    def times(order, m):
+        st, fin, free, why, last = [0.0] * n, [0.0] * n, [0.0] * 7, [-1] * n, [-1] * 7
+        bf, hd, cs, mv = after[m], hold[m], cost[m], work[m]
+        end, e = 0.0, 0
+        for i in order:
+            k = que[i]
+            s, w = free[k], last[k]
+            for d, x in bf[i]:
+                x += fin[d]
+                if x > s: s = x; w = d
+            st[i] = s
+            if k < 5: free[k] = s + hd[i]; last[k] = i
+            if mv[i]:
+                s += hd[i] + 0.5 * cs[i]
+                if free[6] > s: s = free[6]; w = last[6]
+                free[6] = s + mv[i]; last[6] = i
+                s += mv[i] + 0.5 * cs[i]
+            else:
+                s += cs[i]
+            fin[i] = s; why[i] = w
+            if s > end: end = s; e = i
+        return end, st, why, e
+
+    if given: return [times(given, m)[0] for m in range(nm)]
+
+    def score(order):
+        r = [times(order, m) for m in range(nm)]
+        return sum((x[0] + EARLY * sum(x[1]) / n) * w for x, w in zip(r, WEIGHT)), r
+
+    def move(order, pos, a, b, back):
+        lo, hi = pos[a], pos[b]
+        if lo >= hi or "first" in ops[a]: return False
+        mark, near = ({a}, pred) if back else ({b}, succ)
+        for k in range(lo + 1, hi + 1) if back else range(hi - 1, lo - 1, -1):
+            i = order[k]
+            for x in near[i]:
+                if x in mark: mark.add(i); break
+        if a in mark and b in mark: return False
+        seg = order[lo:hi + 1]
+        seg = [i for i in seg if (i in mark) != back] + [i for i in seg if (i in mark) == back]
+        order[lo:hi + 1] = seg
+        for k, i in enumerate(seg): pos[i] = lo + k
+        return True
+
+    tail = [0.0] * n
+    for i in range(n - 1, -1, -1):
+        tail[i] = cost[0][i] + max([tail[s] + lag(i, s, 0) for s in succ[i]], default=0.0)
+    same = {}
+    for o in ops: same.setdefault(o["kind"], {})[o["t"]] = o["i"]
+
+    def place(key):
+        need = [len(x) for x in pred]
         ready = [i for i in range(n) if not need[i]]
         start, busy = [0.0] * n, {}
         while ready:
             i = min(ready, key=lambda k: key[k])
             ready.remove(i)
-            s = max([start[d] + w for d, w in first[i]], default=0.0)
-            shift = cost[i] - hold[i] if back else 0.0
+            s = max([start[d] + w for d, w in before[0][i]], default=0.0)
             line = busy.setdefault(que[i], [])
-            s += shift; k = len(line)
+            k, h = len(line), hold[0][i]
             while k and line[k - 1][1] > s: k -= 1
-            while k < len(line) and line[k][0] < s + hold[i]:
+            while k < len(line) and line[k][0] < s + h:
                 s = max(s, line[k][1]); k += 1
-            if hold[i]: line.insert(k, (s, s + hold[i]))
-            start[i] = s - shift
-            for k in after[i]:
+            if h: line.insert(k, (s, s + h))
+            start[i] = s
+            for k in succ[i]:
                 need[k] -= 1
                 if not need[k]: ready.append(k)
-        return start, max(start[i] + cost[i] for i in range(n))
+        return sorted(range(n), key=lambda i: (start[i], i))
 
-    tail = [0.0] * n
-    for i in range(n - 1, -1, -1):
-        tail[i] = cost[i] + max([tail[s] + lag(i, s) for s in succ[i]], default=0.0)
-    best = place([-x for x in tail], before, succ, False)
-    rng = np.random.default_rng(0)
-    kinds = sorted(set(o["tag"] for o in ops))
-    kind = [kinds.index(o["tag"]) for o in ops]
-    now = best
-    for k in range(PASSES):
-        push = rng.normal(0.0, SHAKE, len(kinds)) * (rng.random(len(kinds)) < SHARE) if k else np.zeros(len(kinds))
-        if k & 1:
-            last = place([s + float(push[j]) for s, j in zip(now[0], kind)], before, succ, False)
-        else:
-            bw = place([-(s + c + float(push[j])) for s, c, j in zip(now[0], cost, kind)], behind, pred, True)[0]
-            last = place([-(s + c) for s, c in zip(bw, cost)], before, succ, False)
-        if last[1] <= now[1] + SLACK * (1 - k / PASSES) * rng.random(): now = last
-        if last[1] <= best[1]: best = last
-    for o in ops: o["s"] = best[0][o["i"]]
-    return sorted(range(n), key=lambda i: (-1.0 if "first" in ops[i] else best[0][i], i)), best[1]
+    def keys(stretch, behind):
+        g1 = {b: same["G1" + b, 1] for b in SETS}
+        loop = tail[g1[SETS[1]][1]] - tail[g1[SETS[1]][2]]
+        key = [0.0] * n
+        for i in range(n - 1, -1, -1):
+            o = ops[i]
+            if "first" in o or "soon" in o: key[i] = -1e9 + i
+            elif o["t"] < 0: key[i] = min([key[s] for s in succ[i]], default=0.0) - cost[0][i] - 0.2
+            else: key[i] = stretch * (loop * (o["t"] + (behind if o["b"] == SETS[1] else 0.0)) + tail[g1[o["b"]][o["t"]]] - tail[i])
+        return key
+    tries = [place(keys(x, y)) for x in STRETCH for y in BEHIND]
+    order = min(tries, key=lambda x: score(x)[0])
+    rng = np.random.default_rng(SEED)
+    now, res = score(order)
+    best = (now, order, [o["q"] for o in ops])
+    free = [o["i"] for o in ops if "alt" in o]
+    for it in range(STEPS):
+        heat = HEAT * (1 - it / STEPS) ** 2 + 1e-3
+        _, st, why, e = res[int(rng.integers(nm))]
+        pairs, can = [], []
+        while why[e] >= 0:
+            d = why[e]
+            if d not in pred[e]:
+                pairs.append((d, e))
+                if "alt" in ops[d]: can.append(d)
+            e = d
+        if not pairs: break
+        if can and rng.random() < FLIP:
+            todo = set()
+            for i in [can[int(rng.integers(len(can)))]] + ([free[int(rng.integers(len(free)))]] if rng.random() < 0.5 else []):
+                todo.update([k for k in same[ops[i]["kind"]].values() if ops[k]["q"] == ops[i]["q"]] if rng.random() < EVERY else [i])
+            for i in todo: flip(i)
+            sc, r2 = score(order)
+            if sc <= now or rng.random() < math.exp((now - sc) / heat):
+                now, res = sc, r2
+                if sc < best[0]: best = (sc, order, [o["q"] for o in ops])
+            else:
+                for i in todo: flip(i)
+            continue
+        a, b = pairs[int(rng.integers(len(pairs)))]
+        new, pos = list(order), [0] * n
+        for k, i in enumerate(new): pos[i] = k
+        r, far, back = rng.random(), int(rng.integers(0, FAR)), rng.random() < 0.5
+        k = pos[b] if back else pos[a]
+        while far and 0 < k < n - 1:
+            k += 1 if back else -1
+            if que[new[k]] == que[a]:
+                far -= 1
+                if back: b = new[k]
+                else: a = new[k]
+        todo = [(a, b)]
+        if r < EVERY:
+            dt = ops[b]["t"] - ops[a]["t"]
+            ka, kb = same[ops[a]["kind"]], same[ops[b]["kind"]]
+            todo = [(ka[t], kb[t + dt]) for t in ka if t + dt in kb]
+        if not sum([move(new, pos, x, y, back) for x, y in todo]): continue
+        sc, r2 = score(new)
+        if sc <= now or rng.random() < math.exp((now - sc) / heat):
+            now, res, st = sc, r2, r2[0][1]
+            if sc < best[0]: best = (sc, new, [o["q"] for o in ops])
+            order = new
+            if it % 8 == 0:
+                order = sorted(new, key=lambda i: st[i])
+                now, res = score(order)
+    for i in free:
+        if ops[i]["q"] != best[2][i]: flip(i)
+    res = score(best[1])[1]
+    for o in ops: o["s"] = res[0][1][o["i"]]; o["why"] = [x[2][o["i"]] for x in res]; o["ss"] = [x[1][o["i"]] for x in res]
+    return best[1], [x[0] for x in res]
 
 
 def rank_program(g, core, T, topo):
     if T.rank_of(core) is None:
         return
-    ops, lanes, peer = make_ops(core, T, topo)
+    ops = make_ops(core, T, topo)
     if not PLAN:
-        PLAN.extend([schedule(ops), [o["s"] for o in ops]])
+        PLAN.extend([schedule(ops), [o["s"] for o in ops], [o["q"] for o in ops]])
     order = PLAN[0][0]
-    for o in ops: o["s"] = PLAN[1][o["i"]]
+    for o in ops:
+        o["s"] = PLAN[1][o["i"]]
+        if "alt" in o: choose(ops, o["i"], PLAN[2][o["i"]])
     eng = {"V": g.vector, "A": g.scalar, "T": g.tensor, "G": g, "S": g.sync, "AD": g.scalar, "GD": g}
     qsem = {"V": "qV", "A": "qA", "T": "qT", "G": "qG"}
+    to, use = lanes(T, topo, core)
     total = {}
     for o in ops:
-        if o["q"] in DMAS: total[o["sem"]] = total.get(o["sem"], 0) + 16
+        if o["q"] in DMAS: total[o["sem"]] = total.get(o["sem"], 0) + 16 * o["n"]
     cnt, known, snap, done = {}, {}, {}, {}
     sent = 0
     for i in order:
         o = ops[i]
+        if o["q"] == "N": continue
         if o["q"] == "R":
             done[i] = (o["sem"], o["n"]); snap[i] = {o["sem"]: o["n"]}
             continue
         qn = DMAS.get(o["q"], o["q"])
         e = eng[o["q"]]
         kn = known.setdefault(qn, {})
-        for d in sorted(o["wait"], key=lambda d: -ops[d]["s"]):
+        for d in sorted(waits(ops, o), key=lambda d: -ops[d]["s"]):
+            if ops[d]["q"] == "N" or ops[d]["q"] == o["q"] == "T": continue
             s, v = done[d]
             if kn.get(s, 0) >= v: continue
             e.wait_ge(T.sem[s], v)
             for k, x in snap[d].items():
                 if kn.get(k, 0) < x: kn[k] = x
         if o["sem"] == "snd":
-            _, src, dst, sem, to = o["fn"]
-            ln = lanes(core, to)
-            rid, pid, _ = topo.addr(to)
-            g.remote_dma(out_ap=dst, in_ap=src, remote_sem=T.sem[sem], local_sem=T.sem.snd, pid=pid, routing_id=rid,
-                         dma_engine_mask=sum(1 << x for x in ln))
-            sent += len(ln)
+            moves = []
+            for (src, dst), d, ln in zip(o["fn"][:2], to, use):
+                rid, pid, _ = topo.addr(d)
+                moves.append(RemoteDMATransfer(dst_ids=[DstId(rid=rid, pnc=pid)], dma_engine_mask=sum(1 << x for x in ln),
+                                               remote_sem=T.sem[o["fn"][2]], srcs=src, dsts=[dst], alu_op=2 * (len(src) - 1)))
+                sent += len(ln)
+            g.remote_dma_fused(moves, local_sem=T.sem.snd)
             done[i] = ("snd", sent); snap[i] = dict(kn)
         else:
             r = o["fn"](e)
             if o["q"] in DMAS:
-                r.then_inc(T.sem[o["sem"]], 16)
+                for x in r: x.then_inc(T.sem[o["sem"]], 16)
                 done[i] = (o["sem"], total[o["sem"]]); cnt[o["sem"]] = total[o["sem"]]
             else:
                 s = qsem[o["q"]]

import math
import numpy as np
from concourse.bass import DstId, RemoteDMATransfer
from concourse.mybir import AluOpType, AxisListType, ActivationFunctionType

A = AluOpType
F = ActivationFunctionType
RO = 4
BF, F32, I32, U16 = "bfloat16", "float32", "int32", "uint16"
MAGIC = 12582912.0
SETS = "AB"

SCRATCH = {}
for _b in SETS:
    for _n in ("p0", "p1", "p2", "z"):
        SCRATCH[_n + _b] = ("psum", [128, 512], F32)
    for _n, _s, _d in (("X", 8192, BF), ("G", 2048, BF), ("M", 2048, BF), ("H", 2048, BF), ("Gc", 2048, BF), ("P", 2048, BF),
                       ("Lp", 128, F32), ("t32", 128, I32), ("c32", 128, I32), ("Wm", 128, BF), ("cm", 128, F32), ("Km", 128, BF),
                       ("pm", 128, F32), ("pass", 128, BF), ("q", 128, BF), ("Z", 128, BF), ("Zt", 128, BF), ("cu", 128, U16),
                       ("uf", 128, F32), ("us", 128, F32), ("Ws", 128, F32), ("Gy", 256, BF), ("lf", 512, F32), ("nw", 128, F32),
                       ("nl", 640, F32), ("zo", 16, U16), ("ku", 16, U16), ("ki", 16, I32), ("rq", 8, I32), ("rd", 8, F32),
                       ("rp", 16, U16), ("Y", 256, I32), ("su", 768, U16), ("lu", 512, U16), ("win", 2048, F32),
                       ("cw", 2048, I32), ("wE", 512, BF), ("col", 8, F32)):
        SCRATCH[_n + _b] = ("sbuf", [128, _s], _d)
    SCRATCH["rows" + _b] = ("dram", [8, 32, 128], F32)
for _n, _s, _d in (("R", 512, BF), ("Bd32", 128, F32), ("Bd128", 128, F32), ("Dm", 128, F32), ("Rk", 128, F32), ("ones", 256, BF),
                   ("Exp", 2048, BF), ("E", 144, BF), ("pE", 144, BF), ("Bd", 128, BF), ("Id", 128, BF), ("Sw", 128, BF),
                   ("Im", 128, BF), ("Bn", 128, BF), ("mask", 128, BF), ("K8", 16, BF), ("sel", 24, BF), ("CV", 32, BF),
                   ("cr", 896, BF), ("kr", 128, BF), ("I32", 128, F32), ("S32", 128, F32), ("neg", 128, BF), ("cols", 8, F32),
                   ("l15", 2, BF), ("prm", 8, I32), ("prf", 8, F32), ("tub", 256, I32), ("pi", 32, I32), ("cv", 32, I32),
                   ("cidx", 8, U16), ("vt", 16, F32), ("cst", 8, F32), ("nb", 8, F32), ("ec", 2, BF), ("eR", 1, F32),
                   ("ej", 128, BF)):
    SCRATCH[_n] = ("sbuf", [128, _s], _d)

PARTS = 4
SEMAPHORES = ["qV", "qA", "qT", "qG", "ltub", "lwt", "lkn", "llim", "snd", "out"]
SEMAPHORES += ["x%d%s" % (_t, _b) for _t in range(2 * PARTS) for _b in SETS]
SEMAPHORES += [_n + str(_t) + _b for _n in "wrc" for _t in range(RO) for _b in SETS]
SEMAPHORES += [_n + str(_t) + _b for _n in ("au", "af") for _t in range(1, RO) for _b in SETS]

CY = np.array([0.85e-3, 1.1e-3])
PEC = np.array([0.55e-3, 0.72e-3])
VFIX, AFIX = 0.03, 0.06
GA = np.array([1.56, 1.6])
SCA = np.array([3.8, 3.8])
WAKE = np.array([0.2, 0.18])
FLY = np.array([2.2, 2.0])
SELF = np.array([0.14, 0.12])
DMA0 = np.array([2.2, 2.0])
LOAD = np.array([5.5, 4.5])
ISSUE = np.array([0.22, 0.15])
DCQ = "S"
WEIGHT = (0.5, 0.5)
EARLY, FLIP = 0.5, 0.1
STEPS, HEAT, EVERY, FAR, SEED = 40000, 0.25, 0.7, 4, 2
G1Q = {"A": "AVAA", "B": "AVAA"}
G2Q = {"A": "AVAA", "B": "AVAA"}
SCQ = "VVVV"
CPQ = {"A": "AVAV", "B": "AVAV"}
MXQ = {"A": "VAAV", "B": "VAAV"}
OPQ = {"A": "VAAAAV", "B": "VAAAAV"}
SUMS = {"A": "W", "B": "G"}
DUP = {"A": "VAVV", "B": "VVVV"}
STRETCH, BEHIND = (1.2,), (0.2,)
FOLD = True
ZERO = {"A": "A", "B": "G"}
CHUNK = 4
PLAN = []
DMAS = {"S": "S", "AD": "A", "GD": "G"}


def pieces(s):
    cut = [j for j in range(4) if j == 0 or s[j] != "-"] + [4]
    return [(s[a].replace("-", "V"), a, z) for a, z in zip(cut, cut[1:])]


def names(s, j0, j1): return [s + str(j) for j in range(j0, j1)]
def vcost(n, f=1.0): return VFIX + max(64, n * f) * CY
def acost(n): return AFIX + max(64, n) * CY
def gcost(n): return 0.06 + n * GA * CY


def choose(ops, i, q):
    o = ops[i]
    o["q"] = q
    o["c"], o["fn"] = o["alt"][q]
    if "twin" in o: ops[o["twin"]]["q"] = "T" if q == "A" else "N"


def waits(ops, o):
    return o["hard"] | set(d for d in o["soft"] if ops[d]["q"] != o["q"] or o["q"] in DMAS)


def lanes(T, topo, core):
    r, n = T.rank_of(core), len(T.cores)
    to = [T.cores[(r + 1) % n], T.cores[(r - 1) % n]]
    may = [topo.engines(core, d) for d in to]
    few = 0 if len(may[0]) <= len(may[1]) else 1
    rest = [x for x in may[1 - few] if x not in may[few]]
    if rest:
        k = min(len(rest), len(may[few]))
        use = {few: may[few][:k], 1 - few: rest[:k]}
    else:
        k = len(may[few]) // 2
        use = {few: may[few][:k], 1 - few: may[few][k:2 * k]}
    return to, [use[0], use[1]]


def make_ops(core, T, topo):
    ops = []
    lastw, readers, bank, seen = {}, {}, {}, {}
    cur = ["", -1]

    def op(q, cost, reads, writes, fn, banks=(), sem=None, cnt=0, sched=(), tag=""):
        o = {"i": len(ops), "q": q, "c": cost, "fn": fn, "hard": set(), "soft": set(), "order": set(sched), "sem": sem,
             "tag": tag + cur[0], "n": cnt, "b": cur[0], "t": cur[1]}
        seen[o["tag"], cur[1]] = seen.get((o["tag"], cur[1]), 0) + 1
        o["kind"] = (o["tag"], seen[o["tag"], cur[1]])
        for k in reads:
            if k in lastw: o["hard"].add(lastw[k])
        for k in writes:
            if k in lastw: o["hard"].add(lastw[k])
            o["soft"].update(readers.get(k, ()))
        for k in banks:
            if k in bank: o["soft"].add(bank[k])
            bank[k] = o["i"]
        for k in reads: readers.setdefault(k, []).append(o["i"])
        for k in writes:
            lastw[k] = o["i"]; readers[k] = []
        o["hard"].discard(o["i"]); o["soft"].discard(o["i"])
        ops.append(o)
        return o["i"]

    def V(n, f, reads, writes, fn, banks=(), tag=""):
        return op("V", vcost(n, f), reads, writes, fn, banks, tag=tag)

    def C(n, reads, writes, fn, banks=(), tag=""):
        return op("A", acost(n), reads, writes, fn, banks, tag=tag)

    def either(q, reads, writes, onv, ona, banks=(), tag=""):
        i = op(q, None, reads, writes, None, banks, tag=tag)
        ops[i]["alt"] = {"V": onv, "A": ona}
        choose(ops, i, q)
        return i

    def P(cyc, reads, fn, banks, tag="", writes=()):
        return op("T", 0.01 + cyc * PEC, reads, writes, fn, banks, tag=tag)

    def Gc(n, reads, writes, fn, tag=""):
        return op("G", 0.17 + 2 * n * CY, reads, writes, fn, tag=tag)

    def moves(i, kb):
        ops[i]["kb"] = kb
        return i

    def DMA(q, kb, reads, writes, out, in_, sem, tag=""):
        return moves(op(q, DMA0, reads, writes, lambda e: [e.dma_start(out, in_)], sem=sem, cnt=1, tag=tag), kb)

    def times(n, reads, write, out, src, scale=1.0, bias=0.0):
        return either("A", reads, (write,), (vcost(n, .75), lambda e: e.tensor_scalar(out, src, scale, bias, A.mult, A.add)),
                      (acost(n), lambda e: e.activation(out, src, F.Copy if isinstance(scale, float) else F.Identity, bias=bias, scale=scale)))

    def gather(q, n, reads, writes, out, src, scale=None, tag=""):
        ona = (lambda e: e.activation(out, src, F.Copy)) if scale is None else (lambda e: e.activation(out, src, F.Copy, scale=scale))
        onv = (lambda e: e.tensor_copy(out, src)) if scale is None else (lambda e: e.tensor_scalar(out, src, scale, None, A.mult))
        return either(q, reads, writes, (gcost(n), onv), (gcost(n) + 0.02, ona), tag=tag)

    rank, ncore = T.rank_of(core), len(T.cores)
    arrive = len(lanes(T, topo, T.cores[(rank - 1) % ncore])[1][0]) + len(lanes(T, topo, T.cores[(rank + 1) % ncore])[1][1])
    half = (slice(0, 64), slice(64, 128))
    own = {"A": half[0], "B": half[1]}
    wins = {b: names("win" + b, 0, 16) for b in SETS}
    xs = {b: names("X" + b, 0, 2 * PARTS) for b in SETS}

    def lists(t, b, j0=0, j1=4, n="lu"):
        return T[n + b][:, t * 128 + 32 * j0:t * 128 + 32 * j1]

    def tubes(h, k):
        return slice(128 * k + 64 * h, 128 * k + 64 * h + 64)

    small = [DMA("S", 128, (), ("tub",), T.tub[:], T.tube[:], "ltub"), DMA("AD", 32, (), ("wi",), T.prm[:, 0:1], T.wt[:], "lwt"),
             DMA("AD", 32, (), ("kni",), T.prm[:, 1:2], T.kn[:], "lkn"), DMA("AD", 32, (), ("limi",), T.prm[:, 4:8], T.lim[:], "llim")]
    w = 8192 // PARTS
    for b in SETS:
        for k in range(PARTS):
            for h in (0, 1) if DUP[b][k] == "D" else (0,):
                small.append(DMA("S", 1024 // PARTS, (), (xs[b][2 * k + h],), T["X" + b][half[(k + h) & 1], k * w:k * w + w],
                                 T.field[own[b], k * w:k * w + w], "x%d%s" % (2 * k + h, b), tag="ld" + b))
    for i in small: ops[i]["first"] = True
    for b in SETS:
        for k in range(PARTS):
            dst, src = T["X" + b][half[1 - (k & 1)], k * w:k * w + w], T["X" + b][half[k & 1], k * w:k * w + w]
            if DUP[b][k] != "D":
                either(DUP[b][k], (xs[b][2 * k],), (xs[b][2 * k + 1],), (vcost(w, .5), lambda e, dst=dst, src=src: e.tensor_copy(dst, src)),
                       (acost(w), lambda e, dst=dst, src=src: e.activation(dst, src, F.Copy)), tag="dup" + b)
    ON, col, cr = T.ones, T.cols, T.cr
    V(256, .5, (), ("ones",), lambda e: e.memset(ON[:], 1.0))
    Gc(128, ("ones",), ("Bd0",), lambda e: e.affine_select(T.Bd[:], ON[:, 0:128], [[-16, 8], [0, 16]], A.is_ge, 0.0, 0, 1))
    Gc(128, ("Bd0",), ("Bd",), lambda e: e.affine_select(T.Bd[:], T.Bd[:], [[16, 8], [0, 16]], A.is_ge, 0.0, 15, -1))
    Gc(128, ("ones",), ("Id",), lambda e: e.affine_select(T.Id[:], ON[:, 0:128], [[-1, 128]], A.is_equal, 0.0, 0, 1))
    Gc(128, ("ones",), ("Sw",), lambda e: e.affine_select(T.Sw[:], ON[:, 0:128], [[64, 2], [-1, 64]], A.is_equal, 0.0, -64, 1))
    Gc(144, ("ones",), ("E0",), lambda e: e.affine_select(T.E[:], ON[:, 0:144], [[0, 9], [1, 16]], A.is_equal, 0.0, -15, 0))
    Gc(144, ("E0",), ("E1",), lambda e: e.affine_select(T.E[:], T.E[:], [[-16, 9], [0, 16]], A.is_ge, 0.0, 0, 1))
    Gc(144, ("E1",), ("E",), lambda e: e.affine_select(T.E[:], T.E[:], [[16, 9], [0, 16]], A.is_ge, 0.0, 15, -1))
    Gc(128, (), ("kr",), lambda e: e.iota(T.kr[:], [[0, 8], [1, 16]], 0, 0, allow_small_or_imprecise_dtypes=True))
    Gc(32, (), ("pi",), lambda e: e.iota(T.pi[:], [[0, 32]], 0, 1))
    for c, pat in ((0, [[256, 8]]), (8, [[16, 8]]), (16, [[128, 2], [16, 4]]), (24, [[1, 8]])):
        Gc(8, (), ("cv%d" % c,), lambda e, c=c, pat=pat: e.iota(T.cv[:, c:c + 8], pat, 0, 0))
    ops[V(2048, .5, (), names("HB", 0, 4), lambda e: e.memset(T.HB[:], 0.0))]["soon"] = True
    Gc(2048, names("HB", 0, 4), ("Exp",), lambda e: e.affine_select(T.Exp[:], T.HB[:], [[-1, 128], [0, 16]], A.not_equal, 1.0, 0, 1))
    for b in SETS:
        for h in (0, 1):
            for k in (0, 1):
                V(64, 1, ("tub",), ("lu0%s%d" % (b, 2 * h + k),),
                  lambda e, b=b, h=h, k=k: e.tensor_copy(T["lu" + b][half[h], 64 * k:64 * k + 64], T.tub[own[b], tubes(h, k)]))
    if "D" in ZERO["A"] + ZERO["B"]: V(128, 1, (), ("usB",), lambda e: e.memset(T.usB[:], 0.0))
    for b in SETS:
        if ZERO[b] == "A":
            ops[C(2048, names("HB", 0, 4), wins[b], lambda e, b=b: e.activation(T["win" + b][:], T.HB[:], F.Copy), tag="wz" + b)]["soon"] = True
        if ZERO[b] == "G":
            Gc(2048, (), wins[b], lambda e, b=b: e.iota(T["win" + b][:], [[0, 2048]], 0, 0, allow_small_or_imprecise_dtypes=True), tag="wz" + b)
        Gc(2048, (), ("cw" + b,), lambda e, b=b: e.iota(T["cw" + b][:], [[0, 2048]], 0, 0))
    V(16, 1, ("pi",), ("pi0",), lambda e: e.tensor_scalar(T.pi[:, 0:16], T.pi[:, 0:16], 15, None, A.bitwise_and))
    V(8, 1, ("pi",), ("pi16",), lambda e: e.tensor_scalar(T.pi[:, 16:24], T.pi[:, 16:24], 79, None, A.bitwise_and))
    V(1, 1, ("pi0",), ("c0",), lambda e: e.tensor_copy(col[:, 0:1], T.pi[:, 0:1]))
    V(1, 1, ("c0",), ("c1",), lambda e: e.tensor_scalar(col[:, 1:2], col[:, 0:1], 0.0, None, A.is_gt))
    V(1, 1, ("c0",), ("l15",), lambda e: e.tensor_scalar(T.l15[:, 0:1], col[:, 0:1], 15.0, None, A.is_equal))
    V(128, .5, ("c0", "kr"), ("mask",), lambda e: e.tensor_scalar(T.mask[:], T.kr[:], col[:, 0:1], None, A.is_equal))
    V(8, 1, ("pi0", "c0"), ("pj",), lambda e: e.tensor_scalar(T.pi[:, 0:8], T.pi[:, 0:8], 16.0, None, A.mult))
    V(24, 2, ("pj", "pi0", "pi16", "cv0", "cv8", "cv16"), ("cv",), lambda e: e.tensor_tensor(T.cv[:, 0:24], T.cv[:, 0:24], T.pi[:, 0:24], A.add))
    V(16, 1, ("cv",), ("CV",), lambda e: e.tensor_copy(T.CV[:, 0:16], T.cv[:, 0:16]))
    V(8, 1, ("cv",), ("vtW",), lambda e: e.tensor_scalar(T.vt[:, 0:8], T.cv[:, 16:24], -63.5, None, A.add))
    times(8, ("vtW",), "V0", T.CV[:, 16:24], T.vt[:, 0:8], 32.0, 2032.0)
    for h in (0, 1): times(8, ("V0",), "V%d" % (h + 1), T.CV[half[h], 24:32], T.CV[half[1 - h], 16:24])
    V(8, 1, ("cv24",), ("cidx",), lambda e: e.tensor_copy(T.cidx[:], T.cv[:, 24:32]))
    pf = T.prf
    V(1, 1, ("wi",), ("prf0",), lambda e: e.tensor_scalar(pf[:, 0:1], T.prm[:, 0:1], 1.0 / 4096, None, A.mult))
    times(1, ("prf0",), "prf1", pf[:, 1:2], pf[:, 0:1], 128.0)
    V(1, 1, ("kni",), ("prf2",), lambda e: e.tensor_scalar(pf[:, 2:3], T.prm[:, 1:2], 8.0, 2047.5, A.mult, A.add))
    V(1, 2, ("kni",), ("kk",), lambda e: e.tensor_tensor(col[:, 2:3], T.prm[:, 1:2], T.prm[:, 1:2], A.mult))
    times(1, ("kk",), "prf3", pf[:, 3:4], col[:, 2:3], -64.0)
    V(4, 1, ("limi",), ("prf4",), lambda e: e.tensor_scalar(pf[:, 4:8], T.prm[:, 4:8], 256.0, 768.0, A.mult, A.add))
    for n, b in enumerate(SETS):
        cb = T["col" + b]
        for h in (0, 1):
            times(4, names("prf", 0, 4), "col%s%d" % (b, h), cb[half[h], 0:4], pf[own[b], 0:4])
            times(4, ("prf4",), "cst%s%d" % (b, h), T.cst[half[h], n:8:2], pf[own[b], 4:8])
        both = names("col" + b, 0, 2)
        wE = T["wE" + b]
        if SUMS[b] == "W":
            times(144, both + ["E"], "wE" + b, wE[:, 0:144], T.E[:], cb[:, 0:1])
        else:
            times(1, both, "col2" + b, cb[:, 4:5], cb[:, 2:3], 1.0, -2047.5)
            times(128, both + ["Bd"], "wq" + b, wE[:, 128:256], T.Bd[:], cb[:, 0:1])
            times(128, ["wq" + b], "wn" + b, wE[:, 0:128], wE[:, 128:256], -1.0)
            times(128, ["wq" + b], "wr" + b, wE[:, 256:384], wE[:, 128:256], -128.0)
            times(128, ["wq" + b], "ws" + b, wE[:, 384:512], wE[:, 128:256], 128.0)
    csts = ("cstA0", "cstA1", "cstB0", "cstB1")
    times(2, csts, "nb0", T.nb[:, 0:2], T.cst[:, 0:2], 1.0, -896.0)
    ops[C(1600, ("ones",), ("ej",), lambda e: e.activation(T.ej[:], ON[:, 0:128], F.Sigmoid))]["soon"] = True
    for name, n, out, src, need, k in (("Im", 128, T.Im[:], T.Id[:], "Id", -1.0), ("pE", 144, T.pE[:], T.E[:], "E", 16384.0),
                                       ("neg", 128, T.neg[:], ON[:, 0:128], "ones", -256.0), ("Bd32", 128, T.Bd32[:], T.Bd[:], "Bd", 1.0),
                                       ("Bd128", 128, T.Bd128[:], T.Bd[:], "Bd", 128.0), ("I32", 128, T.I32[:], T.Id[:], "Id", 32.0),
                                       ("S32", 128, T.S32[:], T.Sw[:], "Sw", 32.0), ("K8a", 8, T.K8[:, 0:8], T.Bd[:, 0:128:16], "Bd", 64.0),
                                       ("K8b", 8, T.K8[:, 8:16], T.Bd[:, 0:128:16], "Bd", -32.0), ("sela", 8, T.sel[:, 0:8], T.Bd[:, 0:128:16], "Bd", 1.0),
                                       ("selb", 8, T.sel[:, 8:16], T.Bd[:, 0:128:16], "Bd", 128.0),
                                       ("selc", 8, T.sel[:, 16:24], T.Bd[:, 0:128:16], "Bd", 32.0)):
        times(n, (need,), name, out, src, k)
    times(128, ("Bd", "c1"), "Bn", T.Bn[:], T.Bd[:], col[:, 1:2])
    V(512, .5, (), ("R0",), lambda e: e.memset(T.R[:], 0.0))
    V(64, .5, ("R0",), ("R",), lambda e: e.memset(T.R[:, 0:512:16], 255.0))
    if "W" in SUMS["A"] + SUMS["B"]:
        Gc(128, ("Bd",), ("Dm0",), lambda e: e.affine_select(T.Dm[:], T.Bd[:], [[-1, 128]], A.is_equal, 0.0, 1, 1))
        V(128, 2, ("Dm0", "Id"), ("Dm",), lambda e: e.tensor_tensor(T.Dm[:], T.Id[:], T.Dm[:], A.subtract))
    V(128, 1, (), ("Rk0",), lambda e: e.memset(T.Rk[:], -33554432.0))
    V(8, 1, ("Rk0",), ("Rk",), lambda e: e.memset(T.Rk[:, 0:128:16], 33554432.0))
    V(128, .5, (), ("crE",), lambda e: e.memset(cr[0:1, 0:128], -896.0))
    V(128, .5, (), ("cr2",), lambda e: e.memset(cr[0:1, 128:256], -172032.0))
    V(8, .5, ("cr2",), ("crX",), lambda e: e.memset(cr[0:1, 128:256:16], -1048576.0))
    V(128, .5, (), ("cr3",), lambda e: e.memset(cr[0:2, 256:384], 1.0 / 8192))
    V(128, .5, ("cr3",), ("crQ",), lambda e: e.memset(cr[0:1, 256:384], -0.5))
    times(128, ("crQ",), "crP", cr[0:2, 640:768], cr[0:2, 256:384], -1.0)
    V(128, .5, (), ("crM",), lambda e: e.memset(cr[0:1, 384:512], MAGIC))
    V(128, .5, (), ("crN",), lambda e: e.memset(cr[0:1, 512:640], -MAGIC))
    V(128, .5, (), ("cr4",), lambda e: e.memset(cr[0:2, 768:896], -1.0 / 64))
    V(128, .5, ("cr4",), ("crR",), lambda e: e.memset(cr[0:1, 768:896], 0.5))

    pend = {}

    def luk(t, b): return names("lu0" + b, 0, 4) if t == 0 else ["lu%d%s" % (t, b)]

    def window(t, b):
        lf = "lf%d%s" % (t, b)
        if t: moves(op("R", FLY, (), luk(t, b), None, sem="au%d%s" % (t, b), cnt=arrive, sched=(pend[b],), tag="fly"), 64)
        if t and not FOLD: moves(op("R", FLY, (), (lf,), None, sem="af%d%s" % (t, b), cnt=arrive, sched=(pend["f" + b],), tag="flyf"), 96)
        else: V(128, 1, luk(t, b), (lf,), lambda e: e.tensor_copy(lists(t, b, n="lf"), lists(t, b)), tag="lf")
        rows, win = T["rows" + b], T["win" + b]
        if t == 0 and ZERO[b] == "D":
            V(128, 1, luk(t, b) + ["c1"], ("nw" + b,), lambda e: e.tensor_scalar(T["nw" + b][:], lists(t, b), col[:, 1:2], None, A.mult), tag="lz")
            moves(op("S", DMA0, ("nw" + b, "usB"), ("rows" + b,),
                     lambda e: [e.dma_start(rows[:, 0:16, :], T.usB[:]), e.dma_start(rows[:, 16:32, :], T["nw" + b][:])], sem="r0" + b, cnt=2, tag="D1"), 160)
            for j0 in range(0, 16, 4):
                moves(op("S", DMA0, ("rows" + b,), wins[b][j0:j0 + 4],
                         lambda e, j0=j0: [e.dma_start(win[j:128:16, :], rows[:, 17 - j:33 - j, :] if j else rows[:, 0:16, :]) for j in range(j0, j0 + 4)],
                         sem="w0" + b, cnt=4, tag="Dz"), 280)
            return
        DMA("S", 80, [lf], ("rows" + b,), rows[:, 16:32, :], lists(t, b, n="lf"), "r%d%s" % (t, b), tag="D1")
        for j0 in range(1, 16, 3):
            moves(op("S", DMA0, ("rows" + b,), wins[b][j0:j0 + 3],
                     lambda e, j0=j0: [e.dma_start(win[j:128:16, 128 * j:2048], rows[:, 17:33 - j, :]) for j in range(j0, j0 + 3)],
                     sem="w%d%s" % (t, b), cnt=3, tag="Dj"), 24 + 12 * (15 - j0))

    def front(t, b):
        last = t == RO - 1
        b0, b1, b2 = "0" + b, "1" + b, "2" + b
        p0, p1, p2 = T["p0" + b], T["p1" + b], T["p2" + b]
        q = {n: T[n + b] for n in ("X", "G", "M", "H", "Lp", "t32", "c32", "Wm", "pass", "zo", "cu", "q", "Z", "Zt", "cm", "col",
                                   "uf", "us", "Ws", "wE", "nw", "rq", "rd", "rp", "win", "cw", "nl", "Gy")}
        G, M, H, cb = q["G"], q["M"], q["H"], q["col"]
        Lp, Gm, cols = q["Lp"][:], q["Gy"][:, 128:256], names("col" + b, 0, 2) + ["col2" + b]
        n, every, who = SETS.index(b), SUMS[b] == "W", OPQ[b]
        nb = T.nb[:, 2 * t + n:2 * t + n + 1]
        C(128, ["lf%d%s" % (t, b)] + cols, ("Lp" + b,), lambda e: e.activation(Lp, lists(t, b, n="lf"), F.Identity, bias=cb[:, 3:4], scale=16.0), tag="Lp")
        for x, j0, j1 in pieces(G1Q[b]):
            gather(x, 512 * (j1 - j0), xs[b] + luk(t, b), names("G" + b, j0, j1), G[:, 512 * j0:512 * j1],
                   q["X"][:, 0:8192].indirect(lists(t, b, j0, j1)), tag="G1")
        for x, j0, j1 in pieces(SCQ):
            f = slice(512 * j0, 512 * j1); k = 512 * (j1 - j0)
            V(k, .5, names("G" + b, j0, j1) + ["R"], names("M" + b, j0, j1),
              lambda e, f=f, k=k: e.tensor_tensor_scan(M[:, f], T.R[:, 0:k], G[:, f], 0.0, A.max, A.min), tag="SC")
        for x, j0, j1 in pieces(CPQ[b]):
            f = slice(512 * j0, 512 * j1); k = 512 * (j1 - j0)
            either(x, names("M" + b, j0, j1) + ["nb%d" % t, "ej"], names("H" + b, j0, j1),
                   (vcost(k, .5), lambda e, f=f: e.tensor_scalar(H[:, f], M[:, f], 256.0, nb, A.mult, A.is_lt)),
                   (acost(k), lambda e, f=f: e.activation(H[:, f], M[:, f], F.Sigmoid, bias=nb, scale=-256.0)), tag="CP")

        def nearest():
            V(128, 1, (), ("q" + b,), lambda e: e.tensor_scalar(q["q"][:], p1[:, 384:512], MAGIC, MAGIC, A.add, A.subtract), (b1,), tag="q")
        for h in (0, 1):
            def sums(e, dst, row, k, w, src, i0, h=h):
                if i0 == 0: e.matmul(dst, row, ON[0:k, 0:64], True, False)
                for i in range(i0, i0 + CHUNK):
                    r = e.matmul(dst, w[:, 15 - i:143 - i], src[:, h * 1024 + i:h * 1024 + 1024:16], False, i == 15)
                return r
            for i0 in range(0, 16 if every else 0, CHUNK):
                P(68 * CHUNK, names("G" + b, 2 * h, 2 * h + 2) + ["wE" + b, "crQ", "ones"],
                  lambda e, f=sums, i0=i0, h=h: f(e, p1[:, 384 + 64 * h:448 + 64 * h], cr[0:2, 256:384], 2, q["wE"], G, i0), (b1,), tag="xS")
            if h and every:
                nearest()
                V(128, 1, ("q" + b,), ("uf" + b,), lambda e: e.tensor_tensor(q["uf"][:], p1[:, 384:512], q["q"][:], A.subtract), (b1,), tag="uf")
                P(512, ("uf" + b, "Dm"), lambda e: e.matmul(p1[:, 0:128], T.Dm[:], q["uf"][:], True, True), (b1,), tag="dq")
            for i0 in range(0, 16, CHUNK):
                P(68 * CHUNK, names("H" + b, 2 * h, 2 * h + 2) + ["pE", "crX", "ones"],
                  lambda e, f=sums, i0=i0, h=h: f(e, p0[:, 64 * h:64 * h + 64], cr[0:1, 128:256], 1, T.pE, H, i0), (b0,), tag="cnt")
        either(who[0], ("ej",), ("pass" + b,), (vcost(128), lambda e: e.tensor_scalar(q["pass"][:], p0[:, 0:128], 0.0, None, A.is_lt)),
               (acost(128), lambda e: e.activation(q["pass"][:], p0[:, 0:128], F.Sigmoid, scale=-1.0)), (b0,), tag="pass")
        P(128, ("pass" + b, "Bn"), lambda e: e.matmul(p0[:, 128:256], q["pass"][:], T.Bn[:], True, True), (b0,), tag="mT")
        V(128, 1, ("mask",), ("Wm" + b,), lambda e: e.tensor_tensor(q["Wm"][:], p0[:, 128:256], T.mask[:], A.mult), (b0,), tag="Wm")

        def mP(e):
            e.matmul(p0[:, 384:400], T.Id[:], T.CV[:, 0:16], True, False)
            return e.matmul(p0[:, 384:400], q["Wm"][:], T.sel[:, 0:16], False, True)
        P(128, ("Wm" + b, "Id", "CV", "sela", "selb"), mP, (b0,), tag="mP")
        V(16, 1, (), ("zo" + b,), lambda e: e.tensor_copy(q["zo"][:], p0[:, 384:400]), (b0,), tag="zo")
        if every:
            V(128, 1, ("pass" + b,), ("us" + b,), lambda e: e.tensor_tensor(q["us"][:], q["pass"][:], p1[:, 0:128], A.mult), (b1,), tag="us")
            P(512, ("us" + b, "Bd32"), lambda e: e.matmul(p2[:, 128:256], T.Bd32[:], q["us"][:], True, True), (b2,), tag="u1")
        else:
            gather(who[5], 128, ["zo" + b] + names("G" + b, 0, 4), ("Gm" + b,), Gm, G[:, 0:2048].indirect(q["zo"][:, 0:8]), tag="Gm")
            dst = p2[:, 128:256]
            P(128, ("crP", "ones"), lambda e: e.matmul(dst, cr[0:2, 640:768], ON[0:2, 0:128], True, False), (b2,), tag="x0")

            def mod(e):
                e.matmul(dst, q["wE"][:, 0:128], Gm, False, False)
                e.matmul(dst, cr[0:1, 384:512], ON[0:1, 0:128], False, False)
                e.matmul(dst, cr[0:1, 512:640], ON[0:1, 0:128], False, False)
                return e.matmul(dst, q["wE"][:, 128:256], Gm, False, True)
            P(512, ("Gm" + b, "wq" + b, "wn" + b, "crM", "crN"), mod, (b2,), tag="x")
        C(128, cols, (), lambda e: e.activation(p2[:, 256:384], p2[:, 128:256], F.Square, bias=cb[:, 2:3] if every else cb[:, 4:5], scale=4096.0), (b2,), tag="Sq")
        gather(who[1], 128, ["zo" + b] + names("M" + b, 0, 4), ("Z" + b,), q["Z"][:], M[:, 0:2048].indirect(q["zo"][:, 0:8]), 0.5, tag="Z")
        V(128, 1, ("Lp" + b,), ("t32" + b,), lambda e: e.tensor_tensor(q["t32"][:], p2[:, 256:384], Lp, A.add), (b2,), tag="t32")
        V(128, 1, ("t32" + b,), ("c32" + b,), lambda e: e.tensor_scalar(q["c32"][:], q["t32"][:], 4, 8191, A.arith_shift_right, A.bitwise_and), tag="c32")
        V(128, 1, ("c32" + b,), ("cu" + b,), lambda e: e.tensor_copy(q["cu"][:], q["c32"][:]), tag="cu")
        DMA(DCQ, 80, ("c32" + b,), ("cw" + b,), q["cw"][0:128:16, :], q["c32"][:], "c%d%s" % (t, b), tag="Dc")
        P(128, ("Z" + b, "Id"), lambda e: e.matmul(p1[:, 256:384], q["Z"][:], T.Id[:], True, True), (b1,), tag="Ztr")
        either("A", (), ("Zt" + b,), (vcost(128), lambda e: e.tensor_copy(q["Zt"][:], p1[:, 256:384])),
               (acost(128), lambda e: e.activation(q["Zt"][:], p1[:, 256:384], F.Copy)), (b1,), tag="Zt")
        if not last:
            P(64, ("pass" + b, "l15"), lambda e: e.matmul(p0[:, 416:417], q["pass"][:], T.l15[:, 0:1], True, True), (b0,), tag="e0")
            either(who[2], (), ("ec" + b,), (vcost(1), lambda e: e.tensor_copy(T.ec[:, n:n + 1], p0[:, 416:417])),
                   (acost(1), lambda e: e.activation(T.ec[:, n:n + 1], p0[:, 416:417], F.Copy)), (b0,), tag="e1")
        if not last and n:
            def full(e):
                e.matmul(p0[:, 420:421], cr[0:1, 0:128], ON[0:1, 0:1], True, False)
                e.matmul(p0[:, 420:421], T.neg[:], T.ec[:, 0:1], False, False)
                return e.matmul(p0[:, 420:421], T.neg[:], T.ec[:, 1:2], False, True)
            P(192, ("crE", "ones", "neg", "ecA", "ecB"), full, (b0,), tag="e2")
            V(1, 1, (), ("eR",), lambda e: e.tensor_scalar(T.eR[:], p0[:, 420:421], 2048 * MAGIC, 2048 * MAGIC, A.add, A.subtract), (b0,), tag="e3")
            V(2, 1, ("eR",) + csts, ("nb%d" % (t + 1),),
              lambda e: e.tensor_scalar(T.nb[:, 2 * t + 2:2 * t + 4], T.cst[:, 2 * t + 2:2 * t + 4], p0[:, 420:421], T.eR[:], A.add, A.subtract), (b0,), tag="e4")
        V(128, 1, ("c32" + b,), ("cm" + b,), lambda e: e.tensor_tensor(q["cm"][:], q["c32"][:], p0[:, 0:128], A.min), (b0,), tag="cm")
        op("V", gcost(128), wins[b] + ["zo" + b, "cm" + b], ("nw" + b,),
           lambda e: e.tensor_tensor(q["nw"][:], q["win"][:, 0:2048].indirect(q["zo"][:, 8:16]), q["cm"][:], A.max), tag="nw")
        if last:
            C(128, ("Z" + b,), ("yzs" + b,), lambda e: e.activation(q["nl"][:, 512:640], q["Z"][:], F.Copy, scale=2.0), tag="yz")
            for h in (0, 1):
                for k in (0, 1):
                    DMA("S", 24, ("yzs" + b,), (), T.yz[own[b], tubes(h, k)], q["nl"][half[h], 512 + 64 * k:576 + 64 * k], "out", tag="out")
            return

        if every:
            P(512, ("us" + b, "Bd128"), lambda e: e.matmul(p1[:, 128:256], q["us"][:], T.Bd128[:], True, True), (b1,), tag="sT")
            V(128, 1, ("mask",), ("Ws" + b,), lambda e: e.tensor_tensor(q["Ws"][:], p1[:, 128:256], T.mask[:], A.mult), (b1,), tag="Ws")
            P(256, ("Ws" + b, "Bd32"), lambda e: e.matmul(p1[:, 0:8], q["Ws"][:], T.Bd32[:, 0:128:16], True, True), (b1,), tag="sP")
        else:
            def sT(e):
                e.matmul(p1[:, 128:256], ON[0:2, 0:128], cr[0:2, 768:896], True, False)
                e.matmul(p1[:, 128:256], Gm, q["wE"][:, 256:384], False, False)
                e.matmul(p1[:, 128:256], ON[0:1, 0:128], cr[0:1, 384:512], False, False)
                e.matmul(p1[:, 128:256], ON[0:1, 0:128], cr[0:1, 512:640], False, False)
                return e.matmul(p1[:, 128:256], Gm, q["wE"][:, 384:512], False, True)
            P(640, ("Gm" + b, "wr" + b, "ws" + b, "crM", "crN", "crR", "ones"), sT, (b1,), tag="sT")
            V(128, 1, ("mask",), ("q" + b,), lambda e: e.tensor_tensor(q["q"][:], p1[:, 128:256], T.mask[:], A.mult), (b1,), tag="Ws")

            def sP(e):
                e.matmul(p1[:, 16:32], T.Id[:], T.CV[:, 16:32], True, False)
                e.matmul(p1[0:64, 24:32], q["q"][:, 64:128], T.sel[:, 16:24], False, False)
                e.matmul(p1[64:128, 24:32], q["q"][:, 0:64], T.sel[:, 16:24], False, False)
                return e.matmul(p1[:, 16:24], q["q"][:], T.sel[:, 16:24], False, True)
            P(256, ("q" + b, "Id", "V0", "V1", "V2", "selc"), sP, (b1,), tag="sP")
            V(16, 1, (), ("rp" + b,), lambda e: e.tensor_copy(q["rp"][:], p1[:, 16:32]), (b1,), tag="w3")
            return
        vt = T.vt[:, 0:8]
        V(8, 1, ("vtW",), ("rq" + b,), lambda e: e.tensor_tensor(q["rq"][:], p1[:, 0:8], vt, A.subtract), (b1,), tag="w1")
        V(8, 1, ("rq" + b,), ("rd" + b,), lambda e: e.tensor_tensor(q["rd"][:], p1[:, 0:8], q["rq"][:], A.subtract), (b1,), tag="w2")

        def rP(e):
            e.matmul(p1[:, 16:24], T.I32[:], q["rd"][:], True, True)
            return e.matmul(p1[:, 24:32], T.S32[:], q["rd"][:], True, True)
        P(512, ("rd" + b, "I32", "S32"), rP, (b1,), tag="rP")
        V(16, 1, (), ("rp" + b,), lambda e: e.tensor_scalar(q["rp"][:], p1[:, 16:32], 2047.5 if every else 0.0, None, A.add), (b1,), tag="w3")

    def middle(t, b):
        Gh, Pm, cu, Zt = T["Gc" + b], T["P" + b], T["cu" + b], T["Zt" + b]
        for who, j0, j1 in pieces(G2Q[b]):
            gather(who, 512 * (j1 - j0), xs[b] + ["cu" + b], names("Gc" + b, j0, j1), Gh[:, 512 * j0:512 * j1],
                   T["X" + b][:, 0:8192].indirect(cu[:, 32 * j0:32 * j1]), 0.5, tag="G2")
        for j in range(4):
            f = slice(j * 512, j * 512 + 512)
            z, bk = (T["p2" + b], "2" + b) if j & 1 else (T["z" + b], "z" + b)
            gk, zk, k = "Gc%s%d" % (b, j), "zx" + bk, len(ops) + 2
            P(512, ("Zt" + b, "Exp"), lambda e, z=z, f=f, k=k: e.matmul(z[:], Zt[:], T.Exp[:, f], True, ops[k]["q"] == "V"), (bk,), tag="Zx", writes=(zk,))
            P(512, (gk, "Im"), lambda e, z=z, f=f: e.matmul(z[:], T.Im[:], Gh[:, f], False, True), (bk,), tag="Zd")
            either("A", (gk, zk), ("P%s%d" % (b, j),), (vcost(512), lambda e, z=z, f=f: e.tensor_tensor(Pm[:, f], Gh[:, f], z[:], A.max)),
                   (acost(512), lambda e, z=z, f=f: e.activation(Pm[:, f], z[:], F.Relu, scale=-1.0)), (bk,), tag="max")
            ops[k]["twin"] = k - 1
            choose(ops, k, MXQ[b][j])

    def back(t, b):
        last = t == RO - 1
        b0, b1 = "0" + b, "1" + b
        p0, p1 = T["p0" + b], T["p1" + b]
        q = {n: T[n + b] for n in ("X", "Gc", "P", "Km", "pm", "ki", "ku", "Gy", "Z", "Y", "rp", "cw", "nw", "nl")}

        def keys(name, w, stop):
            def kd(e, i0):
                for i in range(i0, i0 + CHUNK):
                    r = e.matmul(p0[:, 256 + i:384:16], q[name][:, i:2048:16], w, False, stop and i == 15)
                return r
            for i0 in range(0, 16, CHUNK):
                P(64 * CHUNK, names(name + b, 0, 4) + ["K8a", "K8b"], lambda e, i0=i0: kd(e, i0), (b0,), tag="key" + name[0])
        P(128, ("ones", "kr"), lambda e: e.matmul(p0[:, 256:384], ON[0:1, 0:128], T.kr[0:1, :], True, False), (b0,), tag="kc")
        keys("Gc", T.K8[:, 8:16], False)
        keys("P", T.K8[:, 0:8], True)
        V(128, 1, ("Rk",), ("pm" + b,), lambda e: e.tensor_tensor_scan(q["pm"][:], T.Rk[:], p0[:, 256:384], 0.0, A.max, A.min), (b0,), tag="scan")
        V(8, 1, ("pm" + b,), ("ki" + b,), lambda e: e.tensor_copy(q["ki"][:, 0:8], q["pm"][:, 15:128:16]), tag="k1")
        V(8, 1, ("ki" + b,), ("kj" + b,), lambda e: e.tensor_scalar(q["ki"][:, 8:16], q["ki"][:, 0:8], 15, None, A.bitwise_and), tag="k2")
        op("V", gcost(128), ("kj" + b, "cidx", "mask"), ("Km" + b,),
           lambda e: e.tensor_tensor(q["Km"][:], q["ki"][:, 8:16].indirect(T.cidx[:]), T.mask[:], A.mult), tag="Km")

        def kP(e):
            e.matmul(p0[:, 400:416], T.Id[:], T.CV[:, 0:16], True, False)
            return e.matmul(p0[:, 400:416], q["Km"][:], T.sel[:, 0:16], False, True)
        P(128, ("Km" + b, "Id", "CV", "sela", "selb"), kP, (b0,), tag="Kp")
        V(16, 1, (), ("ku" + b,), lambda e: e.tensor_copy(q["ku"][:], p0[:, 400:416]), (b0,), tag="k3")
        nl, su, best = lists(t, b, n="nl"), T["su" + b], q["cw"][:, 0:2048].indirect(q["ku"][:, 8:16])
        c, nlk, suk = [256 * t, 256 * t + 128][:1 + FOLD], "nl%d%s" % (t, b), "su%d%s" % (t, b)
        if last or not FOLD:
            op("V", gcost(128), ("cw" + b, "ku" + b, "nw" + b), (nlk,), lambda e: e.tensor_tensor(nl, best, q["nw"][:], A.max), tag="n0")
        if last:
            for h in (0, 1):
                for k in (0, 1):
                    DMA("AD" if k else "S", 24, (nlk,), (), T.yl[own[b], tubes(h, k)], q["nl"][half[h], 128 * t + 64 * k:128 * t + 64 * k + 64], "out", tag="out")
            return
        if FOLD:
            V(128, 1, ("nw" + b,), (suk,), lambda e: e.tensor_copy(su[:, c[0]:c[0] + 128], q["nw"][:]), tag="su")
            op("V", gcost(128), ("cw" + b, "ku" + b), (nlk,), lambda e: e.tensor_copy(su[:, c[1]:c[1] + 128], best), tag="n0")
        else:
            V(128, 1, (nlk,), (suk,), lambda e: e.tensor_copy(su[:, c[0]:c[0] + 128], nl), tag="su")
        pend[b] = op("G", 0.8, (suk, nlk), (),
                     [([su[:, x + 64 * k:x + 64 * k + 64] for x in c], lists(t + 1, b, 2 * k, 2 * k + 2)) for k in (0, 1)] + ["au%d%s" % (t + 1, b)],
                     sem="snd", tag="send")
        if not FOLD:
            pend["f" + b] = op("G", 0.8, (nlk,), (), [([lists(t, b, 2 * k, 2 * k + 2, "nl")], lists(t + 1, b, 2 * k, 2 * k + 2, "lf")) for k in (0, 1)]
                               + ["af%d%s" % (t + 1, b)], sem="snd", sched=(pend[b],), tag="sendf")
        gather(OPQ[b][4], 128, ["ku" + b] + names("Gc" + b, 0, 4), ("Gy" + b,), q["Gy"][:, 0:128], q["Gc"][:, 0:2048].indirect(q["ku"][:, 0:8]), tag="Gy")

        def yP(e):
            for c, m in ((0, T.Id), (128, T.Sw)):
                e.matmul(p1[:, c:c + 128], m[:], q["Z"][:], True, False)
                r = e.matmul(p1[:, c:c + 128], m[:], q["Gy"][:, 0:128], False, True)
            return r
        P(512, ("Gy" + b, "Z" + b, "Id", "Sw"), yP, (b1,), tag="yP")
        V(256, 1, (), ("Y" + b,), lambda e: e.tensor_scalar(q["Y"][:], p1[:, 0:256], -0.25, None, A.add), (b1,), tag="Y")
        op("V", 0.06 + 256 * SCA * CY, ("Y" + b, "rp" + b), xs[b], lambda e: e.tensor_copy(q["X"][:, 0:8192].indirect(q["rp"][:]), q["Y"][:]), tag="scat")

    for t in range(RO):
        for b in SETS:
            cur[0:2] = [b, t]
            for step in (window, front, middle, back): step(t, b)
    return ops


def schedule(ops, given=None):
    n, nm = len(ops), len(CY)
    pred = [sorted(o["hard"] | o["soft"] | o["order"]) for o in ops]
    succ = [[] for _ in range(n)]
    for i in range(n):
        for d in pred[i]: succ[d].append(i)
    que, wake, own = [0] * n, [float(x) for x in WAKE], [float(x) for x in SELF]
    cost, hold, after = ([[0.0] * n for m in range(nm)] for _ in range(3))

    def lag(a, b, m):
        qa, qb = ops[a]["q"], ops[b]["q"]
        return 0.0 if "N" in (qa, qb) else wake[m] if qa != qb else own[m] if a in ops[b]["hard"] and qa != "T" else 0.0

    def enter(i):
        o = ops[i]
        que[i] = "VATGSRN".index(DMAS.get(o["q"], o["q"])) if o["q"] != "N" else 5
        for m in range(nm):
            cost[m][i] = 0.0 if o["q"] == "N" else float((o["c"] + 0 * CY)[m])
            hold[m][i] = 0.0 if o["q"] == "R" else float(ISSUE[m]) * o["n"] if o["q"] in DMAS else cost[m][i]
            for k in [i] + succ[i]: after[m][k] = [(d, lag(d, k, m)) for d in pred[k]]

    def flip(i):
        choose(ops, i, "A" if ops[i]["q"] == "V" else "V")
        enter(i)
        if "twin" in ops[i]: enter(ops[i]["twin"])
    for i in range(n): enter(i)
    work = [[o.get("kb", 0) * float(LOAD[m]) / 1024 for o in ops] for m in range(nm)]
    late, at = [0.0] * n, 0.0
    for i in range(n):
        at += work[0][i] if "first" in ops[i] else 0.0
        late[i] = at if "first" in ops[i] else 4 * work[0][i]
    before = [[[(d, cost[0][d] + late[d] + lag(d, i, 0)) for d in pred[i]] for i in range(n)]]

    def times(order, m):
        st, fin, free, why, last = [0.0] * n, [0.0] * n, [0.0] * 7, [-1] * n, [-1] * 7
        bf, hd, cs, mv = after[m], hold[m], cost[m], work[m]
        end, e = 0.0, 0
        for i in order:
            k = que[i]
            s, w = free[k], last[k]
            for d, x in bf[i]:
                x += fin[d]
                if x > s: s = x; w = d
            st[i] = s
            if k < 5: free[k] = s + hd[i]; last[k] = i
            if mv[i]:
                s += hd[i] + 0.5 * cs[i]
                if free[6] > s: s = free[6]; w = last[6]
                free[6] = s + mv[i]; last[6] = i
                s += mv[i] + 0.5 * cs[i]
            else:
                s += cs[i]
            fin[i] = s; why[i] = w
            if s > end: end = s; e = i
        return end, st, why, e

    if given: return [times(given, m)[0] for m in range(nm)]

    def score(order):
        r = [times(order, m) for m in range(nm)]
        return sum((x[0] + EARLY * sum(x[1]) / n) * w for x, w in zip(r, WEIGHT)), r

    def move(order, pos, a, b, back):
        lo, hi = pos[a], pos[b]
        if lo >= hi or "first" in ops[a]: return False
        mark, near = ({a}, pred) if back else ({b}, succ)
        for k in range(lo + 1, hi + 1) if back else range(hi - 1, lo - 1, -1):
            i = order[k]
            for x in near[i]:
                if x in mark: mark.add(i); break
        if a in mark and b in mark: return False
        seg = order[lo:hi + 1]
        seg = [i for i in seg if (i in mark) != back] + [i for i in seg if (i in mark) == back]
        order[lo:hi + 1] = seg
        for k, i in enumerate(seg): pos[i] = lo + k
        return True

    tail = [0.0] * n
    for i in range(n - 1, -1, -1):
        tail[i] = cost[0][i] + max([tail[s] + lag(i, s, 0) for s in succ[i]], default=0.0)
    same = {}
    for o in ops: same.setdefault(o["kind"], {})[o["t"]] = o["i"]

    def place(key):
        need = [len(x) for x in pred]
        ready = [i for i in range(n) if not need[i]]
        start, busy = [0.0] * n, {}
        while ready:
            i = min(ready, key=lambda k: key[k])
            ready.remove(i)
            s = max([start[d] + w for d, w in before[0][i]], default=0.0)
            line = busy.setdefault(que[i], [])
            k, h = len(line), hold[0][i]
            while k and line[k - 1][1] > s: k -= 1
            while k < len(line) and line[k][0] < s + h:
                s = max(s, line[k][1]); k += 1
            if h: line.insert(k, (s, s + h))
            start[i] = s
            for k in succ[i]:
                need[k] -= 1
                if not need[k]: ready.append(k)
        return sorted(range(n), key=lambda i: (start[i], i))

    def keys(stretch, behind):
        g1 = {b: same["G1" + b, 1] for b in SETS}
        loop = tail[g1[SETS[1]][1]] - tail[g1[SETS[1]][2]]
        key = [0.0] * n
        for i in range(n - 1, -1, -1):
            o = ops[i]
            if "first" in o or "soon" in o: key[i] = -1e9 + i
            elif o["t"] < 0: key[i] = min([key[s] for s in succ[i]], default=0.0) - cost[0][i] - 0.2
            else: key[i] = stretch * (loop * (o["t"] + (behind if o["b"] == SETS[1] else 0.0)) + tail[g1[o["b"]][o["t"]]] - tail[i])
        return key
    tries = [place(keys(x, y)) for x in STRETCH for y in BEHIND]
    order = min(tries, key=lambda x: score(x)[0])
    rng = np.random.default_rng(SEED)
    now, res = score(order)
    best = (now, order, [o["q"] for o in ops])
    free = [o["i"] for o in ops if "alt" in o]
    for it in range(STEPS):
        heat = HEAT * (1 - it / STEPS) ** 2 + 1e-3
        _, st, why, e = res[int(rng.integers(nm))]
        pairs, can = [], []
        while why[e] >= 0:
            d = why[e]
            if d not in pred[e]:
                pairs.append((d, e))
                if "alt" in ops[d]: can.append(d)
            e = d
        if not pairs: break
        if can and rng.random() < FLIP:
            todo = set()
            for i in [can[int(rng.integers(len(can)))]] + ([free[int(rng.integers(len(free)))]] if rng.random() < 0.5 else []):
                todo.update([k for k in same[ops[i]["kind"]].values() if ops[k]["q"] == ops[i]["q"]] if rng.random() < EVERY else [i])
            for i in todo: flip(i)
            sc, r2 = score(order)
            if sc <= now or rng.random() < math.exp((now - sc) / heat):
                now, res = sc, r2
                if sc < best[0]: best = (sc, order, [o["q"] for o in ops])
            else:
                for i in todo: flip(i)
            continue
        a, b = pairs[int(rng.integers(len(pairs)))]
        new, pos = list(order), [0] * n
        for k, i in enumerate(new): pos[i] = k
        r, far, back = rng.random(), int(rng.integers(0, FAR)), rng.random() < 0.5
        k = pos[b] if back else pos[a]
        while far and 0 < k < n - 1:
            k += 1 if back else -1
            if que[new[k]] == que[a]:
                far -= 1
                if back: b = new[k]
                else: a = new[k]
        todo = [(a, b)]
        if r < EVERY:
            dt = ops[b]["t"] - ops[a]["t"]
            ka, kb = same[ops[a]["kind"]], same[ops[b]["kind"]]
            todo = [(ka[t], kb[t + dt]) for t in ka if t + dt in kb]
        if not sum([move(new, pos, x, y, back) for x, y in todo]): continue
        sc, r2 = score(new)
        if sc <= now or rng.random() < math.exp((now - sc) / heat):
            now, res, st = sc, r2, r2[0][1]
            if sc < best[0]: best = (sc, new, [o["q"] for o in ops])
            order = new
            if it % 8 == 0:
                order = sorted(new, key=lambda i: st[i])
                now, res = score(order)
    for i in free:
        if ops[i]["q"] != best[2][i]: flip(i)
    res = score(best[1])[1]
    for o in ops: o["s"] = res[0][1][o["i"]]; o["why"] = [x[2][o["i"]] for x in res]; o["ss"] = [x[1][o["i"]] for x in res]
    return best[1], [x[0] for x in res]


def rank_program(g, core, T, topo):
    if T.rank_of(core) is None:
        return
    ops = make_ops(core, T, topo)
    if not PLAN:
        PLAN.extend([schedule(ops), [o["s"] for o in ops], [o["q"] for o in ops]])
    order = PLAN[0][0]
    for o in ops:
        o["s"] = PLAN[1][o["i"]]
        if "alt" in o: choose(ops, o["i"], PLAN[2][o["i"]])
    eng = {"V": g.vector, "A": g.scalar, "T": g.tensor, "G": g, "S": g.sync, "AD": g.scalar, "GD": g}
    qsem = {"V": "qV", "A": "qA", "T": "qT", "G": "qG"}
    to, use = lanes(T, topo, core)
    total = {}
    for o in ops:
        if o["q"] in DMAS: total[o["sem"]] = total.get(o["sem"], 0) + 16 * o["n"]
    cnt, known, snap, done = {}, {}, {}, {}
    sent = 0
    for i in order:
        o = ops[i]
        if o["q"] == "N": continue
        if o["q"] == "R":
            done[i] = (o["sem"], o["n"]); snap[i] = {o["sem"]: o["n"]}
            continue
        qn = DMAS.get(o["q"], o["q"])
        e = eng[o["q"]]
        kn = known.setdefault(qn, {})
        for d in sorted(waits(ops, o), key=lambda d: -ops[d]["s"]):
            if ops[d]["q"] == "N" or ops[d]["q"] == o["q"] == "T": continue
            s, v = done[d]
            if kn.get(s, 0) >= v: continue
            e.wait_ge(T.sem[s], v)
            for k, x in snap[d].items():
                if kn.get(k, 0) < x: kn[k] = x
        if o["sem"] == "snd":
            moves = []
            for (src, dst), d, ln in zip(o["fn"][:2], to, use):
                rid, pid, _ = topo.addr(d)
                moves.append(RemoteDMATransfer(dst_ids=[DstId(rid=rid, pnc=pid)], dma_engine_mask=sum(1 << x for x in ln),
                                               remote_sem=T.sem[o["fn"][2]], srcs=src, dsts=[dst], alu_op=2 * (len(src) - 1)))
                sent += len(ln)
            g.remote_dma_fused(moves, local_sem=T.sem.snd)
            done[i] = ("snd", sent); snap[i] = dict(kn)
        else:
            r = o["fn"](e)
            if o["q"] in DMAS:
                for x in r: x.then_inc(T.sem[o["sem"]], 16)
                done[i] = (o["sem"], total[o["sem"]]); cnt[o["sem"]] = total[o["sem"]]
            else:
                s = qsem[o["q"]]
                cnt[s] = cnt.get(s, 0) + 1
                r.then_inc(T.sem[s], 1)
                done[i] = (s, cnt[s])
            snap[i] = dict(kn); snap[i][done[i][0]] = done[i][1]
    for s, v in cnt.items():
        g.wait_ge(T.sem[s], v)
    g.wait_ge(T.sem.snd, sent)
    for o in ops:
        if o["q"] == "R": g.wait_ge(T.sem[o["sem"]], o["n"])
